import numpy as np
import ml_dtypes


def mxq(x, axis, fmt="e4m3"):
    dtype, down = {"e4m3": (ml_dtypes.float8_e4m3fn, 7), "e5m2": (ml_dtypes.float8_e5m2, 14)}[fmt]
    v = np.moveaxis(np.asarray(x, np.float32).astype(ml_dtypes.bfloat16).astype(np.float64), axis, -1)
    blocks = v.reshape(v.shape[:-1] + (-1, 32))
    amax = np.abs(blocks).max(-1, keepdims=True)
    byte = np.maximum(np.where(amax > 0, np.frexp(amax)[1] - 1 + 127, 0) - down, 1)
    scale = np.exp2(byte - 127.0)
    codes = (blocks / scale).astype(np.float32).astype(dtype).astype(np.float64)
    return np.moveaxis((codes * scale).reshape(v.shape), -1, axis)


WIDE = False


def mx_kscale(k):
    if not WIDE:
        return np.ones(k)
    levels = np.array([10, -10, 5, -5, 0])
    if k % 512:
        return np.exp2(np.random.permutation(np.resize(levels, k // 32))).repeat(32)
    a = np.empty((k // 512, 16))
    for p in range(k // 512):
        a[p, :8] = np.random.permutation(np.resize(levels, 8))
        for g in range(8):
            far = levels[np.abs(levels - a[p, g]) >= 10]
            a[p, g + 8] = far[np.random.randint(len(far))]
    return np.exp2(a.ravel()).repeat(32)


def f64(x):
    return np.asarray(x).astype(np.float64)


def striped(idx):
    return np.tile(idx.reshape(-1, 16).T, (8, 1)).astype(np.uint16)


def unstriped(offs):
    return offs[:16].T.reshape(-1).astype(np.int64)


E2M1 = np.array([0.0, 0.5, 1.0, 1.5, 2.0, 3.0, 4.0, 6.0, -0.0, -0.5, -1.0, -1.5, -2.0, -3.0, -4.0, -6.0])


def pack_weight(w, fmt):
    k, n = w.shape
    w = f64(np.asarray(w, np.float32).astype(ml_dtypes.bfloat16)).reshape(k // 32, 32, n)
    amax = np.abs(w).max(1)
    if fmt == "e4m3":
        byte = np.frexp(amax)[1] - 1 + 127 - 7
    else:
        mant, ex = np.frexp(amax / 6.0)
        byte = np.where(mant > 0.5, ex, ex - 1) + 127
    byte = np.clip(np.where(amax > 0, byte, 1), 1, 254)
    scaled = (w * np.exp2(127.0 - byte)[:, None, :]).reshape(k, n).astype(np.float32)
    by_word = np.ascontiguousarray(scaled.reshape(k // 512, 128, 4, n).transpose(0, 1, 3, 2))
    if fmt == "e4m3":
        words = by_word.astype(ml_dtypes.float8_e4m3fn).view(np.uint8)
    else:
        c = by_word.astype(ml_dtypes.float4_e2m1fn).view(np.uint8) & 0xF
        words = (c[..., 0::2] | (c[..., 1::2] << 4)).reshape(k // 512, 128, 2 * n)
    return np.ascontiguousarray(words), np.ascontiguousarray(byte.astype(np.uint8).reshape(k // 512, 16, n))


def unpack_weight(words, scales, fmt):
    g, _, n = scales.shape
    words = np.ascontiguousarray(words).reshape(g, 128, n, -1)
    if fmt == "e4m3":
        vals = words.view(ml_dtypes.float8_e4m3fn).astype(np.float64)
    else:
        nib = np.empty((g, 128, n, 4), np.uint8)
        nib[..., 0::2] = words & 0xF
        nib[..., 1::2] = words >> 4
        vals = E2M1[nib]
    vals = vals * np.repeat(np.exp2(scales.astype(np.float64) - 127.0), 8, axis=1)[..., None]
    return vals.transpose(0, 1, 3, 2).reshape(g * 512, n)


def gelu(v):
    return 0.5 * v * (1.0 + np.tanh(np.sqrt(2.0 / np.pi) * (v + 0.044715 * v**3)))


K, H, T, S, P = 1536, 1024, 4096, 1024, 512

def setup_inputs():
    n = np.random.standard_normal
    s = mx_kscale(K)[:, None]
    u = mx_kscale(H)[:, None]
    tab_words, tab_scales = pack_weight(n((K, T)) * s, "e4m3")
    w4_words, w4_scales = pack_weight(1.5 * n((H, H)) / np.sqrt(H) / u, "e2m1")
    return {
        "tab_words": tab_words, "tab_scales": tab_scales,
        "offs": striped(np.random.permutation(T)[:S]),
        "pos1": striped(np.random.permutation(S)[:P]),
        "pos2": striped(np.random.permutation(S)[:P]),
        "w1": (n((K, H)) / np.sqrt(K) / s).astype(np.float32),
        "b1": (0.5 * n(H)).astype(np.float32),
        "gain": (np.exp(0.3 * n(H)) * u[:, 0]).astype(np.float32),
        "w4_words": w4_words, "w4_scales": w4_scales,
        "b2": (0.5 * n(H)).astype(np.float32),
    }

def reference(tab_words, tab_scales, offs, pos1, pos2, w1, b1, gain, w4_words, w4_scales, b2):
    v = unpack_weight(tab_words, tab_scales, "e4m3")[:, unstriped(offs)]
    h = mxq(f64(w1), 0, "e4m3").T @ v
    th = np.tanh(h[:, unstriped(pos1)] + f64(b1)[:, None])
    z = f64(gain)[:, None] * th
    w4 = unpack_weight(w4_words, w4_scales, "e2m1")
    y = w4.T @ mxq(z, 0, "e4m3")
    crossed = th * (y + f64(b2)[:, None])
    return crossed + h[:, unstriped(pos2)]

@@ -1,0 +1,233 @@
+from contextlib import ExitStack
+
+import concourse.mybir as mybir
+
+K, H, T, S, M = 1536, 1024, 4096, 1024, 512
+FLOPS = 2 * K * H * S + 2 * H * H * M
+
+F32 = mybir.dt.float32
+BF16 = mybir.dt.bfloat16
+I32 = mybir.dt.int32
+U32 = mybir.dt.uint32
+U16 = mybir.dt.uint16
+U8 = mybir.dt.uint8
+FP8X4 = mybir.dt.float8_e4m3fn_x4
+FP4X4 = mybir.dt.float4_e2m1fn_x4
+ACT = mybir.ActivationFunctionType
+ALU = mybir.AluOpType
+
+P = 128
+KP = K // 512
+HP = H // 512
+BANK = 512
+
+
+def tile_list_recipe_citation_cross_kernel(
+    tc, tab_words, tab_scales, offs, pos1, pos2, w1, b1, gain, w4_words, w4_scales, b2, out
+):
+    nc = tc.nc
+    with ExitStack() as ctx:
+        keep = ctx.enter_context(tc.tile_pool(name="keep", bufs=1))
+        ring = ctx.enter_context(tc.tile_pool(name="ring", bufs=1))
+        psum = ctx.enter_context(tc.psum_pool(name="psum", bufs=1))
+
+        offs_sb = keep.tile([P, S // 16], U16, name="offs_sb")
+        pos1_sb = keep.tile([P, M // 16], U16, name="pos1_sb")
+        pos2_sb = keep.tile([P, M // 16], U16, name="pos2_sb")
+        b1_sb = keep.tile([P, HP, 4], F32, name="b1_sb")
+        gain_sb = keep.tile([P, HP, 4], F32, name="gain_sb")
+        b2_sb = keep.tile([P, HP, 4], F32, name="b2_sb")
+        tab_plane = keep.tile([P, T], U8, name="tab_plane", align_bytes=64)
+        w4_plane_raw = keep.tile([P, HP * H], U8, name="w4_plane_raw", align_bytes=64)
+        w4_raw = keep.tile([P, HP * H], U16, name="w4_raw", align_bytes=64)
+
+        nc.vector.memset(tab_plane[:].bitcast(I32), 0)
+        nc.vector.memset(w4_plane_raw[:].bitcast(I32), 0)
+
+        table = []
+
+        def load_table(a):
+            tile = ring.tile([P, T], U32, name="table", tag="big", bufs=3, align_bytes=64)
+            nc.sync.dma_start(tile[:].bitcast(I32), tab_words[a].rearrange("p t i -> p (t i)").bitcast(I32))
+            table.append(tile)
+
+        w1_raw = {}
+
+        def load_w1(b, a):
+            tile = keep.tile([P, 4, 512], F32, name="w1_raw_%d_%d" % (b, a))
+            nc.sync.dma_start(
+                tile[:],
+                w1[512 * a : 512 * (a + 1), 512 * b : 512 * (b + 1)].rearrange("(p j) c -> p j c", j=4),
+            )
+            w1_raw[b, a] = tile
+
+        def load_vector(tile, vec):
+            nc.sync.dma_start(tile[:], vec.rearrange("(b p t) -> p b t", b=HP, t=4))
+
+        nc.sync.dma_start(offs_sb[:], offs)
+        load_table(0)
+        for q in range(4):
+            nc.sync.dma_start(
+                tab_plane[32 * q : 32 * q + 4 * KP, :].bitcast(I32),
+                tab_scales[:, 4 * q : 4 * q + 4, :].bitcast(I32),
+            )
+        load_w1(0, 0)
+        nc.sync.dma_start(
+            w4_raw[:].bitcast(I32).rearrange("p (a c) -> p a c", a=HP),
+            w4_words.bitcast(I32).rearrange("a p c -> p a c"),
+        )
+        load_vector(b1_sb, b1)
+        load_table(1)
+        for q in range(4):
+            nc.sync.dma_start(
+                w4_plane_raw[32 * q : 32 * q + 4, :].bitcast(I32).rearrange("r (a c) -> r a c", a=HP),
+                w4_scales[:, 4 * q : 4 * q + 4, :].bitcast(I32).rearrange("a r c -> r a c"),
+            )
+        load_w1(0, 1)
+        load_table(2)
+        nc.sync.dma_start(pos1_sb[:], pos1)
+        load_w1(0, 2)
+        load_w1(1, 0)
+        nc.sync.dma_start(pos2_sb[:], pos2)
+        load_vector(gain_sb, gain)
+        load_vector(b2_sb, b2)
+        load_w1(1, 1)
+        load_w1(1, 2)
+
+        warm = keep.tile([P, 1], F32, name="warm")
+        nc.scalar.activation(warm[:], b1_sb[:, 0, 0:1], ACT.Tanh)
+
+        v_words = []
+        v_plane = keep.tile([P, S], U8, name="v_plane", align_bytes=64)
+        for a in range(KP):
+            tile = keep.tile([P, S], U32, name="v_words_%d" % a, align_bytes=64)
+            nc.vector.tensor_copy(tile[:], table[a][:].indirect(offs_sb[:]))
+            v_words.append(tile)
+            if a == 0:
+                nc.vector.tensor_copy(v_plane[:], tab_plane[:].indirect(offs_sb[:]))
+
+        w1_codes, w1_planes = {}, {}
+
+        def quantise_w1(b):
+            for a in range(KP):
+                staged = []
+                for u in range(2):
+                    grouped = ring.tile([P, 1024], BF16, name="w1_bf", tag="stage%d%d" % (a, u), align_bytes=64)
+                    dst = grouped[:].rearrange("p (t m j) -> p m j t", t=2, j=4)
+                    src = w1_raw[b, a][:].rearrange("p j (m t) -> p m j t", t=4)[:, :, :, 2 * u : 2 * u + 2]
+                    if u == 0:
+                        nc.vector.tensor_copy(dst, src)
+                    else:
+                        nc.scalar.copy(dst, src)
+                    staged.append(grouped)
+                for u in range(2):
+                    codes = keep.tile([P, 256], U32, name="w1_codes_%d_%d_%d" % (b, a, u), align_bytes=64)
+                    plane = keep.tile([P, 256], U8, name="w1_plane_%d_%d_%d" % (b, a, u), align_bytes=64)
+                    nc.vector.quantize_mx(out=codes[:].bitcast(FP8X4), scales=plane[:], in_=staged[u][:])
+                    w1_codes[b, a, u], w1_planes[b, a, u] = codes, plane
+
+        h = {}
+
+        def first_product(b):
+            for t in range(4):
+                cols = slice(P * (t % 2), P * (t % 2 + 1))
+                banks = [psum.tile([P, BANK], F32, name="acc", tag="bank%d" % (2 * t + s)) for s in range(2)]
+                for a in range(KP):
+                    for s in range(2):
+                        picked = slice(BANK * s, BANK * (s + 1))
+                        nc.tensor.matmul_mx(
+                            out=banks[s][:],
+                            lhsT=w1_codes[b, a, t // 2][:, cols].bitcast(FP8X4),
+                            lhsT_scale=w1_planes[b, a, t // 2][:, cols],
+                            rhs=v_words[a][:, picked].bitcast(FP8X4),
+                            rhs_scale=v_plane[4 * a : P, picked],
+                            start=(a == 0),
+                            stop=(a == KP - 1),
+                        )
+                rows = keep.tile([P, S], F32, name="h_%d_%d" % (b, t), align_bytes=64)
+                for s in range(2):
+                    nc.scalar.copy(rows[:, BANK * s : BANK * (s + 1)], banks[s][:])
+                h[b, t] = rows
+
+        quantise_w1(0)
+        first_product(0)
+
+        w4_ord = keep.tile([P, HP * H], U16, name="w4_ord", align_bytes=64)
+        w4_plane = keep.tile([P, HP * H], U8, name="w4_plane", align_bytes=64)
+        nc.vector.tensor_copy(
+            w4_ord[:].rearrange("p (g t m) -> p g t m", t=4, m=P),
+            w4_raw[:].rearrange("p (g m t) -> p g t m", t=4, m=P),
+        )
+        nc.vector.tensor_copy(
+            w4_plane[:].rearrange("p (g t m) -> p g t m", t=4, m=P),
+            w4_plane_raw[:].rearrange("p (g m t) -> p g t m", t=4, m=P),
+        )
+
+        quantise_w1(1)
+
+        th = ring.tile([P, 8, M], F32, name="th", tag="big", bufs=3, align_bytes=64)
+        z_codes, z_planes = [], []
+        for b in range(HP):
+            if b == 1:
+                first_product(1)
+            z_rows = ring.tile([P, 4, M], BF16, name="z_rows", tag="z_rows%d" % b, align_bytes=64)
+            for t in range(4):
+                h1 = ring.tile([P, M], F32, name="h1", tag="h1_%d" % (4 * b + t), align_bytes=64)
+                nc.vector.tensor_copy(h1[:], h[b, t][:].indirect(pos1_sb[:]))
+                nc.scalar.activation(th[:, 4 * b + t, :], h1[:], ACT.Tanh, bias=b1_sb[:, b, t : t + 1])
+                nc.scalar.activation(
+                    z_rows[:, t, :], th[:, 4 * b + t, :], ACT.Copy, scale=gain_sb[:, b, t : t + 1]
+                )
+            z_il = ring.tile([P, 4 * M], BF16, name="z_il", tag="z_il", bufs=2, align_bytes=64)
+            nc.vector.tensor_copy(
+                z_il[:].rearrange("p (c i t) -> p c t i", i=4, t=4),
+                z_rows[:].rearrange("p t (c i) -> p c t i", i=4),
+            )
+            codes = keep.tile([P, M], U32, name="z_codes_%d" % b, align_bytes=64)
+            plane = keep.tile([P, M], U8, name="z_plane_%d" % b, align_bytes=64)
+            nc.vector.quantize_mx(out=codes[:].bitcast(FP8X4), scales=plane[:], in_=z_il[:])
+            z_codes.append(codes)
+            z_planes.append(plane)
+        h2 = []
+        for tag in ("stage10", "stage11", "stage20", "stage21", "h1_6", "h1_7"):
+            h2.append(ring.tile([P, M], F32, name="h2", tag=tag, align_bytes=64)[:])
+        h2_last = ring.tile([P, 2, M], F32, name="h2_last", tag="z_rows1", align_bytes=64)
+        h2.extend([h2_last[:, 0, :], h2_last[:, 1, :]])
+        for j in range(8):
+            nc.vector.tensor_copy(h2[j], h[j // 4, j % 4][:].indirect(pos2_sb[:]))
+
+        ys = []
+        for j in range(8):
+            y = psum.tile([P, M], F32, name="y", tag="bank%d" % j)
+            for a in range(HP):
+                cols = slice(H * a + P * j, H * a + P * (j + 1))
+                nc.tensor.matmul_mx(
+                    out=y[:],
+                    lhsT=w4_ord[:].bitcast(U8)[:, 2 * cols.start : 2 * cols.stop].bitcast(FP4X4),
+                    lhsT_scale=w4_plane[:, cols],
+                    rhs=z_codes[a][:].bitcast(FP8X4),
+                    rhs_scale=z_planes[a][:],
+                    start=(a == 0),
+                    stop=(a == HP - 1),
+                )
+            ys.append(y)
+
+        crossed = {}
+
+        def cross(j):
+            tile = ring.tile([P, M], F32, name="crossed", tag="crossed", bufs=4, align_bytes=64)
+            nc.vector.scalar_tensor_tensor(
+                tile[:], ys[j][:], b2_sb[:, j // 4, j % 4 : j % 4 + 1], th[:, j, :], ALU.add, ALU.mult
+            )
+            crossed[j] = tile
+
+        def finish(j):
+            nc.vector.tensor_tensor(h2[j], crossed[j][:], h2[j], ALU.add)
+            rows = out[512 * (j // 4) : 512 * (j // 4 + 1), :].rearrange("(p t) m -> p t m", t=4)
+            nc.sync.dma_start(rows[:, j % 4, :], h2[j])
+
+        cross(0)
+        for j in range(8):
+            if j + 1 < 8:
+                cross(j + 1)
+            finish(j)

@@ -41,7 +41,7 @@ def tile_list_recipe_citation_cross_kernel(
         w4_plane_raw = keep.tile([P, HP * H], U8, name="w4_plane_raw", align_bytes=64)
         w4_raw = keep.tile([P, HP * H], U16, name="w4_raw", align_bytes=64)
 
-        nc.vector.memset(tab_plane[:].bitcast(I32), 0)
+        nc.gpsimd.memset(tab_plane[:].bitcast(I32), 0)
         nc.vector.memset(w4_plane_raw[:].bitcast(I32), 0)
 
         table = []
@@ -64,19 +64,22 @@ def tile_list_recipe_citation_cross_kernel(
         def load_vector(tile, vec):
             nc.sync.dma_start(tile[:], vec.rearrange("(b p t) -> p b t", b=HP, t=4))
 
-        nc.sync.dma_start(offs_sb[:], offs)
-        load_table(0)
         for q in range(4):
-            nc.sync.dma_start(
+            (nc.scalar if q == 3 else nc.gpsimd).dma_start(
                 tab_plane[32 * q : 32 * q + 4 * KP, :].bitcast(I32),
                 tab_scales[:, 4 * q : 4 * q + 4, :].bitcast(I32),
             )
+        nc.sync.dma_start(offs_sb[:], offs)
+        load_table(0)
         load_w1(0, 0)
         nc.sync.dma_start(
             w4_raw[:].bitcast(I32).rearrange("p (a c) -> p a c", a=HP),
             w4_words.bitcast(I32).rearrange("a p c -> p a c"),
         )
         load_vector(b1_sb, b1)
+        nc.sync.dma_start(pos1_sb[:], pos1)
+        nc.sync.dma_start(pos2_sb[:], pos2)
+        load_vector(gain_sb, gain)
         load_table(1)
         for q in range(4):
             nc.sync.dma_start(
@@ -85,14 +88,10 @@ def tile_list_recipe_citation_cross_kernel(
             )
         load_w1(0, 1)
         load_table(2)
-        nc.sync.dma_start(pos1_sb[:], pos1)
         load_w1(0, 2)
-        load_w1(1, 0)
-        nc.sync.dma_start(pos2_sb[:], pos2)
-        load_vector(gain_sb, gain)
         load_vector(b2_sb, b2)
-        load_w1(1, 1)
-        load_w1(1, 2)
+        for a in range(KP):
+            load_w1(1, a)
 
         warm = keep.tile([P, 1], F32, name="warm")
         nc.scalar.activation(warm[:], b1_sb[:, 0, 0:1], ACT.Tanh)
@@ -115,7 +114,7 @@ def tile_list_recipe_citation_cross_kernel(
                     grouped = ring.tile([P, 1024], BF16, name="w1_bf", tag="stage%d%d" % (a, u), align_bytes=64)
                     dst = grouped[:].rearrange("p (t m j) -> p m j t", t=2, j=4)
                     src = w1_raw[b, a][:].rearrange("p j (m t) -> p m j t", t=4)[:, :, :, 2 * u : 2 * u + 2]
-                    if u == 0:
+                    if u == 0 and (b, a) >= (0, KP - 1):
                         nc.vector.tensor_copy(dst, src)
                     else:
                         nc.scalar.copy(dst, src)
@@ -212,22 +211,12 @@ def tile_list_recipe_citation_cross_kernel(
                 )
             ys.append(y)
 
-        crossed = {}
-
-        def cross(j):
-            tile = ring.tile([P, M], F32, name="crossed", tag="crossed", bufs=4, align_bytes=64)
+        for j in range(8):
             nc.vector.scalar_tensor_tensor(
-                tile[:], ys[j][:], b2_sb[:, j // 4, j % 4 : j % 4 + 1], th[:, j, :], ALU.add, ALU.mult
+                th[:, j, :], ys[j][:], b2_sb[:, j // 4, j % 4 : j % 4 + 1], th[:, j, :], ALU.add, ALU.mult
             )
-            crossed[j] = tile
-
-        def finish(j):
-            nc.vector.tensor_tensor(h2[j], crossed[j][:], h2[j], ALU.add)
+        for j in range(8):
+            engine = nc.gpsimd if j < 3 else nc.vector
+            engine.tensor_tensor(h2[j], th[:, j, :], h2[j], ALU.add)
             rows = out[512 * (j // 4) : 512 * (j // 4 + 1), :].rearrange("(p t) m -> p t m", t=4)
             nc.sync.dma_start(rows[:, j % 4, :], h2[j])
-
-        cross(0)
-        for j in range(8):
-            if j + 1 < 8:
-                cross(j + 1)
-            finish(j)

@@ -1,6 +1,7 @@
 from contextlib import ExitStack
 
 import concourse.mybir as mybir
+from concourse.masks import make_identity
 
 K, H, T, S, M = 1536, 1024, 4096, 1024, 512
 FLOPS = 2 * K * H * S + 2 * H * H * M
@@ -20,6 +21,9 @@ P = 128
 KP = K // 512
 HP = H // 512
 BANK = 512
+TILES = H // P
+GROUP = 256
+GROUPS = H // GROUP
 
 
 def tile_list_recipe_citation_cross_kernel(
@@ -34,67 +38,74 @@ def tile_list_recipe_citation_cross_kernel(
         offs_sb = keep.tile([P, S // 16], U16, name="offs_sb")
         pos1_sb = keep.tile([P, M // 16], U16, name="pos1_sb")
         pos2_sb = keep.tile([P, M // 16], U16, name="pos2_sb")
-        b1_sb = keep.tile([P, HP, 4], F32, name="b1_sb")
-        gain_sb = keep.tile([P, HP, 4], F32, name="gain_sb")
-        b2_sb = keep.tile([P, HP, 4], F32, name="b2_sb")
+        vec_rows = keep.tile([P, P], F32, name="vec_rows")
+        vec_cols = keep.tile([P, 3 * TILES], F32, name="vec_cols")
+        ident = keep.tile([P, P], F32, name="ident")
         tab_plane = keep.tile([P, T], U8, name="tab_plane", align_bytes=64)
-        w4_plane_raw = keep.tile([P, HP * H], U8, name="w4_plane_raw", align_bytes=64)
-        w4_raw = keep.tile([P, HP * H], U16, name="w4_raw", align_bytes=64)
+        w4_plane = keep.tile([P, HP * H], U8, name="w4_plane", align_bytes=64)
+        w4_sb = keep.tile([P, HP * 2 * H], U8, name="w4_sb", align_bytes=64)
 
-        nc.gpsimd.memset(tab_plane[:].bitcast(I32), 0)
-        nc.vector.memset(w4_plane_raw[:].bitcast(I32), 0)
+        nc.vector.memset(tab_plane[:].bitcast(I32), 0)
+        nc.vector.memset(vec_rows[:], 0.0)
+        nc.vector.memset(w4_plane[:].bitcast(I32), 0)
 
         table = []
+        w1_raw = {}
 
         def load_table(a):
             tile = ring.tile([P, T], U32, name="table", tag="big", bufs=3, align_bytes=64)
             nc.sync.dma_start(tile[:].bitcast(I32), tab_words[a].rearrange("p t i -> p (t i)").bitcast(I32))
             table.append(tile)
 
-        w1_raw = {}
-
-        def load_w1(b, a):
-            tile = keep.tile([P, 4, 512], F32, name="w1_raw_%d_%d" % (b, a))
+        def load_w1(g, a):
+            tile = keep.tile([P, 4, GROUP], F32, name="w1_raw_%d_%d" % (g, a))
             nc.sync.dma_start(
                 tile[:],
-                w1[512 * a : 512 * (a + 1), 512 * b : 512 * (b + 1)].rearrange("(p j) c -> p j c", j=4),
+                w1[512 * a : 512 * (a + 1), GROUP * g : GROUP * (g + 1)].rearrange("(p j) c -> p j c", j=4),
             )
-            w1_raw[b, a] = tile
+            w1_raw[g, a] = tile
 
-        def load_vector(tile, vec):
-            nc.sync.dma_start(tile[:], vec.rearrange("(b p t) -> p b t", b=HP, t=4))
-
+        nc.sync.dma_start(offs_sb[:], offs)
+        load_table(0)
         for q in range(4):
-            (nc.scalar if q == 3 else nc.gpsimd).dma_start(
+            (nc.sync if q == 3 else nc.gpsimd).dma_start(
                 tab_plane[32 * q : 32 * q + 4 * KP, :].bitcast(I32),
                 tab_scales[:, 4 * q : 4 * q + 4, :].bitcast(I32),
             )
-        nc.sync.dma_start(offs_sb[:], offs)
-        load_table(0)
+        for i, vec in enumerate((b1, gain, b2)):
+            nc.sync.dma_start(vec_rows[TILES * i : TILES * (i + 1), :], vec.rearrange("(j p) -> j p", p=P))
         load_w1(0, 0)
-        nc.sync.dma_start(
-            w4_raw[:].bitcast(I32).rearrange("p (a c) -> p a c", a=HP),
-            w4_words.bitcast(I32).rearrange("a p c -> p a c"),
-        )
-        load_vector(b1_sb, b1)
-        nc.sync.dma_start(pos1_sb[:], pos1)
-        nc.sync.dma_start(pos2_sb[:], pos2)
-        load_vector(gain_sb, gain)
-        load_table(1)
-        for q in range(4):
-            nc.sync.dma_start(
-                w4_plane_raw[32 * q : 32 * q + 4, :].bitcast(I32).rearrange("r (a c) -> r a c", a=HP),
-                w4_scales[:, 4 * q : 4 * q + 4, :].bitcast(I32).rearrange("a r c -> r a c"),
-            )
         load_w1(0, 1)
+        nc.sync.dma_start(pos1_sb[:], pos1)
+        load_table(1)
         load_table(2)
         load_w1(0, 2)
-        load_vector(b2_sb, b2)
-        for a in range(KP):
-            load_w1(1, a)
+        load_w1(1, 0)
+        nc.sync.dma_start(pos2_sb[:], pos2)
+        load_w1(1, 1)
+        load_w1(1, 2)
+        for g in range(2, GROUPS):
+            for a in range(KP):
+                load_w1(g, a)
+        nc.sync.dma_start(
+            w4_sb[:].bitcast(I32).rearrange("p (a c) -> p a c", a=HP),
+            w4_words.bitcast(I32).rearrange("a p c -> p a c"),
+        )
+        for q in range(4):
+            nc.sync.dma_start(
+                w4_plane[32 * q : 32 * q + 4, :].bitcast(I32).rearrange("r (a c) -> r a c", a=HP),
+                w4_scales[:, 4 * q : 4 * q + 4, :].bitcast(I32).rearrange("a r c -> r a c"),
+            )
 
+        make_identity(nc, ident[:])
         warm = keep.tile([P, 1], F32, name="warm")
-        nc.scalar.activation(warm[:], b1_sb[:, 0, 0:1], ACT.Tanh)
+        nc.scalar.activation(warm[:], vec_rows[:, 0:1], ACT.Tanh)
+        turned = psum.tile([P, P], F32, name="turned", tag="bank7")
+        nc.tensor.transpose(turned[:], vec_rows[:], ident[:])
+        nc.scalar.copy(vec_cols[:], turned[:, 0 : 3 * TILES])
+
+        def column(i, j):
+            return vec_cols[:, TILES * i + j : TILES * i + j + 1]
 
         v_words = []
         v_plane = keep.tile([P, S], U8, name="v_plane", align_bytes=64)
@@ -107,103 +118,91 @@ def tile_list_recipe_citation_cross_kernel(
 
         w1_codes, w1_planes = {}, {}
 
-        def quantise_w1(b):
+        def quantise_w1(g):
             for a in range(KP):
-                staged = []
-                for u in range(2):
-                    grouped = ring.tile([P, 1024], BF16, name="w1_bf", tag="stage%d%d" % (a, u), align_bytes=64)
-                    dst = grouped[:].rearrange("p (t m j) -> p m j t", t=2, j=4)
-                    src = w1_raw[b, a][:].rearrange("p j (m t) -> p m j t", t=4)[:, :, :, 2 * u : 2 * u + 2]
-                    if u == 0 and (b, a) >= (0, KP - 1):
-                        nc.vector.tensor_copy(dst, src)
-                    else:
-                        nc.scalar.copy(dst, src)
-                    staged.append(grouped)
-                for u in range(2):
-                    codes = keep.tile([P, 256], U32, name="w1_codes_%d_%d_%d" % (b, a, u), align_bytes=64)
-                    plane = keep.tile([P, 256], U8, name="w1_plane_%d_%d_%d" % (b, a, u), align_bytes=64)
-                    nc.vector.quantize_mx(out=codes[:].bitcast(FP8X4), scales=plane[:], in_=staged[u][:])
-                    w1_codes[b, a, u], w1_planes[b, a, u] = codes, plane
+                grouped = ring.tile([P, 4 * GROUP], BF16, name="w1_bf", tag="stage%d%d" % (g % 2, a), align_bytes=64)
+                dst = grouped[:].rearrange("p (c i j) -> p c j i", i=4, j=4)
+                src = w1_raw[g, a][:].rearrange("p j (c i) -> p c j i", i=4)
+                if g % 2 == 1:
+                    nc.vector.tensor_copy(dst, src)
+                else:
+                    nc.scalar.copy(dst, src)
+                codes = keep.tile([P, GROUP], U32, name="w1_codes_%d_%d" % (g, a), align_bytes=64)
+                plane = keep.tile([P, GROUP], U8, name="w1_plane_%d_%d" % (g, a), align_bytes=64)
+                nc.vector.quantize_mx(out=codes[:].bitcast(FP8X4), scales=plane[:], in_=grouped[:])
+                w1_codes[g, a], w1_planes[g, a] = codes, plane
 
         h = {}
 
-        def first_product(b):
-            for t in range(4):
-                cols = slice(P * (t % 2), P * (t % 2 + 1))
-                banks = [psum.tile([P, BANK], F32, name="acc", tag="bank%d" % (2 * t + s)) for s in range(2)]
+        def first_product(g):
+            for e in range(2):
+                j = 2 * g + e
+                cols = slice(P * e, P * (e + 1))
+                banks = [psum.tile([P, BANK], F32, name="acc", tag="bank%d" % (2 * (j % 4) + s)) for s in range(2)]
                 for a in range(KP):
                     for s in range(2):
                         picked = slice(BANK * s, BANK * (s + 1))
                         nc.tensor.matmul_mx(
                             out=banks[s][:],
-                            lhsT=w1_codes[b, a, t // 2][:, cols].bitcast(FP8X4),
-                            lhsT_scale=w1_planes[b, a, t // 2][:, cols],
+                            lhsT=w1_codes[g, a][:, cols].bitcast(FP8X4),
+                            lhsT_scale=w1_planes[g, a][:, cols],
                             rhs=v_words[a][:, picked].bitcast(FP8X4),
                             rhs_scale=v_plane[4 * a : P, picked],
                             start=(a == 0),
                             stop=(a == KP - 1),
                         )
-                rows = keep.tile([P, S], F32, name="h_%d_%d" % (b, t), align_bytes=64)
+                rows = keep.tile([P, S], F32, name="h_%d" % j, align_bytes=64)
                 for s in range(2):
                     nc.scalar.copy(rows[:, BANK * s : BANK * (s + 1)], banks[s][:])
-                h[b, t] = rows
+                h[j] = rows
 
         quantise_w1(0)
         first_product(0)
+        for g in range(1, GROUPS):
+            quantise_w1(g)
+        first_product(1)
 
-        w4_ord = keep.tile([P, HP * H], U16, name="w4_ord", align_bytes=64)
-        w4_plane = keep.tile([P, HP * H], U8, name="w4_plane", align_bytes=64)
-        nc.vector.tensor_copy(
-            w4_ord[:].rearrange("p (g t m) -> p g t m", t=4, m=P),
-            w4_raw[:].rearrange("p (g m t) -> p g t m", t=4, m=P),
-        )
-        nc.vector.tensor_copy(
-            w4_plane[:].rearrange("p (g t m) -> p g t m", t=4, m=P),
-            w4_plane_raw[:].rearrange("p (g m t) -> p g t m", t=4, m=P),
-        )
-
-        quantise_w1(1)
-
-        th = ring.tile([P, 8, M], F32, name="th", tag="big", bufs=3, align_bytes=64)
+        th = ring.tile([P, TILES, M], F32, name="th", tag="big", bufs=3, align_bytes=64)
         z_codes, z_planes = [], []
         for b in range(HP):
             if b == 1:
-                first_product(1)
-            z_rows = ring.tile([P, 4, M], BF16, name="z_rows", tag="z_rows%d" % b, align_bytes=64)
-            for t in range(4):
-                h1 = ring.tile([P, M], F32, name="h1", tag="h1_%d" % (4 * b + t), align_bytes=64)
-                nc.vector.tensor_copy(h1[:], h[b, t][:].indirect(pos1_sb[:]))
-                nc.scalar.activation(th[:, 4 * b + t, :], h1[:], ACT.Tanh, bias=b1_sb[:, b, t : t + 1])
-                nc.scalar.activation(
-                    z_rows[:, t, :], th[:, 4 * b + t, :], ACT.Copy, scale=gain_sb[:, b, t : t + 1]
-                )
+                first_product(2)
+                first_product(3)
+            z_moved = ring.tile([P, 4 * M], BF16, name="z_moved", tag="z_moved%d" % b, align_bytes=64)
+            for i in range(4):
+                j = 4 * b + i
+                h1 = ring.tile([P, M], F32, name="h1", tag="h1_%d" % j, align_bytes=64)
+                nc.vector.tensor_copy(h1[:], h[j][:].indirect(pos1_sb[:]))
+                nc.scalar.activation(th[:, j, :], h1[:], ACT.Tanh, bias=column(0, j))
+                z_rows = keep.tile([P, M], BF16, name="z_rows_%d" % j, align_bytes=64)
+                nc.scalar.activation(z_rows[:], th[:, j, :], ACT.Copy, scale=column(1, j))
+                nc.sync.dma_start(z_moved[32 * i : 32 * (i + 1), :], z_rows[:])
             z_il = ring.tile([P, 4 * M], BF16, name="z_il", tag="z_il", bufs=2, align_bytes=64)
             nc.vector.tensor_copy(
                 z_il[:].rearrange("p (c i t) -> p c t i", i=4, t=4),
-                z_rows[:].rearrange("p t (c i) -> p c t i", i=4),
+                z_moved[:].rearrange("p (t c i) -> p c t i", i=4, t=4),
             )
             codes = keep.tile([P, M], U32, name="z_codes_%d" % b, align_bytes=64)
             plane = keep.tile([P, M], U8, name="z_plane_%d" % b, align_bytes=64)
             nc.vector.quantize_mx(out=codes[:].bitcast(FP8X4), scales=plane[:], in_=z_il[:])
             z_codes.append(codes)
             z_planes.append(plane)
+
         h2 = []
-        for tag in ("stage10", "stage11", "stage20", "stage21", "h1_6", "h1_7"):
-            h2.append(ring.tile([P, M], F32, name="h2", tag=tag, align_bytes=64)[:])
-        h2_last = ring.tile([P, 2, M], F32, name="h2_last", tag="z_rows1", align_bytes=64)
-        h2.extend([h2_last[:, 0, :], h2_last[:, 1, :]])
-        for j in range(8):
-            nc.vector.tensor_copy(h2[j], h[j // 4, j % 4][:].indirect(pos2_sb[:]))
+        reused = ["stage1%d" % a for a in range(KP)] + ["h1_%d" % j for j in range(4, TILES)] + ["z_moved1"]
+        for j in range(TILES):
+            h2.append(ring.tile([P, M], F32, name="h2", tag=reused[j], align_bytes=64))
+            nc.vector.tensor_copy(h2[j][:], h[j][:].indirect(pos2_sb[:]))
 
         ys = []
-        for j in range(8):
+        for j in range(TILES):
             y = psum.tile([P, M], F32, name="y", tag="bank%d" % j)
             for a in range(HP):
-                cols = slice(H * a + P * j, H * a + P * (j + 1))
+                n0 = H * a + P * j
                 nc.tensor.matmul_mx(
                     out=y[:],
-                    lhsT=w4_ord[:].bitcast(U8)[:, 2 * cols.start : 2 * cols.stop].bitcast(FP4X4),
-                    lhsT_scale=w4_plane[:, cols],
+                    lhsT=w4_sb[:, 2 * n0 : 2 * (n0 + P)].bitcast(FP4X4),
+                    lhsT_scale=w4_plane[:, n0 : n0 + P],
                     rhs=z_codes[a][:].bitcast(FP8X4),
                     rhs_scale=z_planes[a][:],
                     start=(a == 0),
@@ -211,12 +210,9 @@ def tile_list_recipe_citation_cross_kernel(
                 )
             ys.append(y)
 
-        for j in range(8):
-            nc.vector.scalar_tensor_tensor(
-                th[:, j, :], ys[j][:], b2_sb[:, j // 4, j % 4 : j % 4 + 1], th[:, j, :], ALU.add, ALU.mult
-            )
-        for j in range(8):
+        for j in range(TILES):
+            nc.vector.scalar_tensor_tensor(th[:, j, :], ys[j][:], column(2, j), th[:, j, :], ALU.add, ALU.mult)
+        for j in range(TILES):
             engine = nc.gpsimd if j < 3 else nc.vector
-            engine.tensor_tensor(h2[j], th[:, j, :], h2[j], ALU.add)
-            rows = out[512 * (j // 4) : 512 * (j // 4 + 1), :].rearrange("(p t) m -> p t m", t=4)
-            nc.sync.dma_start(rows[:, j % 4, :], h2[j])
+            engine.tensor_tensor(h2[j][:], th[:, j, :], h2[j][:], ALU.add)
+            nc.sync.dma_start(out[P * j : P * (j + 1), :], h2[j][:])

@@ -75,10 +75,10 @@ def tile_list_recipe_citation_cross_kernel(
         for i, vec in enumerate((b1, gain, b2)):
             nc.sync.dma_start(vec_rows[TILES * i : TILES * (i + 1), :], vec.rearrange("(j p) -> j p", p=P))
         load_w1(0, 0)
-        load_w1(0, 1)
-        nc.sync.dma_start(pos1_sb[:], pos1)
         load_table(1)
+        load_w1(0, 1)
         load_table(2)
+        nc.sync.dma_start(pos1_sb[:], pos1)
         load_w1(0, 2)
         load_w1(1, 0)
         nc.sync.dma_start(pos2_sb[:], pos2)
@@ -123,7 +123,7 @@ def tile_list_recipe_citation_cross_kernel(
                 grouped = ring.tile([P, 4 * GROUP], BF16, name="w1_bf", tag="stage%d%d" % (g % 2, a), align_bytes=64)
                 dst = grouped[:].rearrange("p (c i j) -> p c j i", i=4, j=4)
                 src = w1_raw[g, a][:].rearrange("p j (c i) -> p c j i", i=4)
-                if g % 2 == 1:
+                if g > 0 and a > 0:
                     nc.vector.tensor_copy(dst, src)
                 else:
                     nc.scalar.copy(dst, src)
@@ -156,37 +156,42 @@ def tile_list_recipe_citation_cross_kernel(
                     nc.scalar.copy(rows[:, BANK * s : BANK * (s + 1)], banks[s][:])
                 h[j] = rows
 
-        quantise_w1(0)
-        first_product(0)
-        for g in range(1, GROUPS):
-            quantise_w1(g)
-        first_product(1)
-
         th = ring.tile([P, TILES, M], F32, name="th", tag="big", bufs=3, align_bytes=64)
-        z_codes, z_planes = [], []
-        for b in range(HP):
-            if b == 1:
-                first_product(2)
-                first_product(3)
-            z_moved = ring.tile([P, 4 * M], BF16, name="z_moved", tag="z_moved%d" % b, align_bytes=64)
-            for i in range(4):
-                j = 4 * b + i
+        z_moved, z_codes, z_planes = [], [], []
+
+        def bound(g):
+            b = g // 2
+            if g % 2 == 0:
+                z_moved.append(ring.tile([P, 4 * M], BF16, name="z_moved", tag="z_moved%d" % b, align_bytes=64))
+            for j in (2 * g, 2 * g + 1):
+                i = j % 4
                 h1 = ring.tile([P, M], F32, name="h1", tag="h1_%d" % j, align_bytes=64)
                 nc.vector.tensor_copy(h1[:], h[j][:].indirect(pos1_sb[:]))
                 nc.scalar.activation(th[:, j, :], h1[:], ACT.Tanh, bias=column(0, j))
                 z_rows = keep.tile([P, M], BF16, name="z_rows_%d" % j, align_bytes=64)
                 nc.scalar.activation(z_rows[:], th[:, j, :], ACT.Copy, scale=column(1, j))
-                nc.sync.dma_start(z_moved[32 * i : 32 * (i + 1), :], z_rows[:])
-            z_il = ring.tile([P, 4 * M], BF16, name="z_il", tag="z_il", bufs=2, align_bytes=64)
-            nc.vector.tensor_copy(
-                z_il[:].rearrange("p (c i t) -> p c t i", i=4, t=4),
-                z_moved[:].rearrange("p (t c i) -> p c t i", i=4, t=4),
-            )
-            codes = keep.tile([P, M], U32, name="z_codes_%d" % b, align_bytes=64)
-            plane = keep.tile([P, M], U8, name="z_plane_%d" % b, align_bytes=64)
-            nc.vector.quantize_mx(out=codes[:].bitcast(FP8X4), scales=plane[:], in_=z_il[:])
-            z_codes.append(codes)
-            z_planes.append(plane)
+                nc.sync.dma_start(z_moved[b][32 * i : 32 * (i + 1), :], z_rows[:])
+            if g % 2 == 1:
+                z_il = ring.tile([P, 4 * M], BF16, name="z_il", tag="z_il", bufs=2, align_bytes=64)
+                nc.vector.tensor_copy(
+                    z_il[:].rearrange("p (c i t) -> p c t i", i=4, t=4),
+                    z_moved[b][:].rearrange("p (t c i) -> p c t i", i=4, t=4),
+                )
+                codes = keep.tile([P, M], U32, name="z_codes_%d" % b, align_bytes=64)
+                plane = keep.tile([P, M], U8, name="z_plane_%d" % b, align_bytes=64)
+                nc.vector.quantize_mx(out=codes[:].bitcast(FP8X4), scales=plane[:], in_=z_il[:])
+                z_codes.append(codes)
+                z_planes.append(plane)
+
+        for g in range(2):
+            quantise_w1(g)
+            first_product(g)
+        for g in range(2, GROUPS):
+            quantise_w1(g)
+        for g in range(GROUPS):
+            bound(g)
+            if g + 2 < GROUPS:
+                first_product(g + 2)
 
         h2 = []
         reused = ["stage1%d" % a for a in range(KP)] + ["h1_%d" % j for j in range(4, TILES)] + ["z_moved1"]
@@ -214,5 +219,8 @@ def tile_list_recipe_citation_cross_kernel(
             nc.vector.scalar_tensor_tensor(th[:, j, :], ys[j][:], column(2, j), th[:, j, :], ALU.add, ALU.mult)
         for j in range(TILES):
             engine = nc.gpsimd if j < 3 else nc.vector
-            engine.tensor_tensor(h2[j][:], th[:, j, :], h2[j][:], ALU.add)
-            nc.sync.dma_start(out[P * j : P * (j + 1), :], h2[j][:])
+            width = M // 2 if j == TILES - 1 else M
+            for m0 in range(0, M, width):
+                cols = slice(m0, m0 + width)
+                engine.tensor_tensor(h2[j][:, cols], th[:, j, cols], h2[j][:, cols], ALU.add)
+                nc.sync.dma_start(out[P * j : P * (j + 1), cols], h2[j][:, cols])

@@ -98,8 +98,6 @@ def tile_list_recipe_citation_cross_kernel(
             )
 
         make_identity(nc, ident[:])
-        warm = keep.tile([P, 1], F32, name="warm")
-        nc.scalar.activation(warm[:], vec_rows[:, 0:1], ACT.Tanh)
         turned = psum.tile([P, P], F32, name="turned", tag="bank7")
         nc.tensor.transpose(turned[:], vec_rows[:], ident[:])
         nc.scalar.copy(vec_cols[:], turned[:, 0 : 3 * TILES])

@@ -24,6 +24,7 @@ BANK = 512
 TILES = H // P
 GROUP = 256
 GROUPS = H // GROUP
+PLAIN = 4
 
 
 def tile_list_recipe_citation_cross_kernel(
@@ -192,8 +193,8 @@ def tile_list_recipe_citation_cross_kernel(
                 first_product(g + 2)
 
         h2 = []
-        reused = ["stage1%d" % a for a in range(KP)] + ["h1_%d" % j for j in range(4, TILES)] + ["z_moved1"]
-        for j in range(TILES):
+        reused = ["h1_%d" % j for j in range(5, TILES)] + ["z_moved1"]
+        for j in range(PLAIN):
             h2.append(ring.tile([P, M], F32, name="h2", tag=reused[j], align_bytes=64))
             nc.vector.tensor_copy(h2[j][:], h[j][:].indirect(pos2_sb[:]))
 
@@ -215,10 +216,15 @@ def tile_list_recipe_citation_cross_kernel(
 
         for j in range(TILES):
             nc.vector.scalar_tensor_tensor(th[:, j, :], ys[j][:], column(2, j), th[:, j, :], ALU.add, ALU.mult)
-        for j in range(TILES):
+        for j in range(PLAIN):
             engine = nc.gpsimd if j < 3 else nc.vector
+            engine.tensor_tensor(h2[j][:], th[:, j, :], h2[j][:], ALU.add)
+            nc.sync.dma_start(out[P * j : P * (j + 1), :], h2[j][:])
+        result = ring.tile([P, TILES - PLAIN, M], F32, name="result", tag="big", bufs=3, align_bytes=64)
+        for j in range(PLAIN, TILES):
             width = M // 2 if j == TILES - 1 else M
             for m0 in range(0, M, width):
                 cols = slice(m0, m0 + width)
-                engine.tensor_tensor(h2[j][:, cols], th[:, j, cols], h2[j][:, cols], ALU.add)
-                nc.sync.dma_start(out[P * j : P * (j + 1), cols], h2[j][:, cols])
+                picks = pos2_sb[:, m0 // 16 : (m0 + width) // 16]
+                nc.vector.tensor_tensor(result[:, j - PLAIN, cols], h[j][:].indirect(picks), th[:, j, cols], ALU.add)
+                nc.sync.dma_start(out[P * j : P * (j + 1), cols], result[:, j - PLAIN, cols])

@@ -24,7 +24,8 @@ BANK = 512
 TILES = H // P
 GROUP = 256
 GROUPS = H // GROUP
-PLAIN = 4
+PLAIN = 5
+ON_GPSIMD = 3
 
 
 def tile_list_recipe_citation_cross_kernel(
@@ -172,10 +173,12 @@ def tile_list_recipe_citation_cross_kernel(
                 nc.sync.dma_start(z_moved[b][32 * i : 32 * (i + 1), :], z_rows[:])
             if g % 2 == 1:
                 z_il = ring.tile([P, 4 * M], BF16, name="z_il", tag="z_il", bufs=2, align_bytes=64)
-                nc.vector.tensor_copy(
-                    z_il[:].rearrange("p (c i t) -> p c t i", i=4, t=4),
-                    z_moved[b][:].rearrange("p (t c i) -> p c t i", i=4, t=4),
-                )
+                dst = z_il[:].rearrange("p (c i t) -> p c t i", i=4, t=4)
+                src = z_moved[b][:].rearrange("p (t c i) -> p c t i", i=4, t=4)
+                shared = 40 if b == HP - 1 else 0
+                if shared:
+                    nc.scalar.copy(dst[:, 0:shared], src[:, 0:shared])
+                nc.vector.tensor_copy(dst[:, shared:], src[:, shared:])
                 codes = keep.tile([P, M], U32, name="z_codes_%d" % b, align_bytes=64)
                 plane = keep.tile([P, M], U8, name="z_plane_%d" % b, align_bytes=64)
                 nc.vector.quantize_mx(out=codes[:].bitcast(FP8X4), scales=plane[:], in_=z_il[:])
@@ -193,10 +196,11 @@ def tile_list_recipe_citation_cross_kernel(
                 first_product(g + 2)
 
         h2 = []
-        reused = ["h1_%d" % j for j in range(5, TILES)] + ["z_moved1"]
-        for j in range(PLAIN):
-            h2.append(ring.tile([P, M], F32, name="h2", tag=reused[j], align_bytes=64))
-            nc.vector.tensor_copy(h2[j][:], h[j][:].indirect(pos2_sb[:]))
+        for tag, count in (("h1_5", 1), ("h1_6", 1), ("h1_7", 2), ("z_moved1", 1)):
+            picked = ring.tile([P, count, M], F32, name="h2", tag=tag, align_bytes=64)
+            for e in range(count):
+                nc.vector.tensor_copy(picked[:, e, :], h[len(h2)][:].indirect(pos2_sb[:]))
+                h2.append(picked[:, e, :])
 
         ys = []
         for j in range(TILES):
@@ -216,10 +220,24 @@ def tile_list_recipe_citation_cross_kernel(
 
         for j in range(TILES):
             nc.vector.scalar_tensor_tensor(th[:, j, :], ys[j][:], column(2, j), th[:, j, :], ALU.add, ALU.mult)
-        for j in range(PLAIN):
-            engine = nc.gpsimd if j < 3 else nc.vector
-            engine.tensor_tensor(h2[j][:], th[:, j, :], h2[j][:], ALU.add)
-            nc.sync.dma_start(out[P * j : P * (j + 1), :], h2[j][:])
+        for j in range(ON_GPSIMD):
+            nc.gpsimd.tensor_tensor(h2[j], th[:, j, :], h2[j], ALU.add)
+            nc.sync.dma_start(out[P * j : P * (j + 1), :], h2[j])
+        for j in range(ON_GPSIMD, PLAIN):
+            first = 2 * (j - ON_GPSIMD)
+            summed = psum.tile([P, M], F32, name="summed", tag="bank%d" % first)
+            for m0 in range(0, M, P):
+                cols = slice(m0, m0 + P)
+                nc.tensor.matmul(summed[:, cols], h2[j][:, cols], ident[:], start=True, stop=False, is_transpose=True)
+                nc.tensor.matmul(summed[:, cols], th[:, j, cols], ident[:], start=False, stop=True, is_transpose=True)
+            turned_sum = keep.tile([P, M], F32, name="turned_sum_%d" % j, align_bytes=64)
+            nc.scalar.copy(turned_sum[:], summed[:])
+            back = psum.tile([P, M], F32, name="back", tag="bank%d" % (first + 1))
+            for m0 in range(0, M, P):
+                cols = slice(m0, m0 + P)
+                nc.tensor.transpose(back[:, cols], turned_sum[:, cols], ident[:])
+            nc.scalar.copy(h2[j], back[:])
+            nc.scalar.dma_start(out[P * j : P * (j + 1), :], h2[j])
         result = ring.tile([P, TILES - PLAIN, M], F32, name="result", tag="big", bufs=3, align_bytes=64)
         for j in range(PLAIN, TILES):
             width = M // 2 if j == TILES - 1 else M

@@ -43,7 +43,7 @@ def tile_list_recipe_citation_cross_kernel(
         vec_rows = keep.tile([P, P], F32, name="vec_rows")
         vec_cols = keep.tile([P, 3 * TILES], F32, name="vec_cols")
         ident = keep.tile([P, P], F32, name="ident")
-        tab_plane = keep.tile([P, T], U8, name="tab_plane", align_bytes=64)
+        tab_plane = ring.tile([P, T], U8, name="tab_plane", tag="words1", align_bytes=64)
         w4_plane = keep.tile([P, HP * H], U8, name="w4_plane", align_bytes=64)
         w4_sb = keep.tile([P, HP * 2 * H], U8, name="w4_sb", align_bytes=64)
 
@@ -60,7 +60,7 @@ def tile_list_recipe_citation_cross_kernel(
             table.append(tile)
 
         def load_w1(g, a):
-            tile = keep.tile([P, 4, GROUP], F32, name="w1_raw_%d_%d" % (g, a))
+            tile = ring.tile([P, 4, GROUP], F32, name="w1_raw", tag="raw%d%d" % (g, a), align_bytes=64)
             nc.sync.dma_start(
                 tile[:],
                 w1[512 * a : 512 * (a + 1), GROUP * g : GROUP * (g + 1)].rearrange("(p j) c -> p j c", j=4),
@@ -74,14 +74,19 @@ def tile_list_recipe_citation_cross_kernel(
                 tab_plane[32 * q : 32 * q + 4 * KP, :].bitcast(I32),
                 tab_scales[:, 4 * q : 4 * q + 4, :].bitcast(I32),
             )
+        load_w1(0, 0)
+        load_w1(0, 1)
         for i, vec in enumerate((b1, gain, b2)):
             nc.sync.dma_start(vec_rows[TILES * i : TILES * (i + 1), :], vec.rearrange("(j p) -> j p", p=P))
-        load_w1(0, 0)
-        load_table(1)
-        load_w1(0, 1)
-        load_table(2)
         nc.sync.dma_start(pos1_sb[:], pos1)
-        load_w1(0, 2)
+        load_table(1)
+        load_table(2)
+        w1_last = []
+        for e in range(2):
+            w1_last.append(keep.tile([P, 4, P], F32, name="w1_last_%d" % e))
+            nc.sync.dma_start(
+                w1_last[e][:], w1[512 * (KP - 1) :, P * e : P * (e + 1)].rearrange("(p j) c -> p j c", j=4)
+            )
         load_w1(1, 0)
         nc.sync.dma_start(pos2_sb[:], pos2)
         load_w1(1, 1)
@@ -109,44 +114,61 @@ def tile_list_recipe_citation_cross_kernel(
 
         v_words = []
         v_plane = keep.tile([P, S], U8, name="v_plane", align_bytes=64)
-        for a in range(KP):
-            tile = keep.tile([P, S], U32, name="v_words_%d" % a, align_bytes=64)
+        for a in range(KP - 1):
+            tile = ring.tile([P, S], U32, name="v_words", tag="words%d" % a, align_bytes=64)
             nc.vector.tensor_copy(tile[:], table[a][:].indirect(offs_sb[:]))
-            v_words.append(tile)
+            v_words.append([tile[:, BANK * s : BANK * (s + 1)] for s in range(2)])
             if a == 0:
                 nc.vector.tensor_copy(v_plane[:], tab_plane[:].indirect(offs_sb[:]))
 
-        w1_codes, w1_planes = {}, {}
+        w1_codes = {}
+
+        def quantise_piece(raw, first, a, tag, on_vector):
+            width = raw.shape[2]
+            grouped = ring.tile([P, 4 * width], BF16, name="w1_bf", tag=tag, align_bytes=64)
+            dst = grouped[:].rearrange("p (c i j) -> p c j i", i=4, j=4)
+            src = raw[:].rearrange("p j (c i) -> p c j i", i=4)
+            if on_vector:
+                nc.vector.tensor_copy(dst, src)
+            else:
+                nc.scalar.copy(dst, src)
+            codes = ring.tile([P, width], U32, name="w1_codes", tag="codes%d%d" % (first, a), align_bytes=64)
+            plane = keep.tile([P, width], U8, name="w1_plane_%d_%d" % (first, a), align_bytes=64)
+            nc.vector.quantize_mx(out=codes[:].bitcast(FP8X4), scales=plane[:], in_=grouped[:])
+            for e in range(width // P):
+                w1_codes[first + e, a] = (codes[:, P * e : P * (e + 1)], plane[:, P * e : P * (e + 1)])
 
         def quantise_w1(g):
             for a in range(KP):
-                grouped = ring.tile([P, 4 * GROUP], BF16, name="w1_bf", tag="stage%d%d" % (g % 2, a), align_bytes=64)
-                dst = grouped[:].rearrange("p (c i j) -> p c j i", i=4, j=4)
-                src = w1_raw[g, a][:].rearrange("p j (c i) -> p c j i", i=4)
-                if g > 0 and a > 0:
-                    nc.vector.tensor_copy(dst, src)
-                else:
-                    nc.scalar.copy(dst, src)
-                codes = keep.tile([P, GROUP], U32, name="w1_codes_%d_%d" % (g, a), align_bytes=64)
-                plane = keep.tile([P, GROUP], U8, name="w1_plane_%d_%d" % (g, a), align_bytes=64)
-                nc.vector.quantize_mx(out=codes[:].bitcast(FP8X4), scales=plane[:], in_=grouped[:])
-                w1_codes[g, a], w1_planes[g, a] = codes, plane
+                quantise_piece(w1_raw[g, a], 2 * g, a, "stage%d%d" % (g % 2, a), a > 0)
+
+        def gather_last(s, tag):
+            tile = ring.tile([P, BANK], U32, name="v_last", tag=tag, align_bytes=64)
+            picks = offs_sb[:, BANK * s // 16 : BANK * (s + 1) // 16]
+            nc.vector.tensor_copy(tile[:], table[KP - 1][:].indirect(picks))
+            return tile[:]
+
+        for a in range(KP - 1):
+            quantise_piece(w1_raw[0, a], 0, a, "stage0%d" % a, False)
+        v_words.append([gather_last(0, "last0")])
+        quantise_piece(w1_last[0], 0, KP - 1, "last1", False)
+        v_words[KP - 1].append(gather_last(1, "last1"))
+        quantise_piece(w1_last[1], 1, KP - 1, "stage02", True)
 
         h = {}
 
         def first_product(g):
             for e in range(2):
                 j = 2 * g + e
-                cols = slice(P * e, P * (e + 1))
                 banks = [psum.tile([P, BANK], F32, name="acc", tag="bank%d" % (2 * (j % 4) + s)) for s in range(2)]
                 for a in range(KP):
                     for s in range(2):
                         picked = slice(BANK * s, BANK * (s + 1))
                         nc.tensor.matmul_mx(
                             out=banks[s][:],
-                            lhsT=w1_codes[g, a][:, cols].bitcast(FP8X4),
-                            lhsT_scale=w1_planes[g, a][:, cols],
-                            rhs=v_words[a][:, picked].bitcast(FP8X4),
+                            lhsT=w1_codes[j, a][0].bitcast(FP8X4),
+                            lhsT_scale=w1_codes[j, a][1],
+                            rhs=v_words[a][s].bitcast(FP8X4),
                             rhs_scale=v_plane[4 * a : P, picked],
                             start=(a == 0),
                             stop=(a == KP - 1),
@@ -156,7 +178,8 @@ def tile_list_recipe_citation_cross_kernel(
                     nc.scalar.copy(rows[:, BANK * s : BANK * (s + 1)], banks[s][:])
                 h[j] = rows
 
-        th = ring.tile([P, TILES, M], F32, name="th", tag="big", bufs=3, align_bytes=64)
+        th_free = ring.tile([P, TILES, M], F32, name="th_free", tag="big", bufs=3, align_bytes=64)
+        th = {}
         z_moved, z_codes, z_planes = [], [], []
 
         def bound(g):
@@ -165,11 +188,13 @@ def tile_list_recipe_citation_cross_kernel(
                 z_moved.append(ring.tile([P, 4 * M], BF16, name="z_moved", tag="z_moved%d" % b, align_bytes=64))
             for j in (2 * g, 2 * g + 1):
                 i = j % 4
-                h1 = ring.tile([P, M], F32, name="h1", tag="h1_%d" % j, align_bytes=64)
+                tag = "raw%d%d" % (g + 1, 1 + j % 2) if g + 1 < GROUPS else "h1_%d" % j
+                h1 = ring.tile([P, M], F32, name="h1", tag=tag, align_bytes=64)
                 nc.vector.tensor_copy(h1[:], h[j][:].indirect(pos1_sb[:]))
-                nc.scalar.activation(th[:, j, :], h1[:], ACT.Tanh, bias=column(0, j))
+                th[j] = th_free[:, j, :]
+                nc.scalar.activation(th[j], h1[:], ACT.Tanh, bias=column(0, j))
                 z_rows = keep.tile([P, M], BF16, name="z_rows_%d" % j, align_bytes=64)
-                nc.scalar.activation(z_rows[:], th[:, j, :], ACT.Copy, scale=column(1, j))
+                nc.scalar.activation(z_rows[:], th[j], ACT.Copy, scale=column(1, j))
                 nc.sync.dma_start(z_moved[b][32 * i : 32 * (i + 1), :], z_rows[:])
             if g % 2 == 1:
                 z_il = ring.tile([P, 4 * M], BF16, name="z_il", tag="z_il", bufs=2, align_bytes=64)
@@ -185,18 +210,18 @@ def tile_list_recipe_citation_cross_kernel(
                 z_codes.append(codes)
                 z_planes.append(plane)
 
-        for g in range(2):
-            quantise_w1(g)
-            first_product(g)
+        first_product(0)
+        quantise_w1(1)
+        first_product(1)
         for g in range(2, GROUPS):
             quantise_w1(g)
         for g in range(GROUPS):
+            if 2 <= g + 1 < GROUPS:
+                first_product(g + 1)
             bound(g)
-            if g + 2 < GROUPS:
-                first_product(g + 2)
 
         h2 = []
-        for tag, count in (("h1_5", 1), ("h1_6", 1), ("h1_7", 2), ("z_moved1", 1)):
+        for tag, count in (("raw32", 1), ("h1_6", 1), ("h1_7", 2), ("z_moved1", 1)):
             picked = ring.tile([P, count, M], F32, name="h2", tag=tag, align_bytes=64)
             for e in range(count):
                 nc.vector.tensor_copy(picked[:, e, :], h[len(h2)][:].indirect(pos2_sb[:]))
@@ -219,9 +244,9 @@ def tile_list_recipe_citation_cross_kernel(
             ys.append(y)
 
         for j in range(TILES):
-            nc.vector.scalar_tensor_tensor(th[:, j, :], ys[j][:], column(2, j), th[:, j, :], ALU.add, ALU.mult)
+            nc.vector.scalar_tensor_tensor(th[j], ys[j][:], column(2, j), th[j], ALU.add, ALU.mult)
         for j in range(ON_GPSIMD):
-            nc.gpsimd.tensor_tensor(h2[j], th[:, j, :], h2[j], ALU.add)
+            nc.gpsimd.tensor_tensor(h2[j], th[j], h2[j], ALU.add)
             nc.sync.dma_start(out[P * j : P * (j + 1), :], h2[j])
         for j in range(ON_GPSIMD, PLAIN):
             first = 2 * (j - ON_GPSIMD)
@@ -229,7 +254,7 @@ def tile_list_recipe_citation_cross_kernel(
             for m0 in range(0, M, P):
                 cols = slice(m0, m0 + P)
                 nc.tensor.matmul(summed[:, cols], h2[j][:, cols], ident[:], start=True, stop=False, is_transpose=True)
-                nc.tensor.matmul(summed[:, cols], th[:, j, cols], ident[:], start=False, stop=True, is_transpose=True)
+                nc.tensor.matmul(summed[:, cols], th[j][:, cols], ident[:], start=False, stop=True, is_transpose=True)
             turned_sum = keep.tile([P, M], F32, name="turned_sum_%d" % j, align_bytes=64)
             nc.scalar.copy(turned_sum[:], summed[:])
             back = psum.tile([P, M], F32, name="back", tag="bank%d" % (first + 1))
@@ -244,5 +269,5 @@ def tile_list_recipe_citation_cross_kernel(
             for m0 in range(0, M, width):
                 cols = slice(m0, m0 + width)
                 picks = pos2_sb[:, m0 // 16 : (m0 + width) // 16]
-                nc.vector.tensor_tensor(result[:, j - PLAIN, cols], h[j][:].indirect(picks), th[:, j, cols], ALU.add)
+                nc.vector.tensor_tensor(result[:, j - PLAIN, cols], h[j][:].indirect(picks), th[j][:, cols], ALU.add)
                 nc.sync.dma_start(out[P * j : P * (j + 1), cols], result[:, j - PLAIN, cols])

@@ -35,6 +35,7 @@ def tile_list_recipe_citation_cross_kernel(
     with ExitStack() as ctx:
         keep = ctx.enter_context(tc.tile_pool(name="keep", bufs=1))
         ring = ctx.enter_context(tc.tile_pool(name="ring", bufs=1))
+        laid = ctx.enter_context(tc.tile_pool(name="laid", bufs=1))
         psum = ctx.enter_context(tc.psum_pool(name="psum", bufs=1))
 
         offs_sb = keep.tile([P, S // 16], U16, name="offs_sb")
@@ -60,12 +61,24 @@ def tile_list_recipe_citation_cross_kernel(
             table.append(tile)
 
         def load_w1(g, a):
-            tile = ring.tile([P, 4, GROUP], F32, name="w1_raw", tag="raw%d%d" % (g, a), align_bytes=64)
+            if (g, a) == (1, KP - 1):
+                tile = laid.tile([P, 4, GROUP], F32, name="w1_raw_laid", align_bytes=64, offset=0)
+            else:
+                tile = ring.tile([P, 4, GROUP], F32, name="w1_raw", tag="raw%d%d" % (g, a), align_bytes=64)
             nc.sync.dma_start(
                 tile[:],
                 w1[512 * a : 512 * (a + 1), GROUP * g : GROUP * (g + 1)].rearrange("(p j) c -> p j c", j=4),
             )
             w1_raw[g, a] = tile
+
+        w1_last = {}
+
+        def load_last_pass(g):
+            for j in (2 * g, 2 * g + 1):
+                w1_last[j] = keep.tile([P, 4, P], F32, name="w1_last_%d" % j)
+                nc.sync.dma_start(
+                    w1_last[j][:], w1[512 * (KP - 1) :, P * j : P * (j + 1)].rearrange("(p j) c -> p j c", j=4)
+                )
 
         nc.sync.dma_start(offs_sb[:], offs)
         load_table(0)
@@ -81,19 +94,16 @@ def tile_list_recipe_citation_cross_kernel(
         nc.sync.dma_start(pos1_sb[:], pos1)
         load_table(1)
         load_table(2)
-        w1_last = []
-        for e in range(2):
-            w1_last.append(keep.tile([P, 4, P], F32, name="w1_last_%d" % e))
-            nc.sync.dma_start(
-                w1_last[e][:], w1[512 * (KP - 1) :, P * e : P * (e + 1)].rearrange("(p j) c -> p j c", j=4)
-            )
+        load_last_pass(0)
         load_w1(1, 0)
         nc.sync.dma_start(pos2_sb[:], pos2)
         load_w1(1, 1)
         load_w1(1, 2)
-        for g in range(2, GROUPS):
-            for a in range(KP):
-                load_w1(g, a)
+        for a in range(KP):
+            load_w1(2, a)
+        for a in range(KP - 1):
+            load_w1(3, a)
+        load_last_pass(3)
         nc.sync.dma_start(
             w4_sb[:].bitcast(I32).rearrange("p (a c) -> p a c", a=HP),
             w4_words.bitcast(I32).rearrange("a p c -> p a c"),
@@ -139,8 +149,11 @@ def tile_list_recipe_citation_cross_kernel(
                 w1_codes[first + e, a] = (codes[:, P * e : P * (e + 1)], plane[:, P * e : P * (e + 1)])
 
         def quantise_w1(g):
-            for a in range(KP):
-                quantise_piece(w1_raw[g, a], 2 * g, a, "stage%d%d" % (g % 2, a), a > 0)
+            for a in range(KP - 1 if g == GROUPS - 1 else KP):
+                quantise_piece(w1_raw[g, a], 2 * g, a, "stage%d%d" % (g % 2, a), a != (KP - 1 if g == 1 else 0))
+            if g == GROUPS - 1:
+                for j in (2 * g, 2 * g + 1):
+                    quantise_piece(w1_last[j], j, KP - 1, "stage_last%d" % j, True)
 
         def gather_last(s, tag):
             tile = ring.tile([P, BANK], U32, name="v_last", tag=tag, align_bytes=64)
@@ -178,8 +191,8 @@ def tile_list_recipe_citation_cross_kernel(
                     nc.scalar.copy(rows[:, BANK * s : BANK * (s + 1)], banks[s][:])
                 h[j] = rows
 
-        th_free = ring.tile([P, TILES, M], F32, name="th_free", tag="big", bufs=3, align_bytes=64)
-        th = {}
+        th_rest = ring.tile([P, TILES, M], F32, name="th_rest", tag="big", bufs=3, align_bytes=64)
+        th = []
         z_moved, z_codes, z_planes = [], [], []
 
         def bound(g):
@@ -188,19 +201,30 @@ def tile_list_recipe_citation_cross_kernel(
                 z_moved.append(ring.tile([P, 4 * M], BF16, name="z_moved", tag="z_moved%d" % b, align_bytes=64))
             for j in (2 * g, 2 * g + 1):
                 i = j % 4
-                tag = "raw%d%d" % (g + 1, 1 + j % 2) if g + 1 < GROUPS else "h1_%d" % j
-                h1 = ring.tile([P, M], F32, name="h1", tag=tag, align_bytes=64)
-                nc.vector.tensor_copy(h1[:], h[j][:].indirect(pos1_sb[:]))
-                th[j] = th_free[:, j, :]
-                nc.scalar.activation(th[j], h1[:], ACT.Tanh, bias=column(0, j))
+                tag = "raw%d%d" % (g + 1, 1 + j % 2) if j < 5 else "h1_%d" % j
+                if j == 1:
+                    h1 = laid.tile([P, M], F32, name="h1_laid", align_bytes=64, offset=2048)
+                else:
+                    h1 = ring.tile([P, M], F32, name="h1", tag=tag, align_bytes=64)
+                if j == 0:
+                    th.append(laid.tile([P, M], F32, name="th_laid", align_bytes=64, offset=0)[:])
+                else:
+                    th.append(th_rest[:, j, :])
                 z_rows = keep.tile([P, M], BF16, name="z_rows_%d" % j, align_bytes=64)
-                nc.scalar.activation(z_rows[:], th[j], ACT.Copy, scale=column(1, j))
-                nc.sync.dma_start(z_moved[b][32 * i : 32 * (i + 1), :], z_rows[:])
+                moved = z_moved[b][32 * i : 32 * (i + 1), :].rearrange("q (t m) -> q t m", t=4)
+                width = M // 2 if j == TILES - 1 else M
+                for m0 in range(0, M, width):
+                    cols = slice(m0, m0 + width)
+                    picks = pos1_sb[:, m0 // 16 : (m0 + width) // 16]
+                    nc.vector.tensor_copy(h1[:, cols], h[j][:].indirect(picks))
+                    nc.scalar.activation(th[j][:, cols], h1[:, cols], ACT.Tanh, bias=column(0, j))
+                    nc.scalar.activation(z_rows[:, cols], th[j][:, cols], ACT.Copy, scale=column(1, j))
+                    nc.sync.dma_start(moved[:, :, cols], z_rows[:, cols])
             if g % 2 == 1:
                 z_il = ring.tile([P, 4 * M], BF16, name="z_il", tag="z_il", bufs=2, align_bytes=64)
                 dst = z_il[:].rearrange("p (c i t) -> p c t i", i=4, t=4)
                 src = z_moved[b][:].rearrange("p (t c i) -> p c t i", i=4, t=4)
-                shared = 40 if b == HP - 1 else 0
+                shared = 72 if b == HP - 1 else 0
                 if shared:
                     nc.scalar.copy(dst[:, 0:shared], src[:, 0:shared])
                 nc.vector.tensor_copy(dst[:, shared:], src[:, shared:])
@@ -221,7 +245,7 @@ def tile_list_recipe_citation_cross_kernel(
             bound(g)
 
         h2 = []
-        for tag, count in (("raw32", 1), ("h1_6", 1), ("h1_7", 2), ("z_moved1", 1)):
+        for tag, count in (("h1_5", 1), ("h1_6", 1), ("h1_7", 2), ("z_moved1", 1)):
             picked = ring.tile([P, count, M], F32, name="h2", tag=tag, align_bytes=64)
             for e in range(count):
                 nc.vector.tensor_copy(picked[:, e, :], h[len(h2)][:].indirect(pos2_sb[:]))

@@ -224,13 +224,20 @@ def tile_list_recipe_citation_cross_kernel(
                 z_il = ring.tile([P, 4 * M], BF16, name="z_il", tag="z_il", bufs=2, align_bytes=64)
                 dst = z_il[:].rearrange("p (c i t) -> p c t i", i=4, t=4)
                 src = z_moved[b][:].rearrange("p (t c i) -> p c t i", i=4, t=4)
-                shared = 72 if b == HP - 1 else 0
-                if shared:
-                    nc.scalar.copy(dst[:, 0:shared], src[:, 0:shared])
-                nc.vector.tensor_copy(dst[:, shared:], src[:, shared:])
                 codes = keep.tile([P, M], U32, name="z_codes_%d" % b, align_bytes=64)
                 plane = keep.tile([P, M], U8, name="z_plane_%d" % b, align_bytes=64)
-                nc.vector.quantize_mx(out=codes[:].bitcast(FP8X4), scales=plane[:], in_=z_il[:])
+                width = M // 2 if b == HP - 1 else M
+                shared = 36 if b == HP - 1 else 0
+                for m0 in range(0, M, width):
+                    c0, c1 = m0 // 4, (m0 + width) // 4
+                    if shared:
+                        nc.scalar.copy(dst[:, c0 : c0 + shared], src[:, c0 : c0 + shared])
+                    nc.vector.tensor_copy(dst[:, c0 + shared : c1], src[:, c0 + shared : c1])
+                    nc.vector.quantize_mx(
+                        out=codes[:, m0 : m0 + width].bitcast(FP8X4),
+                        scales=plane[:, m0 : m0 + width],
+                        in_=z_il[:, 4 * m0 : 4 * (m0 + width)],
+                    )
                 z_codes.append(codes)
                 z_planes.append(plane)
 
@@ -245,7 +252,7 @@ def tile_list_recipe_citation_cross_kernel(
             bound(g)
 
         h2 = []
-        for tag, count in (("h1_5", 1), ("h1_6", 1), ("h1_7", 2), ("z_moved1", 1)):
+        for tag, count in (("stage_last6", 1), ("h1_5", 1), ("h1_6", 1), ("h1_7", 1), ("z_moved1", 1)):
             picked = ring.tile([P, count, M], F32, name="h2", tag=tag, align_bytes=64)
             for e in range(count):
                 nc.vector.tensor_copy(picked[:, e, :], h[len(h2)][:].indirect(pos2_sb[:]))

@@ -80,8 +80,8 @@ def tile_list_recipe_citation_cross_kernel(
                     w1_last[j][:], w1[512 * (KP - 1) :, P * j : P * (j + 1)].rearrange("(p j) c -> p j c", j=4)
                 )
 
-        nc.sync.dma_start(offs_sb[:], offs)
         load_table(0)
+        nc.sync.dma_start(offs_sb[:], offs)
         for q in range(4):
             (nc.sync if q == 3 else nc.gpsimd).dma_start(
                 tab_plane[32 * q : 32 * q + 4 * KP, :].bitcast(I32),
@@ -89,9 +89,9 @@ def tile_list_recipe_citation_cross_kernel(
             )
         load_w1(0, 0)
         load_w1(0, 1)
+        nc.sync.dma_start(pos1_sb[:], pos1)
         for i, vec in enumerate((b1, gain, b2)):
             nc.sync.dma_start(vec_rows[TILES * i : TILES * (i + 1), :], vec.rearrange("(j p) -> j p", p=P))
-        nc.sync.dma_start(pos1_sb[:], pos1)
         load_table(1)
         load_table(2)
         load_last_pass(0)
@@ -99,11 +99,9 @@ def tile_list_recipe_citation_cross_kernel(
         nc.sync.dma_start(pos2_sb[:], pos2)
         load_w1(1, 1)
         load_w1(1, 2)
-        for a in range(KP):
-            load_w1(2, a)
-        for a in range(KP - 1):
-            load_w1(3, a)
-        load_last_pass(3)
+        for g in range(2, GROUPS):
+            for a in range(KP):
+                load_w1(g, a)
         nc.sync.dma_start(
             w4_sb[:].bitcast(I32).rearrange("p (a c) -> p a c", a=HP),
             w4_words.bitcast(I32).rearrange("a p c -> p a c"),
@@ -149,11 +147,8 @@ def tile_list_recipe_citation_cross_kernel(
                 w1_codes[first + e, a] = (codes[:, P * e : P * (e + 1)], plane[:, P * e : P * (e + 1)])
 
         def quantise_w1(g):
-            for a in range(KP - 1 if g == GROUPS - 1 else KP):
+            for a in range(KP):
                 quantise_piece(w1_raw[g, a], 2 * g, a, "stage%d%d" % (g % 2, a), a != (KP - 1 if g == 1 else 0))
-            if g == GROUPS - 1:
-                for j in (2 * g, 2 * g + 1):
-                    quantise_piece(w1_last[j], j, KP - 1, "stage_last%d" % j, True)
 
         def gather_last(s, tag):
             tile = ring.tile([P, BANK], U32, name="v_last", tag=tag, align_bytes=64)
@@ -201,7 +196,7 @@ def tile_list_recipe_citation_cross_kernel(
                 z_moved.append(ring.tile([P, 4 * M], BF16, name="z_moved", tag="z_moved%d" % b, align_bytes=64))
             for j in (2 * g, 2 * g + 1):
                 i = j % 4
-                tag = "raw%d%d" % (g + 1, 1 + j % 2) if j < 5 else "h1_%d" % j
+                tag = "raw%d%d" % (g + 1, 1 + j % 2) if j < 6 else "h1_%d" % j
                 if j == 1:
                     h1 = laid.tile([P, M], F32, name="h1_laid", align_bytes=64, offset=2048)
                 else:
@@ -252,7 +247,7 @@ def tile_list_recipe_citation_cross_kernel(
             bound(g)
 
         h2 = []
-        for tag, count in (("stage_last6", 1), ("h1_5", 1), ("h1_6", 1), ("h1_7", 1), ("z_moved1", 1)):
+        for tag, count in (("stage12", 1), ("raw32", 1), ("h1_6", 1), ("h1_7", 1), ("z_moved1", 1)):
             picked = ring.tile([P, count, M], F32, name="h2", tag=tag, align_bytes=64)
             for e in range(count):
                 nc.vector.tensor_copy(picked[:, e, :], h[len(h2)][:].indirect(pos2_sb[:]))
@@ -296,9 +291,7 @@ def tile_list_recipe_citation_cross_kernel(
             nc.scalar.dma_start(out[P * j : P * (j + 1), :], h2[j])
         result = ring.tile([P, TILES - PLAIN, M], F32, name="result", tag="big", bufs=3, align_bytes=64)
         for j in range(PLAIN, TILES):
-            width = M // 2 if j == TILES - 1 else M
-            for m0 in range(0, M, width):
-                cols = slice(m0, m0 + width)
-                picks = pos2_sb[:, m0 // 16 : (m0 + width) // 16]
+            for cols in (slice(0, M - P), slice(M - P, M)) if j == TILES - 1 else (slice(0, M),):
+                picks = pos2_sb[:, cols.start // 16 : cols.stop // 16]
                 nc.vector.tensor_tensor(result[:, j - PLAIN, cols], h[j][:].indirect(picks), th[j][:, cols], ALU.add)
                 nc.sync.dma_start(out[P * j : P * (j + 1), cols], result[:, j - PLAIN, cols])

@@ -61,8 +61,8 @@ def tile_list_recipe_citation_cross_kernel(
             table.append(tile)
 
         def load_w1(g, a):
-            if (g, a) == (1, KP - 1):
-                tile = laid.tile([P, 4, GROUP], F32, name="w1_raw_laid", align_bytes=64, offset=0)
+            if (g, a) in ((1, KP - 1), (2, 0)):
+                tile = laid.tile([P, 4, GROUP], F32, name="w1_raw_laid_%d" % g, align_bytes=64, offset=4096 * (g - 1))
             else:
                 tile = ring.tile([P, 4, GROUP], F32, name="w1_raw", tag="raw%d%d" % (g, a), align_bytes=64)
             nc.sync.dma_start(
@@ -190,64 +190,79 @@ def tile_list_recipe_citation_cross_kernel(
         th = []
         z_moved, z_codes, z_planes = [], [], []
 
-        def bound(g):
+        def bound(tiles):
+            g = tiles[0] // 2
             b = g // 2
-            if g % 2 == 0:
+            if tiles[0] % 4 == 0:
                 z_moved.append(ring.tile([P, 4 * M], BF16, name="z_moved", tag="z_moved%d" % b, align_bytes=64))
-            for j in (2 * g, 2 * g + 1):
-                i = j % 4
+            for j in tiles:
                 tag = "raw%d%d" % (g + 1, 1 + j % 2) if j < 6 else "h1_%d" % j
                 if j == 1:
-                    h1 = laid.tile([P, M], F32, name="h1_laid", align_bytes=64, offset=2048)
+                    h1 = laid.tile([P, M], F32, name="h1_laid", align_bytes=64, offset=0)
                 else:
                     h1 = ring.tile([P, M], F32, name="h1", tag=tag, align_bytes=64)
                 if j == 0:
-                    th.append(laid.tile([P, M], F32, name="th_laid", align_bytes=64, offset=0)[:])
+                    th.append(laid.tile([P, M], F32, name="th_laid", align_bytes=64, offset=3072)[:])
+                elif j in (4,):
+                    th_pair = ring.tile([P, 2 * M], F32, name="th_pair", tag="codes%d2" % (j + 2), align_bytes=64)
+                    th.append(th_pair[:, 0:M])
+                elif j - 1 in (4,):
+                    th.append(th_pair[:, M:])
                 else:
                     th.append(th_rest[:, j, :])
+                width = M // 2 if j == TILES - 1 else M
+                for m0 in range(0, M, width):
+                    cols = slice(m0, m0 + width)
+                    picks = pos1_sb[:, m0 // 16 : (m0 + width) // 16]
+                    if m0:
+                        h1 = keep.tile([P, width], F32, name="h1_last", align_bytes=64)
+                    nc.vector.tensor_copy(h1[:, 0:width], h[j][:].indirect(picks))
+                    nc.scalar.activation(th[j][:, cols], h1[:, 0:width], ACT.Tanh, bias=column(0, j))
+            for j in tiles:
+                i = j % 4
                 z_rows = keep.tile([P, M], BF16, name="z_rows_%d" % j, align_bytes=64)
                 moved = z_moved[b][32 * i : 32 * (i + 1), :].rearrange("q (t m) -> q t m", t=4)
                 width = M // 2 if j == TILES - 1 else M
                 for m0 in range(0, M, width):
                     cols = slice(m0, m0 + width)
-                    picks = pos1_sb[:, m0 // 16 : (m0 + width) // 16]
-                    nc.vector.tensor_copy(h1[:, cols], h[j][:].indirect(picks))
-                    nc.scalar.activation(th[j][:, cols], h1[:, cols], ACT.Tanh, bias=column(0, j))
                     nc.scalar.activation(z_rows[:, cols], th[j][:, cols], ACT.Copy, scale=column(1, j))
                     nc.sync.dma_start(moved[:, :, cols], z_rows[:, cols])
-            if g % 2 == 1:
-                z_il = ring.tile([P, 4 * M], BF16, name="z_il", tag="z_il", bufs=2, align_bytes=64)
-                dst = z_il[:].rearrange("p (c i t) -> p c t i", i=4, t=4)
-                src = z_moved[b][:].rearrange("p (t c i) -> p c t i", i=4, t=4)
-                codes = keep.tile([P, M], U32, name="z_codes_%d" % b, align_bytes=64)
-                plane = keep.tile([P, M], U8, name="z_plane_%d" % b, align_bytes=64)
-                width = M // 2 if b == HP - 1 else M
-                shared = 36 if b == HP - 1 else 0
-                for m0 in range(0, M, width):
-                    c0, c1 = m0 // 4, (m0 + width) // 4
-                    if shared:
-                        nc.scalar.copy(dst[:, c0 : c0 + shared], src[:, c0 : c0 + shared])
-                    nc.vector.tensor_copy(dst[:, c0 + shared : c1], src[:, c0 + shared : c1])
-                    nc.vector.quantize_mx(
-                        out=codes[:, m0 : m0 + width].bitcast(FP8X4),
-                        scales=plane[:, m0 : m0 + width],
-                        in_=z_il[:, 4 * m0 : 4 * (m0 + width)],
-                    )
-                z_codes.append(codes)
-                z_planes.append(plane)
+
+        def quantise_z(b, tag, width, shared):
+            z_il = ring.tile([P, 4 * M], BF16, name="z_il", tag=tag, align_bytes=64)
+            dst = z_il[:].rearrange("p (c i t) -> p c t i", i=4, t=4)
+            src = z_moved[b][:].rearrange("p (t c i) -> p c t i", i=4, t=4)
+            codes = keep.tile([P, M], U32, name="z_codes_%d" % b, align_bytes=64)
+            plane = keep.tile([P, M], U8, name="z_plane_%d" % b, align_bytes=64)
+            for m0 in range(0, M, width):
+                c0, c1 = m0 // 4, (m0 + width) // 4
+                if shared:
+                    nc.scalar.copy(dst[:, c0 : c0 + shared], src[:, c0 : c0 + shared])
+                nc.vector.tensor_copy(dst[:, c0 + shared : c1], src[:, c0 + shared : c1])
+                nc.vector.quantize_mx(
+                    out=codes[:, m0 : m0 + width].bitcast(FP8X4),
+                    scales=plane[:, m0 : m0 + width],
+                    in_=z_il[:, 4 * m0 : 4 * (m0 + width)],
+                )
+            z_codes.append(codes)
+            z_planes.append(plane)
 
         first_product(0)
         quantise_w1(1)
+        quantise_w1(2)
+        bound((0,))
         first_product(1)
-        for g in range(2, GROUPS):
-            quantise_w1(g)
-        for g in range(GROUPS):
-            if 2 <= g + 1 < GROUPS:
+        quantise_w1(3)
+        bound((1,))
+        for g in range(1, GROUPS):
+            if g + 1 < GROUPS:
                 first_product(g + 1)
-            bound(g)
+            bound((2 * g, 2 * g + 1))
+        quantise_z(0, "raw32", M, 0)
+        quantise_z(1, "z_il", M // 2, 36)
 
         h2 = []
-        for tag, count in (("stage12", 1), ("raw32", 1), ("h1_6", 1), ("h1_7", 1), ("z_moved1", 1)):
+        for tag, count in (("stage12", 2), ("raw32", 2), ("z_moved1", 1)):
             picked = ring.tile([P, count, M], F32, name="h2", tag=tag, align_bytes=64)
             for e in range(count):
                 nc.vector.tensor_copy(picked[:, e, :], h[len(h2)][:].indirect(pos2_sb[:]))

@@ -99,9 +99,11 @@ def tile_list_recipe_citation_cross_kernel(
         nc.sync.dma_start(pos2_sb[:], pos2)
         load_w1(1, 1)
         load_w1(1, 2)
-        for g in range(2, GROUPS):
-            for a in range(KP):
-                load_w1(g, a)
+        for a in range(KP):
+            load_w1(2, a)
+        for a in range(KP - 1):
+            load_w1(3, a)
+        load_last_pass(3)
         nc.sync.dma_start(
             w4_sb[:].bitcast(I32).rearrange("p (a c) -> p a c", a=HP),
             w4_words.bitcast(I32).rearrange("a p c -> p a c"),
@@ -147,8 +149,11 @@ def tile_list_recipe_citation_cross_kernel(
                 w1_codes[first + e, a] = (codes[:, P * e : P * (e + 1)], plane[:, P * e : P * (e + 1)])
 
         def quantise_w1(g):
-            for a in range(KP):
+            for a in range(KP - 1 if g == GROUPS - 1 else KP):
                 quantise_piece(w1_raw[g, a], 2 * g, a, "stage%d%d" % (g % 2, a), a != (KP - 1 if g == 1 else 0))
+            if g == GROUPS - 1:
+                for j in (2 * g, 2 * g + 1):
+                    quantise_piece(w1_last[j], j, KP - 1, "stage_last%d" % j, True)
 
         def gather_last(s, tag):
             tile = ring.tile([P, BANK], U32, name="v_last", tag=tag, align_bytes=64)
@@ -196,7 +201,7 @@ def tile_list_recipe_citation_cross_kernel(
             if tiles[0] % 4 == 0:
                 z_moved.append(ring.tile([P, 4 * M], BF16, name="z_moved", tag="z_moved%d" % b, align_bytes=64))
             for j in tiles:
-                tag = "raw%d%d" % (g + 1, 1 + j % 2) if j < 6 else "h1_%d" % j
+                tag = "raw%d%d" % (g + 1, 1 + j % 2) if j < 5 else "h1_%d" % j
                 if j == 1:
                     h1 = laid.tile([P, M], F32, name="h1_laid", align_bytes=64, offset=0)
                 else:
@@ -204,7 +209,7 @@ def tile_list_recipe_citation_cross_kernel(
                 if j == 0:
                     th.append(laid.tile([P, M], F32, name="th_laid", align_bytes=64, offset=3072)[:])
                 elif j in (4,):
-                    th_pair = ring.tile([P, 2 * M], F32, name="th_pair", tag="codes%d2" % (j + 2), align_bytes=64)
+                    th_pair = ring.tile([P, 2 * M], F32, name="th_pair", tag="codes72", align_bytes=64)
                     th.append(th_pair[:, 0:M])
                 elif j - 1 in (4,):
                     th.append(th_pair[:, M:])
@@ -258,11 +263,11 @@ def tile_list_recipe_citation_cross_kernel(
             if g + 1 < GROUPS:
                 first_product(g + 1)
             bound((2 * g, 2 * g + 1))
-        quantise_z(0, "raw32", M, 0)
+        quantise_z(0, "h1_5", M, 0)
         quantise_z(1, "z_il", M // 2, 36)
 
         h2 = []
-        for tag, count in (("stage12", 2), ("raw32", 2), ("z_moved1", 1)):
+        for tag, count in (("stage_last7", 2), ("h1_5", 2), ("z_moved1", 1)):
             picked = ring.tile([P, count, M], F32, name="h2", tag=tag, align_bytes=64)
             for e in range(count):
                 nc.vector.tensor_copy(picked[:, e, :], h[len(h2)][:].indirect(pos2_sb[:]))

@@ -233,13 +233,14 @@ def tile_list_recipe_citation_cross_kernel(
                     nc.scalar.activation(z_rows[:, cols], th[j][:, cols], ACT.Copy, scale=column(1, j))
                     nc.sync.dma_start(moved[:, :, cols], z_rows[:, cols])
 
-        def quantise_z(b, tag, width, shared):
+        def quantise_z(b, tag, shares):
             z_il = ring.tile([P, 4 * M], BF16, name="z_il", tag=tag, align_bytes=64)
             dst = z_il[:].rearrange("p (c i t) -> p c t i", i=4, t=4)
             src = z_moved[b][:].rearrange("p (t c i) -> p c t i", i=4, t=4)
             codes = keep.tile([P, M], U32, name="z_codes_%d" % b, align_bytes=64)
             plane = keep.tile([P, M], U8, name="z_plane_%d" % b, align_bytes=64)
-            for m0 in range(0, M, width):
+            width = M // len(shares)
+            for m0, shared in zip(range(0, M, width), shares):
                 c0, c1 = m0 // 4, (m0 + width) // 4
                 if shared:
                     nc.scalar.copy(dst[:, c0 : c0 + shared], src[:, c0 : c0 + shared])
@@ -263,8 +264,8 @@ def tile_list_recipe_citation_cross_kernel(
             if g + 1 < GROUPS:
                 first_product(g + 1)
             bound((2 * g, 2 * g + 1))
-        quantise_z(0, "h1_5", M, 0)
-        quantise_z(1, "z_il", M // 2, 36)
+        quantise_z(0, "h1_5", (0,))
+        quantise_z(1, "z_il", (36, 20))
 
         h2 = []
         for tag, count in (("stage_last7", 2), ("h1_5", 2), ("z_moved1", 1)):

@@ -26,17 +26,81 @@ GROUP = 256
 GROUPS = H // GROUP
 PLAIN = 5
 ON_GPSIMD = 3
+IN_PSUM = 2
+LAP = 64
+KB = 1024
+DIGIT = {str(n): n for n in range(TILES)}
+
+
+def lay_out():
+    place = {}
+    end = 0
+
+    def chain(start, *items):
+        for name, size in items:
+            place[name] = start
+            start = start + size - LAP
+        return start + LAP
+
+    for a in range(KP):
+        place["table%d" % a] = 16 * KB * a
+    for j in range(4, TILES):
+        place["h%d" % j] = 4 * KB * (j - 4)
+    for i, name in enumerate(("z_moved0", "z_moved1", "z_il1")):
+        place[name] = 16 * KB + 4 * KB * i
+    place["z_codes0"], place["z_codes1"] = 28 * KB, 30 * KB
+    place["z_il0"], place["h1_7b"] = 32 * KB, 32 * KB
+    place["result"], place["turned"] = 36 * KB, 40 * KB
+    place["h1_6"], place["h2_4"], place["th7"] = 44 * KB, 44 * KB, 46 * KB
+    end = chain(48 * KB, ("stage_10", 2 * KB), ("stage_t1", KB), ("stage_11", 2 * KB), ("h2_0", 2 * KB), ("raw_12", 4 * KB))
+    place["raw_11"] = place["codes_10"] = end
+    end = chain(
+        end + 3 * KB // 2,
+        ("h2_1", 2 * KB),
+        ("stage_12", 2 * KB),
+        ("stage_21", 2 * KB),
+        ("h1_2", 2 * KB),
+        ("raw_22", 4 * KB),
+    )
+    place["z0"] = place["stage_12"] + 2 * LAP
+    place["raw_21"] = place["codes_20"] = end
+    end = chain(end + 3 * KB // 2, ("h1_3", 2 * KB), ("stage_22", 2 * KB), ("stage_31", 2 * KB))
+    place["z1"] = place["stage_22"] + 2 * LAP
+    chain(end, ("z2", 2 * KB), ("stage_t7", KB), ("h1_5", 2 * KB))
+    place["raw_31"] = place["stage_t7"]
+    place["codes_30"] = place["raw_31"] + 3 * KB // 2
+    end = chain(place["raw_31"] + 3 * KB, ("stage_t6", KB), ("h1_4", 2 * KB), ("raw_t7", 2 * KB))
+    place["z7"] = place["z2"]
+    place["h2_2"], place["h2_3"] = place["h1_4"], place["h1_5"]
+    for size, names in (
+        (2 * KB, ("th0", "plane_t1")),
+        (2 * KB, ("h1_0", "stage_20")),
+        (2 * KB, ("codes_12", "stage_30")),
+        (4 * KB, ("codes_22", "th2")),
+        (6 * KB, ("codes_t7", "th4")),
+        (2 * KB, ("h1_7a", "h2_5")),
+    ):
+        for name in names:
+            place[name] = end
+        end = end + size
+    return place
 
 
 def tile_list_recipe_citation_cross_kernel(
     tc, tab_words, tab_scales, offs, pos1, pos2, w1, b1, gain, w4_words, w4_scales, b2, out
 ):
     nc = tc.nc
+    place = lay_out()
     with ExitStack() as ctx:
         keep = ctx.enter_context(tc.tile_pool(name="keep", bufs=1))
         ring = ctx.enter_context(tc.tile_pool(name="ring", bufs=1))
         laid = ctx.enter_context(tc.tile_pool(name="laid", bufs=1))
         psum = ctx.enter_context(tc.psum_pool(name="psum", bufs=1))
+
+        def new(name, shape, dtype):
+            if name in place:
+                return laid.tile(shape, dtype, name=name, align_bytes=64, offset=place[name])
+            return keep.tile(shape, dtype, name=name, align_bytes=64)
 
         offs_sb = keep.tile([P, S // 16], U16, name="offs_sb")
         pos1_sb = keep.tile([P, M // 16], U16, name="pos1_sb")
@@ -53,32 +117,22 @@ def tile_list_recipe_citation_cross_kernel(
         nc.vector.memset(w4_plane[:].bitcast(I32), 0)
 
         table = []
-        w1_raw = {}
 
         def load_table(a):
-            tile = ring.tile([P, T], U32, name="table", tag="big", bufs=3, align_bytes=64)
+            tile = new("table%d" % a, [P, T], U32)
             nc.sync.dma_start(tile[:].bitcast(I32), tab_words[a].rearrange("p t i -> p (t i)").bitcast(I32))
             table.append(tile)
 
-        def load_w1(g, a):
-            if (g, a) in ((1, KP - 1), (2, 0)):
-                tile = laid.tile([P, 4, GROUP], F32, name="w1_raw_laid_%d" % g, align_bytes=64, offset=4096 * (g - 1))
-            else:
-                tile = ring.tile([P, 4, GROUP], F32, name="w1_raw", tag="raw%d%d" % (g, a), align_bytes=64)
+        def load_w1(dst, a, first, count):
             nc.sync.dma_start(
-                tile[:],
-                w1[512 * a : 512 * (a + 1), GROUP * g : GROUP * (g + 1)].rearrange("(p j) c -> p j c", j=4),
+                dst, w1[512 * a : 512 * (a + 1), P * first : P * (first + count)].rearrange("(p j) c -> p j c", j=4)
             )
-            w1_raw[g, a] = tile
 
-        w1_last = {}
+        raw = {}
 
-        def load_last_pass(g):
-            for j in (2 * g, 2 * g + 1):
-                w1_last[j] = keep.tile([P, 4, P], F32, name="w1_last_%d" % j)
-                nc.sync.dma_start(
-                    w1_last[j][:], w1[512 * (KP - 1) :, P * j : P * (j + 1)].rearrange("(p j) c -> p j c", j=4)
-                )
+        def load_piece(name, a, first, count):
+            raw[name] = new("raw_" + name, [P, 4, P * count], F32)
+            load_w1(raw[name][:], a, first, count)
 
         load_table(0)
         nc.sync.dma_start(offs_sb[:], offs)
@@ -87,23 +141,25 @@ def tile_list_recipe_citation_cross_kernel(
                 tab_plane[32 * q : 32 * q + 4 * KP, :].bitcast(I32),
                 tab_scales[:, 4 * q : 4 * q + 4, :].bitcast(I32),
             )
-        load_w1(0, 0)
-        load_w1(0, 1)
+        load_piece("first0", 0, 0, 2)
+        load_piece("first1", 1, 0, 2)
         nc.sync.dma_start(pos1_sb[:], pos1)
         for i, vec in enumerate((b1, gain, b2)):
             nc.sync.dma_start(vec_rows[TILES * i : TILES * (i + 1), :], vec.rearrange("(j p) -> j p", p=P))
         load_table(1)
         load_table(2)
-        load_last_pass(0)
-        load_w1(1, 0)
+        load_piece("t0", 2, 0, 1)
+        load_piece("t1", 2, 1, 1)
+        load_piece("10", 0, 2, 2)
         nc.sync.dma_start(pos2_sb[:], pos2)
-        load_w1(1, 1)
-        load_w1(1, 2)
+        load_piece("11", 1, 2, 2)
+        load_piece("12", 2, 2, 2)
         for a in range(KP):
-            load_w1(2, a)
+            load_piece("2%d" % a, a, 4, 2)
         for a in range(KP - 1):
-            load_w1(3, a)
-        load_last_pass(3)
+            load_piece("3%d" % a, a, 6, 2)
+        load_piece("t6", 2, 6, 1)
+        load_piece("t7", 2, 7, 1)
         nc.sync.dma_start(
             w4_sb[:].bitcast(I32).rearrange("p (a c) -> p a c", a=HP),
             w4_words.bitcast(I32).rearrange("a p c -> p a c"),
@@ -133,27 +189,35 @@ def tile_list_recipe_citation_cross_kernel(
 
         w1_codes = {}
 
-        def quantise_piece(raw, first, a, tag, on_vector):
-            width = raw.shape[2]
-            grouped = ring.tile([P, 4 * width], BF16, name="w1_bf", tag=tag, align_bytes=64)
-            dst = grouped[:].rearrange("p (c i j) -> p c j i", i=4, j=4)
-            src = raw[:].rearrange("p j (c i) -> p c j i", i=4)
-            if on_vector:
-                nc.vector.tensor_copy(dst, src)
-            else:
-                nc.scalar.copy(dst, src)
-            codes = ring.tile([P, width], U32, name="w1_codes", tag="codes%d%d" % (first, a), align_bytes=64)
-            plane = keep.tile([P, width], U8, name="w1_plane_%d_%d" % (first, a), align_bytes=64)
-            nc.vector.quantize_mx(out=codes[:].bitcast(FP8X4), scales=plane[:], in_=grouped[:])
-            for e in range(width // P):
-                w1_codes[first + e, a] = (codes[:, P * e : P * (e + 1)], plane[:, P * e : P * (e + 1)])
+        def round_on_scalar(grouped, rows):
+            nc.scalar.copy(
+                grouped.rearrange("p (c i j) -> p c j i", i=4, j=4), rows.rearrange("p j (c i) -> p c j i", i=4)
+            )
 
-        def quantise_w1(g):
-            for a in range(KP - 1 if g == GROUPS - 1 else KP):
-                quantise_piece(w1_raw[g, a], 2 * g, a, "stage%d%d" % (g % 2, a), a != (KP - 1 if g == 1 else 0))
-            if g == GROUPS - 1:
-                for j in (2 * g, 2 * g + 1):
-                    quantise_piece(w1_last[j], j, KP - 1, "stage_last%d" % j, True)
+        def round_on_vector(grouped, rows):
+            nc.vector.tensor_copy(
+                grouped.rearrange("p (c i j) -> p c j i", i=4, j=4), rows.rearrange("p j (c i) -> p c j i", i=4)
+            )
+
+        def round_on_gpsimd(grouped, rows):
+            nc.gpsimd.tensor_scalar(
+                grouped.rearrange("p (c i j) -> p c j i", i=2, j=4),
+                rows.rearrange("p j (c i) -> p c j i", i=2),
+                1.0,
+                0.0,
+                ALU.mult,
+                ALU.add,
+            )
+
+        def quantise(name, grouped, first, count, passes):
+            width = P * count * len(passes)
+            codes = new("codes_" + name, [P, width], U32)
+            plane = new("plane_" + name, [P, width], U8)
+            nc.vector.quantize_mx(out=codes[:].bitcast(FP8X4), scales=plane[:], in_=grouped[:])
+            for n, a in enumerate(passes):
+                for e in range(count):
+                    cols = slice(P * (count * n + e), P * (count * n + e + 1))
+                    w1_codes[first + e, a] = (codes[:, cols], plane[:, cols])
 
         def gather_last(s, tag):
             tile = ring.tile([P, BANK], U32, name="v_last", tag=tag, align_bytes=64)
@@ -162,89 +226,164 @@ def tile_list_recipe_citation_cross_kernel(
             return tile[:]
 
         for a in range(KP - 1):
-            quantise_piece(w1_raw[0, a], 0, a, "stage0%d" % a, False)
+            grouped = new("stage_first%d" % a, [P, 4 * GROUP], BF16)
+            round_on_scalar(grouped[:], raw["first%d" % a][:])
+            quantise("first%d" % a, grouped, 0, 2, (a,))
         v_words.append([gather_last(0, "last0")])
-        quantise_piece(w1_last[0], 0, KP - 1, "last1", False)
+        grouped = ring.tile([P, 4 * P], BF16, name="stage_t0", tag="last1", align_bytes=64)
+        round_on_scalar(grouped[:], raw["t0"][:])
+        quantise("t0", grouped, 0, 1, (2,))
         v_words[KP - 1].append(gather_last(1, "last1"))
-        quantise_piece(w1_last[1], 1, KP - 1, "stage02", True)
+        grouped = new("stage_t1", [P, 4 * P], BF16)
+        round_on_gpsimd(grouped[:], raw["t1"][:])
+        quantise("t1", grouped, 1, 1, (2,))
 
-        h = {}
+        h, banks, h1, th, h2, z_rows, staged = {}, {}, {}, {}, {}, {}, {}
+        z_moved = [new("z_moved%d" % b, [P, 4 * M], BF16) for b in range(HP)]
 
-        def first_product(g):
-            for e in range(2):
-                j = 2 * g + e
-                banks = [psum.tile([P, BANK], F32, name="acc", tag="bank%d" % (2 * (j % 4) + s)) for s in range(2)]
-                for a in range(KP):
-                    for s in range(2):
-                        picked = slice(BANK * s, BANK * (s + 1))
-                        nc.tensor.matmul_mx(
-                            out=banks[s][:],
-                            lhsT=w1_codes[j, a][0].bitcast(FP8X4),
-                            lhsT_scale=w1_codes[j, a][1],
-                            rhs=v_words[a][s].bitcast(FP8X4),
-                            rhs_scale=v_plane[4 * a : P, picked],
-                            start=(a == 0),
-                            stop=(a == KP - 1),
-                        )
-                rows = keep.tile([P, S], F32, name="h_%d" % j, align_bytes=64)
+        def multiply(j):
+            banks[j] = [psum.tile([P, BANK], F32, name="acc", tag="bank%d" % (2 * (j % 4) + s)) for s in range(2)]
+            for a in range(KP):
                 for s in range(2):
-                    nc.scalar.copy(rows[:, BANK * s : BANK * (s + 1)], banks[s][:])
-                h[j] = rows
+                    nc.tensor.matmul_mx(
+                        out=banks[j][s][:],
+                        lhsT=w1_codes[j, a][0].bitcast(FP8X4),
+                        lhsT_scale=w1_codes[j, a][1],
+                        rhs=v_words[a][s].bitcast(FP8X4),
+                        rhs_scale=v_plane[4 * a : P, BANK * s : BANK * (s + 1)],
+                        start=(a == 0),
+                        stop=(a == KP - 1),
+                    )
 
-        th_rest = ring.tile([P, TILES, M], F32, name="th_rest", tag="big", bufs=3, align_bytes=64)
-        th = []
-        z_moved, z_codes, z_planes = [], [], []
+        def empty(j):
+            h[j] = new("h%d" % j, [P, S], F32)
+            for s in range(2):
+                nc.scalar.copy(h[j][:, BANK * s : BANK * (s + 1)], banks[j][s][:])
 
-        def bound(tiles):
-            g = tiles[0] // 2
-            b = g // 2
-            if tiles[0] % 4 == 0:
-                z_moved.append(ring.tile([P, 4 * M], BF16, name="z_moved", tag="z_moved%d" % b, align_bytes=64))
-            for j in tiles:
-                tag = "raw%d%d" % (g + 1, 1 + j % 2) if j < 5 else "h1_%d" % j
-                if j == 1:
-                    h1 = laid.tile([P, M], F32, name="h1_laid", align_bytes=64, offset=0)
-                else:
-                    h1 = ring.tile([P, M], F32, name="h1", tag=tag, align_bytes=64)
-                if j == 0:
-                    th.append(laid.tile([P, M], F32, name="th_laid", align_bytes=64, offset=3072)[:])
-                elif j in (4,):
-                    th_pair = ring.tile([P, 2 * M], F32, name="th_pair", tag="codes72", align_bytes=64)
-                    th.append(th_pair[:, 0:M])
-                elif j - 1 in (4,):
-                    th.append(th_pair[:, M:])
-                else:
-                    th.append(th_rest[:, j, :])
-                width = M // 2 if j == TILES - 1 else M
-                for m0 in range(0, M, width):
-                    cols = slice(m0, m0 + width)
-                    picks = pos1_sb[:, m0 // 16 : (m0 + width) // 16]
-                    if m0:
-                        h1 = keep.tile([P, width], F32, name="h1_last", align_bytes=64)
-                    nc.vector.tensor_copy(h1[:, 0:width], h[j][:].indirect(picks))
-                    nc.scalar.activation(th[j][:, cols], h1[:, 0:width], ACT.Tanh, bias=column(0, j))
-            for j in tiles:
-                i = j % 4
-                z_rows = keep.tile([P, M], BF16, name="z_rows_%d" % j, align_bytes=64)
-                moved = z_moved[b][32 * i : 32 * (i + 1), :].rearrange("q (t m) -> q t m", t=4)
-                width = M // 2 if j == TILES - 1 else M
-                for m0 in range(0, M, width):
-                    cols = slice(m0, m0 + width)
-                    nc.scalar.activation(z_rows[:, cols], th[j][:, cols], ACT.Copy, scale=column(1, j))
-                    nc.sync.dma_start(moved[:, :, cols], z_rows[:, cols])
+        def round_piece(name, rounder):
+            staged[name] = new("stage_" + name, [P, 4 * raw[name].shape[2]], BF16)
+            rounder(staged[name][:], raw[name][:])
 
-        def quantise_z(b, tag, shares):
-            z_il = ring.tile([P, 4 * M], BF16, name="z_il", tag=tag, align_bytes=64)
-            dst = z_il[:].rearrange("p (c i t) -> p c t i", i=4, t=4)
-            src = z_moved[b][:].rearrange("p (t c i) -> p c t i", i=4, t=4)
-            codes = keep.tile([P, M], U32, name="z_codes_%d" % b, align_bytes=64)
-            plane = keep.tile([P, M], U8, name="z_plane_%d" % b, align_bytes=64)
+        def quantise_piece(name):
+            if name[0] == "t":
+                quantise(name, staged[name], DIGIT[name[1]], 1, (KP - 1,))
+            else:
+                quantise(name, staged[name], 2 * DIGIT[name[0]], 2, (DIGIT[name[1]],))
+
+        def gather1(j, name=None, cols=slice(0, M)):
+            name = name or "h1_%d" % j
+            h1[name] = new(name, [P, cols.stop - cols.start], F32)
+            nc.vector.tensor_copy(h1[name][:], h[j][:].indirect(pos1_sb[:, cols.start // 16 : cols.stop // 16]))
+
+        def gather2(j):
+            h2[j] = new("h2_%d" % j, [P, M], F32)
+            nc.vector.tensor_copy(h2[j][:], h[j][:].indirect(pos2_sb[:]))
+
+        def bound(j, name=None, cols=slice(0, M)):
+            if j not in th:
+                count = {2: 2, 4: 3}.get(j, 1)
+                tile = new("th%d" % j, [P, count * M], F32)
+                for e in range(count):
+                    th[j + e] = tile[:, M * e : M * (e + 1)]
+            nc.scalar.activation(th[j][:, cols], h1[name or "h1_%d" % j][:], ACT.Tanh, bias=column(0, j))
+
+        def scale(j, on_gpsimd, cols=slice(0, M)):
+            if j not in z_rows:
+                count = 2 if j == 2 else 1
+                tile = new("z%d" % j, [P, count * M], BF16)
+                for e in range(count):
+                    z_rows[j + e] = tile[:, M * e : M * (e + 1)]
+            if on_gpsimd:
+                nc.gpsimd.tensor_scalar(z_rows[j][:, cols], th[j][:, cols], column(1, j), 0.0, ALU.mult, ALU.add)
+            else:
+                nc.scalar.activation(z_rows[j][:, cols], th[j][:, cols], ACT.Copy, scale=column(1, j))
+            moved = z_moved[j // 4][32 * (j % 4) : 32 * (j % 4 + 1), :].rearrange("q (t m) -> q t m", t=4)
+            nc.sync.dma_start(moved[:, :, cols], z_rows[j][:, cols])
+
+        multiply(0)
+        multiply(1)
+        round_piece("10", round_on_gpsimd)
+        round_piece("11", round_on_gpsimd)
+        empty(0)
+        gather1(0)
+        empty(1)
+        bound(0)
+        gather1(1)
+        bound(1)
+        round_piece("20", round_on_scalar)
+        quantise_piece("10")
+        round_piece("12", round_on_vector)
+        quantise_piece("11")
+        quantise_piece("12")
+        multiply(2)
+        multiply(3)
+        scale(0, True)
+        round_piece("21", round_on_gpsimd)
+        gather2(0)
+        gather2(1)
+        empty(2)
+        empty(3)
+        round_piece("30", round_on_scalar)
+        quantise_piece("20")
+        round_piece("22", round_on_vector)
+        quantise_piece("21")
+        quantise_piece("22")
+        multiply(4)
+        multiply(5)
+        scale(1, True)
+        round_piece("31", round_on_gpsimd)
+        gather1(2)
+        gather1(3)
+        empty(4)
+        empty(5)
+        bound(2)
+        bound(3)
+        quantise_piece("30")
+        round_piece("t6", round_on_vector)
+        round_piece("t7", round_on_vector)
+        quantise_piece("31")
+        quantise_piece("t6")
+        quantise_piece("t7")
+        multiply(6)
+        multiply(7)
+        scale(2, True)
+        scale(3, True)
+        gather1(4)
+        gather1(5)
+        empty(6)
+        gather1(6)
+        empty(7)
+        halves = (("h1_7a", slice(0, M // 2)), ("h1_7b", slice(M // 2, M)))
+        for name, cols in halves:
+            gather1(7, name, cols)
+        for j in range(4, 7):
+            bound(j)
+            scale(j, True)
+        for name, cols in halves:
+            bound(7, name, cols)
+        for name, cols in halves:
+            scale(7, False, cols)
+        for j in range(2, PLAIN):
+            gather2(j)
+
+        z_codes, z_planes = [], []
+
+        def quantise_z(b, shares):
+            z_il = new("z_il%d" % b, [P, 4 * M], BF16)
+            codes = new("z_codes%d" % b, [P, M], U32)
+            plane = new("z_plane%d" % b, [P, M], U8)
             width = M // len(shares)
             for m0, shared in zip(range(0, M, width), shares):
+                dst = z_il[:].rearrange("p (c i t) -> p c t i", i=4, t=4)
+                src = z_moved[b][:].rearrange("p (t c i) -> p c t i", i=4, t=4)
                 c0, c1 = m0 // 4, (m0 + width) // 4
-                if shared:
-                    nc.scalar.copy(dst[:, c0 : c0 + shared], src[:, c0 : c0 + shared])
-                nc.vector.tensor_copy(dst[:, c0 + shared : c1], src[:, c0 + shared : c1])
+                nc.scalar.copy(dst[:, c0 : c0 + shared], src[:, c0 : c0 + shared])
+                if b == 0:
+                    dst = z_il[:].rearrange("p (m t) -> p m t", t=4)[:, 4 * (c0 + shared) : 4 * c1]
+                    src = z_moved[b][:].rearrange("p (t m) -> p m t", t=4)[:, 4 * (c0 + shared) : 4 * c1]
+                    nc.gpsimd.tensor_scalar(dst, src, 1.0, 0.0, ALU.mult, ALU.add)
+                else:
+                    nc.vector.tensor_copy(dst[:, c0 + shared : c1], src[:, c0 + shared : c1])
                 nc.vector.quantize_mx(
                     out=codes[:, m0 : m0 + width].bitcast(FP8X4),
                     scales=plane[:, m0 : m0 + width],
@@ -253,26 +392,8 @@ def tile_list_recipe_citation_cross_kernel(
             z_codes.append(codes)
             z_planes.append(plane)
 
-        first_product(0)
-        quantise_w1(1)
-        quantise_w1(2)
-        bound((0,))
-        first_product(1)
-        quantise_w1(3)
-        bound((1,))
-        for g in range(1, GROUPS):
-            if g + 1 < GROUPS:
-                first_product(g + 1)
-            bound((2 * g, 2 * g + 1))
-        quantise_z(0, "h1_5", (0,))
-        quantise_z(1, "z_il", (36, 20))
-
-        h2 = []
-        for tag, count in (("stage_last7", 2), ("h1_5", 2), ("z_moved1", 1)):
-            picked = ring.tile([P, count, M], F32, name="h2", tag=tag, align_bytes=64)
-            for e in range(count):
-                nc.vector.tensor_copy(picked[:, e, :], h[len(h2)][:].indirect(pos2_sb[:]))
-                h2.append(picked[:, e, :])
+        quantise_z(0, (64,))
+        quantise_z(1, (36, 20))
 
         ys = []
         for j in range(TILES):
@@ -293,24 +414,27 @@ def tile_list_recipe_citation_cross_kernel(
         for j in range(TILES):
             nc.vector.scalar_tensor_tensor(th[j], ys[j][:], column(2, j), th[j], ALU.add, ALU.mult)
         for j in range(ON_GPSIMD):
-            nc.gpsimd.tensor_tensor(h2[j], th[j], h2[j], ALU.add)
-            nc.sync.dma_start(out[P * j : P * (j + 1), :], h2[j])
-        for j in range(ON_GPSIMD, PLAIN):
-            first = 2 * (j - ON_GPSIMD)
-            summed = psum.tile([P, M], F32, name="summed", tag="bank%d" % first)
+            nc.gpsimd.tensor_tensor(h2[j][:], th[j], h2[j][:], ALU.add)
+            nc.sync.dma_start(out[P * j : P * (j + 1), :], h2[j][:])
+        turned_sums = new("turned", [P, IN_PSUM, M], F32)
+        for j in range(ON_GPSIMD, ON_GPSIMD + IN_PSUM):
+            e = j - ON_GPSIMD
+            summed = psum.tile([P, M], F32, name="summed", tag="bank%d" % (2 * e))
             for m0 in range(0, M, P):
                 cols = slice(m0, m0 + P)
                 nc.tensor.matmul(summed[:, cols], h2[j][:, cols], ident[:], start=True, stop=False, is_transpose=True)
                 nc.tensor.matmul(summed[:, cols], th[j][:, cols], ident[:], start=False, stop=True, is_transpose=True)
-            turned_sum = keep.tile([P, M], F32, name="turned_sum_%d" % j, align_bytes=64)
-            nc.scalar.copy(turned_sum[:], summed[:])
-            back = psum.tile([P, M], F32, name="back", tag="bank%d" % (first + 1))
+            nc.scalar.copy(turned_sums[:, e, :], summed[:])
+            back = psum.tile([P, M], F32, name="back", tag="bank%d" % (2 * e + 1))
             for m0 in range(0, M, P):
                 cols = slice(m0, m0 + P)
-                nc.tensor.transpose(back[:, cols], turned_sum[:, cols], ident[:])
-            nc.scalar.copy(h2[j], back[:])
-            nc.scalar.dma_start(out[P * j : P * (j + 1), :], h2[j])
-        result = ring.tile([P, TILES - PLAIN, M], F32, name="result", tag="big", bufs=3, align_bytes=64)
+                nc.tensor.transpose(back[:, cols], turned_sums[:, e, cols], ident[:])
+            nc.scalar.copy(h2[j][:], back[:])
+            nc.scalar.dma_start(out[P * j : P * (j + 1), :], h2[j][:])
+        for j in range(ON_GPSIMD + IN_PSUM, PLAIN):
+            nc.vector.tensor_tensor(h2[j][:], th[j], h2[j][:], ALU.add)
+            nc.sync.dma_start(out[P * j : P * (j + 1), :], h2[j][:])
+        result = new("result", [P, TILES - PLAIN, M], F32)
         for j in range(PLAIN, TILES):
             for cols in (slice(0, M - P), slice(M - P, M)) if j == TILES - 1 else (slice(0, M),):
                 picks = pos2_sb[:, cols.start // 16 : cols.stop // 16]

@@ -25,7 +25,6 @@ TILES = H // P
 GROUP = 256
 GROUPS = H // GROUP
 PLAIN = 5
-ON_GPSIMD = 3
 IN_PSUM = 2
 LAP = 64
 KB = 1024
@@ -50,8 +49,8 @@ def lay_out():
         place[name] = 16 * KB + 4 * KB * i
     place["z_codes0"], place["z_codes1"] = 28 * KB, 30 * KB
     place["z_il0"], place["h1_7b"] = 32 * KB, 32 * KB
-    place["result"], place["turned"] = 36 * KB, 40 * KB
-    place["h1_6"], place["h2_4"], place["th7"] = 44 * KB, 44 * KB, 46 * KB
+    place["result"] = 36 * KB
+    place["h1_6"], place["h2_4"], place["th7"] = 44 * KB, place["z_moved1"], 46 * KB
     end = chain(48 * KB, ("stage_10", 2 * KB), ("stage_t1", KB), ("stage_11", 2 * KB), ("h2_0", 2 * KB), ("raw_12", 4 * KB))
     place["raw_11"] = place["codes_10"] = end
     end = chain(
@@ -62,10 +61,8 @@ def lay_out():
         ("h1_2", 2 * KB),
         ("raw_22", 4 * KB),
     )
-    place["z0"] = place["stage_12"] + 2 * LAP
     place["raw_21"] = place["codes_20"] = end
     end = chain(end + 3 * KB // 2, ("h1_3", 2 * KB), ("stage_22", 2 * KB), ("stage_31", 2 * KB))
-    place["z1"] = place["stage_22"] + 2 * LAP
     chain(end, ("z2", 2 * KB), ("stage_t7", KB), ("h1_5", 2 * KB))
     place["raw_31"] = place["stage_t7"]
     place["codes_30"] = place["raw_31"] + 3 * KB // 2
@@ -74,7 +71,7 @@ def lay_out():
     place["h2_2"], place["h2_3"] = place["h1_4"], place["h1_5"]
     for size, names in (
         (2 * KB, ("th0", "plane_t1")),
-        (2 * KB, ("h1_0", "stage_20")),
+        (2 * KB, ("h1_1", "stage_20")),
         (2 * KB, ("codes_12", "stage_30")),
         (4 * KB, ("codes_22", "th2")),
         (6 * KB, ("codes_t7", "th4")),
@@ -201,8 +198,8 @@ def tile_list_recipe_citation_cross_kernel(
 
         def round_on_gpsimd(grouped, rows):
             nc.gpsimd.tensor_scalar(
-                grouped.rearrange("p (c i j) -> p c j i", i=2, j=4),
-                rows.rearrange("p j (c i) -> p c j i", i=2),
+                grouped.rearrange("p (c j) -> p c j", j=4),
+                rows.rearrange("p j c -> p c j"),
                 1.0,
                 0.0,
                 ALU.mult,
@@ -235,7 +232,7 @@ def tile_list_recipe_citation_cross_kernel(
         quantise("t0", grouped, 0, 1, (2,))
         v_words[KP - 1].append(gather_last(1, "last1"))
         grouped = new("stage_t1", [P, 4 * P], BF16)
-        round_on_gpsimd(grouped[:], raw["t1"][:])
+        round_on_scalar(grouped[:], raw["t1"][:])
         quantise("t1", grouped, 1, 1, (2,))
 
         h, banks, h1, th, h2, z_rows, staged = {}, {}, {}, {}, {}, {}, {}
@@ -243,8 +240,8 @@ def tile_list_recipe_citation_cross_kernel(
 
         def multiply(j):
             banks[j] = [psum.tile([P, BANK], F32, name="acc", tag="bank%d" % (2 * (j % 4) + s)) for s in range(2)]
-            for a in range(KP):
-                for s in range(2):
+            for s, a in [(s, a) for s in range(2) for a in range(KP)]:
+                if True:
                     nc.tensor.matmul_mx(
                         out=banks[j][s][:],
                         lhsT=w1_codes[j, a][0].bitcast(FP8X4),
@@ -308,8 +305,10 @@ def tile_list_recipe_citation_cross_kernel(
         gather1(0)
         empty(1)
         bound(0)
+        scale(0, False)
         gather1(1)
         bound(1)
+        scale(1, False)
         round_piece("20", round_on_scalar)
         quantise_piece("10")
         round_piece("12", round_on_vector)
@@ -317,7 +316,6 @@ def tile_list_recipe_citation_cross_kernel(
         quantise_piece("12")
         multiply(2)
         multiply(3)
-        scale(0, True)
         round_piece("21", round_on_gpsimd)
         gather2(0)
         gather2(1)
@@ -330,7 +328,6 @@ def tile_list_recipe_citation_cross_kernel(
         quantise_piece("22")
         multiply(4)
         multiply(5)
-        scale(1, True)
         round_piece("31", round_on_gpsimd)
         gather1(2)
         gather1(3)
@@ -363,7 +360,7 @@ def tile_list_recipe_citation_cross_kernel(
             bound(7, name, cols)
         for name, cols in halves:
             scale(7, False, cols)
-        for j in range(2, PLAIN):
+        for j in range(2, PLAIN - 1):
             gather2(j)
 
         z_codes, z_planes = [], []
@@ -392,13 +389,15 @@ def tile_list_recipe_citation_cross_kernel(
             z_codes.append(codes)
             z_planes.append(plane)
 
-        quantise_z(0, (64,))
+        quantise_z(0, (76,))
         quantise_z(1, (36, 20))
+        gather2(PLAIN - 1)
 
         ys = []
         for j in range(TILES):
             y = psum.tile([P, M], F32, name="y", tag="bank%d" % j)
-            for a in range(HP):
+            order = range(HP) if j < TILES - 2 else range(HP - 1, -1, -1)
+            for a in order:
                 n0 = H * a + P * j
                 nc.tensor.matmul_mx(
                     out=y[:],
@@ -406,19 +405,19 @@ def tile_list_recipe_citation_cross_kernel(
                     lhsT_scale=w4_plane[:, n0 : n0 + P],
                     rhs=z_codes[a][:].bitcast(FP8X4),
                     rhs_scale=z_planes[a][:],
-                    start=(a == 0),
-                    stop=(a == HP - 1),
+                    start=(a == order[0]),
+                    stop=(a == order[-1]),
                 )
             ys.append(y)
 
         for j in range(TILES):
             nc.vector.scalar_tensor_tensor(th[j], ys[j][:], column(2, j), th[j], ALU.add, ALU.mult)
-        for j in range(ON_GPSIMD):
+        for j in range(0, PLAIN, 2):
             nc.gpsimd.tensor_tensor(h2[j][:], th[j], h2[j][:], ALU.add)
             nc.sync.dma_start(out[P * j : P * (j + 1), :], h2[j][:])
         turned_sums = new("turned", [P, IN_PSUM, M], F32)
-        for j in range(ON_GPSIMD, ON_GPSIMD + IN_PSUM):
-            e = j - ON_GPSIMD
+        for j in range(1, PLAIN, 2):
+            e = j // 2
             summed = psum.tile([P, M], F32, name="summed", tag="bank%d" % (2 * e))
             for m0 in range(0, M, P):
                 cols = slice(m0, m0 + P)
@@ -431,9 +430,6 @@ def tile_list_recipe_citation_cross_kernel(
                 nc.tensor.transpose(back[:, cols], turned_sums[:, e, cols], ident[:])
             nc.scalar.copy(h2[j][:], back[:])
             nc.scalar.dma_start(out[P * j : P * (j + 1), :], h2[j][:])
-        for j in range(ON_GPSIMD + IN_PSUM, PLAIN):
-            nc.vector.tensor_tensor(h2[j][:], th[j], h2[j][:], ALU.add)
-            nc.sync.dma_start(out[P * j : P * (j + 1), :], h2[j][:])
         result = new("result", [P, TILES - PLAIN, M], F32)
         for j in range(PLAIN, TILES):
             for cols in (slice(0, M - P), slice(M - P, M)) if j == TILES - 1 else (slice(0, M),):

@@ -26,61 +26,25 @@ GROUP = 256
 GROUPS = H // GROUP
 PLAIN = 5
 IN_PSUM = 2
-LAP = 64
 KB = 1024
-DIGIT = {str(n): n for n in range(TILES)}
+SPLIT = 2560
 
 
 def lay_out():
-    place = {}
-    end = 0
-
-    def chain(start, *items):
-        for name, size in items:
-            place[name] = start
-            start = start + size - LAP
-        return start + LAP
-
-    for a in range(KP):
-        place["table%d" % a] = 16 * KB * a
-    for j in range(4, TILES):
-        place["h%d" % j] = 4 * KB * (j - 4)
-    for i, name in enumerate(("z_moved0", "z_moved1", "z_il1")):
-        place[name] = 16 * KB + 4 * KB * i
-    place["z_codes0"], place["z_codes1"] = 28 * KB, 30 * KB
-    place["z_il0"], place["h1_7b"] = 32 * KB, 32 * KB
-    place["result"] = 36 * KB
-    place["h1_6"], place["h2_4"], place["th7"] = 44 * KB, place["z_moved1"], 46 * KB
-    end = chain(48 * KB, ("stage_10", 2 * KB), ("stage_t1", KB), ("stage_11", 2 * KB), ("h2_0", 2 * KB), ("raw_12", 4 * KB))
-    place["raw_11"] = place["codes_10"] = end
-    end = chain(
-        end + 3 * KB // 2,
-        ("h2_1", 2 * KB),
-        ("stage_12", 2 * KB),
-        ("stage_21", 2 * KB),
-        ("h1_2", 2 * KB),
-        ("raw_22", 4 * KB),
-    )
-    place["raw_21"] = place["codes_20"] = end
-    end = chain(end + 3 * KB // 2, ("h1_3", 2 * KB), ("stage_22", 2 * KB), ("stage_31", 2 * KB))
-    chain(end, ("z2", 2 * KB), ("stage_t7", KB), ("h1_5", 2 * KB))
-    place["raw_31"] = place["stage_t7"]
-    place["codes_30"] = place["raw_31"] + 3 * KB // 2
-    end = chain(place["raw_31"] + 3 * KB, ("stage_t6", KB), ("h1_4", 2 * KB), ("raw_t7", 2 * KB))
-    place["z7"] = place["z2"]
-    place["h2_2"], place["h2_3"] = place["h1_4"], place["h1_5"]
-    for size, names in (
-        (2 * KB, ("th0", "plane_t1")),
-        (2 * KB, ("h1_1", "stage_20")),
-        (2 * KB, ("codes_12", "stage_30")),
-        (4 * KB, ("codes_22", "th2")),
-        (6 * KB, ("codes_t7", "th4")),
-        (2 * KB, ("h1_7a", "h2_5")),
-    ):
-        for name in names:
-            place[name] = end
-        end = end + size
-    return place
+    half_kb = {
+        "table0": 0, "table1": 32, "table2": 64,
+        "h4": 0, "h5": 8, "h6": 16, "h7": 24,
+        "z_moved0": 32, "z_moved1": 40, "h2_4": 40, "z_il1": 48, "z_codes0": 56, "z_codes1": 60,
+        "z_il0": 64, "h1_7b": 64, "result": 72, "h1_6": 88, "th7": 92,
+        "raw_02": 96, "v_last1": 96, "stage_02": 100, "stage_1ab": 100,
+        "raw_10": 104, "raw_12": 108, "codes_12": 104, "h1_0": 106, "stage_A2": 101, "stage_B1": 101,
+        "raw_A1": 210, "codes_A2": 210, "stage_C0": 208, "h2_0": 216, "raw_A2": 218, "th0": 224,
+        "raw_B1": 136, "raw_B2": 144, "codes_B0": 136, "stage_B2": 138, "stage_C1": 138, "h1_2": 144,
+        "raw_C1": 156, "th3": 153, "codes_C0": 157, "stage_62": 159, "stage_72": 161, "z0": 161,
+        "raw_72": 170, "h1_4": 170, "h2_2": 170, "codes_72": 178, "th4": 178,
+        "tab_plane": 190, "v_last0": 190, "codes_02": 198, "stage_A0": 198, "stage_A1": 198,
+    }
+    return {name: at * KB // 2 for name, at in half_kb.items()}
 
 
 def tile_list_recipe_citation_cross_kernel(
@@ -90,7 +54,6 @@ def tile_list_recipe_citation_cross_kernel(
     place = lay_out()
     with ExitStack() as ctx:
         keep = ctx.enter_context(tc.tile_pool(name="keep", bufs=1))
-        ring = ctx.enter_context(tc.tile_pool(name="ring", bufs=1))
         laid = ctx.enter_context(tc.tile_pool(name="laid", bufs=1))
         psum = ctx.enter_context(tc.psum_pool(name="psum", bufs=1))
 
@@ -105,7 +68,7 @@ def tile_list_recipe_citation_cross_kernel(
         vec_rows = keep.tile([P, P], F32, name="vec_rows")
         vec_cols = keep.tile([P, 3 * TILES], F32, name="vec_cols")
         ident = keep.tile([P, P], F32, name="ident")
-        tab_plane = ring.tile([P, T], U8, name="tab_plane", tag="words1", align_bytes=64)
+        tab_plane = new("tab_plane", [P, T], U8)
         w4_plane = keep.tile([P, HP * H], U8, name="w4_plane", align_bytes=64)
         w4_sb = keep.tile([P, HP * 2 * H], U8, name="w4_sb", align_bytes=64)
 
@@ -115,10 +78,11 @@ def tile_list_recipe_citation_cross_kernel(
 
         table = []
 
-        def load_table(a):
-            tile = new("table%d" % a, [P, T], U32)
-            nc.sync.dma_start(tile[:].bitcast(I32), tab_words[a].rearrange("p t i -> p (t i)").bitcast(I32))
-            table.append(tile)
+        def load_table(a, first=0, stop=T):
+            if first == 0:
+                table.append(new("table%d" % a, [P, T], U32))
+            words = tab_words[a].rearrange("p t i -> p (t i)").bitcast(I32)
+            nc.sync.dma_start(table[a][:, first:stop].bitcast(I32), words[:, first:stop])
 
         def load_w1(dst, a, first, count):
             nc.sync.dma_start(
@@ -138,25 +102,27 @@ def tile_list_recipe_citation_cross_kernel(
                 tab_plane[32 * q : 32 * q + 4 * KP, :].bitcast(I32),
                 tab_scales[:, 4 * q : 4 * q + 4, :].bitcast(I32),
             )
-        load_piece("first0", 0, 0, 2)
-        load_piece("first1", 1, 0, 2)
+        load_piece("00", 0, 0, 1)
+        load_table(1)
         nc.sync.dma_start(pos1_sb[:], pos1)
         for i, vec in enumerate((b1, gain, b2)):
             nc.sync.dma_start(vec_rows[TILES * i : TILES * (i + 1), :], vec.rearrange("(j p) -> j p", p=P))
-        load_table(1)
-        load_table(2)
-        load_piece("t0", 2, 0, 1)
-        load_piece("t1", 2, 1, 1)
-        load_piece("10", 0, 2, 2)
-        nc.sync.dma_start(pos2_sb[:], pos2)
-        load_piece("11", 1, 2, 2)
-        load_piece("12", 2, 2, 2)
+        load_table(2, 0, SPLIT)
+        load_piece("01", 1, 0, 1)
+        load_table(2, SPLIT, T)
+        load_piece("02", 2, 0, 1)
         for a in range(KP):
-            load_piece("2%d" % a, a, 4, 2)
+            load_piece("1%d" % a, a, 1, 1)
+        load_piece("A0", 0, 2, 2)
+        nc.sync.dma_start(pos2_sb[:], pos2)
+        load_piece("A1", 1, 2, 2)
+        load_piece("A2", 2, 2, 2)
+        for a in range(KP):
+            load_piece("B%d" % a, a, 4, 2)
         for a in range(KP - 1):
-            load_piece("3%d" % a, a, 6, 2)
-        load_piece("t6", 2, 6, 1)
-        load_piece("t7", 2, 7, 1)
+            load_piece("C%d" % a, a, 6, 2)
+        load_piece("62", 2, 6, 1)
+        load_piece("72", 2, 7, 1)
         nc.sync.dma_start(
             w4_sb[:].bitcast(I32).rearrange("p (a c) -> p a c", a=HP),
             w4_words.bitcast(I32).rearrange("a p c -> p a c"),
@@ -178,7 +144,7 @@ def tile_list_recipe_citation_cross_kernel(
         v_words = []
         v_plane = keep.tile([P, S], U8, name="v_plane", align_bytes=64)
         for a in range(KP - 1):
-            tile = ring.tile([P, S], U32, name="v_words", tag="words%d" % a, align_bytes=64)
+            tile = new("v_words%d" % a, [P, S], U32)
             nc.vector.tensor_copy(tile[:], table[a][:].indirect(offs_sb[:]))
             v_words.append([tile[:, BANK * s : BANK * (s + 1)] for s in range(2)])
             if a == 0:
@@ -216,80 +182,84 @@ def tile_list_recipe_citation_cross_kernel(
                     cols = slice(P * (count * n + e), P * (count * n + e + 1))
                     w1_codes[first + e, a] = (codes[:, cols], plane[:, cols])
 
-        def gather_last(s, tag):
-            tile = ring.tile([P, BANK], U32, name="v_last", tag=tag, align_bytes=64)
-            picks = offs_sb[:, BANK * s // 16 : BANK * (s + 1) // 16]
-            nc.vector.tensor_copy(tile[:], table[KP - 1][:].indirect(picks))
-            return tile[:]
+        def gather_last(dst, first, count):
+            nc.vector.tensor_copy(dst, table[KP - 1][:].indirect(offs_sb[:, first // 16 : (first + count) // 16]))
 
-        for a in range(KP - 1):
-            grouped = new("stage_first%d" % a, [P, 4 * GROUP], BF16)
-            round_on_scalar(grouped[:], raw["first%d" % a][:])
-            quantise("first%d" % a, grouped, 0, 2, (a,))
-        v_words.append([gather_last(0, "last0")])
-        grouped = ring.tile([P, 4 * P], BF16, name="stage_t0", tag="last1", align_bytes=64)
-        round_on_scalar(grouped[:], raw["t0"][:])
-        quantise("t0", grouped, 0, 1, (2,))
-        v_words[KP - 1].append(gather_last(1, "last1"))
-        grouped = new("stage_t1", [P, 4 * P], BF16)
-        round_on_scalar(grouped[:], raw["t1"][:])
-        quantise("t1", grouped, 1, 1, (2,))
+        staged = {}
 
-        h, banks, h1, th, h2, z_rows, staged = {}, {}, {}, {}, {}, {}, {}
+        def round_into(stage, *pieces):
+            width = sum(4 * raw[name].shape[2] for name, rounder in pieces)
+            staged[stage] = new("stage_" + stage, [P, width], BF16)
+            at = 0
+            for name, rounder in pieces:
+                cols = 4 * raw[name].shape[2]
+                rounder(staged[stage][:, at : at + cols], raw[name][:])
+                at = at + cols
+
+        def quantise_stage(stage, first, count, passes):
+            quantise(stage, staged[stage], first, count, passes)
+
+        h, banks, h1, th, h2, z_rows = {}, {}, {}, {}, {}, {}
         z_moved = [new("z_moved%d" % b, [P, 4 * M], BF16) for b in range(HP)]
+        bank_tags = []
+
+        def spans(j):
+            return ((0, 512), (512, 256), (768, 256)) if j == 0 else ((0, 512), (512, 512))
+
+        def open_banks(j):
+            banks[j] = []
+            for first, count in spans(j):
+                banks[j].append(psum.tile([P, count], F32, name="acc", tag="bank%d" % (len(bank_tags) % 8)))
+                bank_tags.append(j)
+
+        def product(j, s, a):
+            first, count = spans(j)[s]
+            nc.tensor.matmul_mx(
+                out=banks[j][s][:],
+                lhsT=w1_codes[j, a][0].bitcast(FP8X4),
+                lhsT_scale=w1_codes[j, a][1],
+                rhs=v_words[a][first // BANK][:, first % BANK : first % BANK + count].bitcast(FP8X4),
+                rhs_scale=v_plane[4 * a : P, first : first + count],
+                start=(a == 0),
+                stop=(a == KP - 1),
+            )
 
         def multiply(j):
-            banks[j] = [psum.tile([P, BANK], F32, name="acc", tag="bank%d" % (2 * (j % 4) + s)) for s in range(2)]
-            for s, a in [(s, a) for s in range(2) for a in range(KP)]:
-                if True:
-                    nc.tensor.matmul_mx(
-                        out=banks[j][s][:],
-                        lhsT=w1_codes[j, a][0].bitcast(FP8X4),
-                        lhsT_scale=w1_codes[j, a][1],
-                        rhs=v_words[a][s].bitcast(FP8X4),
-                        rhs_scale=v_plane[4 * a : P, BANK * s : BANK * (s + 1)],
-                        start=(a == 0),
-                        stop=(a == KP - 1),
-                    )
+            open_banks(j)
+            for s in range(len(spans(j))):
+                for a in range(KP):
+                    product(j, s, a)
 
         def empty(j):
             h[j] = new("h%d" % j, [P, S], F32)
-            for s in range(2):
-                nc.scalar.copy(h[j][:, BANK * s : BANK * (s + 1)], banks[j][s][:])
+            for s, (first, count) in enumerate(spans(j)):
+                nc.scalar.copy(h[j][:, first : first + count], banks[j][s][:])
 
-        def round_piece(name, rounder):
-            staged[name] = new("stage_" + name, [P, 4 * raw[name].shape[2]], BF16)
-            rounder(staged[name][:], raw[name][:])
-
-        def quantise_piece(name):
-            if name[0] == "t":
-                quantise(name, staged[name], DIGIT[name[1]], 1, (KP - 1,))
-            else:
-                quantise(name, staged[name], 2 * DIGIT[name[0]], 2, (DIGIT[name[1]],))
+        def shared(book, prefix, j, counts, dtype):
+            if j not in book:
+                count = counts.get(j, 1)
+                tile = new("%s%d" % (prefix, j), [P, count * M], dtype)
+                for e in range(count):
+                    book[j + e] = tile[:, M * e : M * (e + 1)]
+            return book[j]
 
         def gather1(j, name=None, cols=slice(0, M)):
-            name = name or "h1_%d" % j
-            h1[name] = new(name, [P, cols.stop - cols.start], F32)
-            nc.vector.tensor_copy(h1[name][:], h[j][:].indirect(pos1_sb[:, cols.start // 16 : cols.stop // 16]))
+            if name:
+                h1[name] = new(name, [P, cols.stop - cols.start], F32)[:]
+                dst = h1[name]
+            else:
+                dst = shared(h1, "h1_", j, {2: 2, 4: 2}, F32)
+            nc.vector.tensor_copy(dst, h[j][:].indirect(pos1_sb[:, cols.start // 16 : cols.stop // 16]))
 
         def gather2(j):
-            h2[j] = new("h2_%d" % j, [P, M], F32)
-            nc.vector.tensor_copy(h2[j][:], h[j][:].indirect(pos2_sb[:]))
+            nc.vector.tensor_copy(shared(h2, "h2_", j, {0: 2, 2: 2}, F32), h[j][:].indirect(pos2_sb[:]))
 
         def bound(j, name=None, cols=slice(0, M)):
-            if j not in th:
-                count = {2: 2, 4: 3}.get(j, 1)
-                tile = new("th%d" % j, [P, count * M], F32)
-                for e in range(count):
-                    th[j + e] = tile[:, M * e : M * (e + 1)]
-            nc.scalar.activation(th[j][:, cols], h1[name or "h1_%d" % j][:], ACT.Tanh, bias=column(0, j))
+            dst = shared(th, "th", j, {0: 2, 4: 3}, F32)
+            nc.scalar.activation(dst[:, cols], h1[name or j], ACT.Tanh, bias=column(0, j))
 
         def scale(j, on_gpsimd, cols=slice(0, M)):
-            if j not in z_rows:
-                count = 2 if j == 2 else 1
-                tile = new("z%d" % j, [P, count * M], BF16)
-                for e in range(count):
-                    z_rows[j + e] = tile[:, M * e : M * (e + 1)]
+            shared(z_rows, "z", j, {0: 4}, BF16)
             if on_gpsimd:
                 nc.gpsimd.tensor_scalar(z_rows[j][:, cols], th[j][:, cols], column(1, j), 0.0, ALU.mult, ALU.add)
             else:
@@ -297,54 +267,65 @@ def tile_list_recipe_citation_cross_kernel(
             moved = z_moved[j // 4][32 * (j % 4) : 32 * (j % 4 + 1), :].rearrange("q (t m) -> q t m", t=4)
             nc.sync.dma_start(moved[:, :, cols], z_rows[j][:, cols])
 
+        round_into("0ab", ("00", round_on_scalar), ("01", round_on_scalar))
+        quantise_stage("0ab", 0, 1, (0, 1))
+        last = [new("v_last%d" % s, [P, BANK], U32) for s in range(2)]
+        v_words.append([tile[:] for tile in last])
+        gather_last(last[0][:], 0, 512)
+        round_into("02", ("02", round_on_scalar))
+        quantise_stage("02", 0, 1, (2,))
+        gather_last(last[1][:, 0:256], 512, 256)
+        gather_last(last[1][:, 256:512], 768, 256)
         multiply(0)
-        multiply(1)
-        round_piece("10", round_on_gpsimd)
-        round_piece("11", round_on_gpsimd)
+        round_into("1ab", ("10", round_on_gpsimd), ("11", round_on_scalar))
         empty(0)
+        round_into("12", ("12", round_on_vector))
+        quantise_stage("1ab", 1, 1, (0, 1))
+        quantise_stage("12", 1, 1, (2,))
+        multiply(1)
+        round_into("A0", ("A0", round_on_scalar))
         gather1(0)
+        quantise_stage("A0", 2, 2, (0,))
+        round_into("A1", ("A1", round_on_gpsimd))
         empty(1)
-        bound(0)
-        scale(0, False)
+        round_into("A2", ("A2", round_on_scalar))
         gather1(1)
+        bound(0)
         bound(1)
-        scale(1, False)
-        round_piece("20", round_on_scalar)
-        quantise_piece("10")
-        round_piece("12", round_on_vector)
-        quantise_piece("11")
-        quantise_piece("12")
+        round_into("B0", ("B0", round_on_scalar))
+        quantise_stage("A1", 2, 2, (1,))
+        quantise_stage("A2", 2, 2, (2,))
         multiply(2)
         multiply(3)
-        round_piece("21", round_on_gpsimd)
+        round_into("B1", ("B1", round_on_gpsimd))
         gather2(0)
         gather2(1)
         empty(2)
         empty(3)
-        round_piece("30", round_on_scalar)
-        quantise_piece("20")
-        round_piece("22", round_on_vector)
-        quantise_piece("21")
-        quantise_piece("22")
+        round_into("C0", ("C0", round_on_scalar))
+        quantise_stage("B0", 4, 2, (0,))
+        round_into("B2", ("B2", round_on_vector))
+        quantise_stage("B1", 4, 2, (1,))
+        quantise_stage("B2", 4, 2, (2,))
         multiply(4)
         multiply(5)
-        round_piece("31", round_on_gpsimd)
+        round_into("C1", ("C1", round_on_gpsimd))
         gather1(2)
         gather1(3)
-        empty(4)
-        empty(5)
         bound(2)
+        empty(4)
         bound(3)
-        quantise_piece("30")
-        round_piece("t6", round_on_vector)
-        round_piece("t7", round_on_vector)
-        quantise_piece("31")
-        quantise_piece("t6")
-        quantise_piece("t7")
+        empty(5)
+        quantise_stage("C0", 6, 2, (0,))
+        round_into("62", ("62", round_on_vector))
+        round_into("72", ("72", round_on_vector))
+        quantise_stage("C1", 6, 2, (1,))
+        quantise_stage("62", 6, 1, (2,))
+        quantise_stage("72", 7, 1, (2,))
         multiply(6)
         multiply(7)
-        scale(2, True)
-        scale(3, True)
+        for j in range(4):
+            scale(j, True)
         gather1(4)
         gather1(5)
         empty(6)
@@ -395,7 +376,7 @@ def tile_list_recipe_citation_cross_kernel(
 
         ys = []
         for j in range(TILES):
-            y = psum.tile([P, M], F32, name="y", tag="bank%d" % j)
+            y = psum.tile([P, M], F32, name="y", tag="bank%d" % ((j + 1) % 8))
             order = range(HP) if j < TILES - 2 else range(HP - 1, -1, -1)
             for a in order:
                 n0 = H * a + P * j
@@ -413,23 +394,23 @@ def tile_list_recipe_citation_cross_kernel(
         for j in range(TILES):
             nc.vector.scalar_tensor_tensor(th[j], ys[j][:], column(2, j), th[j], ALU.add, ALU.mult)
         for j in range(0, PLAIN, 2):
-            nc.gpsimd.tensor_tensor(h2[j][:], th[j], h2[j][:], ALU.add)
-            nc.sync.dma_start(out[P * j : P * (j + 1), :], h2[j][:])
+            nc.gpsimd.tensor_tensor(h2[j], th[j], h2[j], ALU.add)
+            nc.sync.dma_start(out[P * j : P * (j + 1), :], h2[j])
         turned_sums = new("turned", [P, IN_PSUM, M], F32)
         for j in range(1, PLAIN, 2):
             e = j // 2
-            summed = psum.tile([P, M], F32, name="summed", tag="bank%d" % (2 * e))
+            summed = psum.tile([P, M], F32, name="summed", tag="bank%d" % (2 * e + 1))
             for m0 in range(0, M, P):
                 cols = slice(m0, m0 + P)
                 nc.tensor.matmul(summed[:, cols], h2[j][:, cols], ident[:], start=True, stop=False, is_transpose=True)
                 nc.tensor.matmul(summed[:, cols], th[j][:, cols], ident[:], start=False, stop=True, is_transpose=True)
             nc.scalar.copy(turned_sums[:, e, :], summed[:])
-            back = psum.tile([P, M], F32, name="back", tag="bank%d" % (2 * e + 1))
+            back = psum.tile([P, M], F32, name="back", tag="bank%d" % (2 * e + 2))
             for m0 in range(0, M, P):
                 cols = slice(m0, m0 + P)
                 nc.tensor.transpose(back[:, cols], turned_sums[:, e, cols], ident[:])
-            nc.scalar.copy(h2[j][:], back[:])
-            nc.scalar.dma_start(out[P * j : P * (j + 1), :], h2[j][:])
+            nc.scalar.copy(h2[j], back[:])
+            nc.scalar.dma_start(out[P * j : P * (j + 1), :], h2[j])
         result = new("result", [P, TILES - PLAIN, M], F32)
         for j in range(PLAIN, TILES):
             for cols in (slice(0, M - P), slice(M - P, M)) if j == TILES - 1 else (slice(0, M),):

@@ -27,22 +27,23 @@ GROUPS = H // GROUP
 PLAIN = 5
 IN_PSUM = 2
 KB = 1024
-SPLIT = 2560
+LAG = 4
+SHARES = (24, 20)
 
 
 def lay_out():
     half_kb = {
         "table0": 0, "table1": 32, "table2": 64,
         "h4": 0, "h5": 8, "h6": 16, "h7": 24,
-        "z_moved0": 32, "z_moved1": 40, "h2_4": 40, "z_il1": 48, "z_codes0": 56, "z_codes1": 60,
-        "z_il0": 64, "h1_7b": 64, "result": 72, "h1_6": 88, "th7": 92,
-        "raw_02": 96, "v_last1": 96, "stage_02": 100, "stage_1ab": 100,
-        "raw_10": 104, "raw_12": 108, "codes_12": 104, "h1_0": 106, "stage_A2": 101, "stage_B1": 101,
-        "raw_A1": 210, "codes_A2": 210, "stage_C0": 208, "h2_0": 216, "raw_A2": 218, "th0": 224,
-        "raw_B1": 136, "raw_B2": 144, "codes_B0": 136, "stage_B2": 138, "stage_C1": 138, "h1_2": 144,
-        "raw_C1": 156, "th3": 153, "codes_C0": 157, "stage_62": 159, "stage_72": 161, "z0": 161,
-        "raw_72": 170, "h1_4": 170, "h2_2": 170, "codes_72": 178, "th4": 178,
-        "tab_plane": 190, "v_last0": 190, "codes_02": 198, "stage_A0": 198, "stage_A1": 198,
+        "codes_F": 32, "z_moved0": 36, "h1_7a": 36, "h1_7b": 38, "z_il1": 52, "z_codes1": 60,
+        "result": 70, "h1_6": 44, "h2_4": 42, "th7": 92,
+        "raw_02": 96, "v_last1": 96, "stage_12": 100, "stage_A0": 100, "stage_21": 100, "codes_12": 104, "th0": 104,
+        "raw_A1": 108, "codes_21": 108, "codes_31": 109, "stage_A2": 110, "stage_W0a": 110, "stage_W1a": 108, "h1_2": 112, "raw_A2": 118, "h2_0": 118,
+        "th2": 157, "raw_W0": 164, "codes_W1a": 167, "stage_W2b": 169, "stage_W2a": 172, "h2_2": 175,
+        "codes_A2": 148, "stage_W0b": 148, "h1_3": 152, "stage_W1b": 152,
+        "raw_W2": 184, "h1_4": 184, "z_codes0": 184, "h1_5": 188, "codes_62": 192, "codes_72": 193, "codes_W1b": 194,
+        "tab_plane": 200, "v_words1": 200, "plane_12": 208, "stage_31": 208,
+        "plane_62": 212, "th4": 212, "plane_72": 216, "th5": 216, "z_il0": 165, "z_moved1": 165, "w4_dealt": 165, "plane_dealt": 169,
     }
     return {name: at * KB // 2 for name, at in half_kb.items()}
 
@@ -66,7 +67,8 @@ def tile_list_recipe_citation_cross_kernel(
         pos1_sb = keep.tile([P, M // 16], U16, name="pos1_sb")
         pos2_sb = keep.tile([P, M // 16], U16, name="pos2_sb")
         vec_rows = keep.tile([P, P], F32, name="vec_rows")
-        vec_cols = keep.tile([P, 3 * TILES], F32, name="vec_cols")
+        vec_cols = keep.tile([P, 12], F32, name="vec_cols")
+        vec_dealt = keep.tile([P, 3, 8], F32, name="vec_dealt")
         ident = keep.tile([P, P], F32, name="ident")
         tab_plane = new("tab_plane", [P, T], U8)
         w4_plane = keep.tile([P, HP * H], U8, name="w4_plane", align_bytes=64)
@@ -78,11 +80,9 @@ def tile_list_recipe_citation_cross_kernel(
 
         table = []
 
-        def load_table(a, first=0, stop=T):
-            if first == 0:
-                table.append(new("table%d" % a, [P, T], U32))
-            words = tab_words[a].rearrange("p t i -> p (t i)").bitcast(I32)
-            nc.sync.dma_start(table[a][:, first:stop].bitcast(I32), words[:, first:stop])
+        def load_table(a):
+            table.append(new("table%d" % a, [P, T], U32))
+            nc.sync.dma_start(table[a][:].bitcast(I32), tab_words[a].rearrange("p t i -> p (t i)").bitcast(I32))
 
         def load_w1(dst, a, first, count):
             nc.sync.dma_start(
@@ -102,27 +102,23 @@ def tile_list_recipe_citation_cross_kernel(
                 tab_plane[32 * q : 32 * q + 4 * KP, :].bitcast(I32),
                 tab_scales[:, 4 * q : 4 * q + 4, :].bitcast(I32),
             )
-        load_piece("00", 0, 0, 1)
-        load_table(1)
+        load_piece("F0", 0, 0, 2)
+        load_piece("F1", 1, 0, 2)
         nc.sync.dma_start(pos1_sb[:], pos1)
         for i, vec in enumerate((b1, gain, b2)):
-            nc.sync.dma_start(vec_rows[TILES * i : TILES * (i + 1), :], vec.rearrange("(j p) -> j p", p=P))
-        load_table(2, 0, SPLIT)
-        load_piece("01", 1, 0, 1)
-        load_table(2, SPLIT, T)
+            nc.sync.dma_start(vec_rows[4 * i : 4 * (i + 1), :], vec[0 : H // 2].rearrange("(j p) -> j p", p=P))
+        load_table(1)
+        load_table(2)
         load_piece("02", 2, 0, 1)
-        for a in range(KP):
-            load_piece("1%d" % a, a, 1, 1)
+        load_piece("12", 2, 1, 1)
         load_piece("A0", 0, 2, 2)
         nc.sync.dma_start(pos2_sb[:], pos2)
         load_piece("A1", 1, 2, 2)
         load_piece("A2", 2, 2, 2)
         for a in range(KP):
-            load_piece("B%d" % a, a, 4, 2)
-        for a in range(KP - 1):
-            load_piece("C%d" % a, a, 6, 2)
-        load_piece("62", 2, 6, 1)
-        load_piece("72", 2, 7, 1)
+            load_piece("W%d" % a, a, 4, 4)
+        for i, vec in enumerate((b1, gain, b2)):
+            nc.sync.dma_start(vec_dealt[:, i, 0:4], vec[H // 2 : H].rearrange("(p t) -> p t", t=4))
         nc.sync.dma_start(
             w4_sb[:].bitcast(I32).rearrange("p (a c) -> p a c", a=HP),
             w4_words.bitcast(I32).rearrange("a p c -> p a c"),
@@ -136,17 +132,20 @@ def tile_list_recipe_citation_cross_kernel(
         make_identity(nc, ident[:])
         turned = psum.tile([P, P], F32, name="turned", tag="bank7")
         nc.tensor.transpose(turned[:], vec_rows[:], ident[:])
-        nc.scalar.copy(vec_cols[:], turned[:, 0 : 3 * TILES])
+        nc.scalar.copy(vec_cols[:], turned[:, 0:12])
 
         def column(i, j):
-            return vec_cols[:, TILES * i + j : TILES * i + j + 1]
+            return vec_cols[:, 4 * i + j : 4 * i + j + 1] if j < 4 else vec_dealt[:, i, j - 4 : j - 3]
+
+        def rows_of(j):
+            return out[P * j : P * (j + 1), :] if j < 4 else out[H // 2 : H, :].rearrange("(p t) m -> t p m", t=4)[j - 4]
 
         v_words = []
         v_plane = keep.tile([P, S], U8, name="v_plane", align_bytes=64)
         for a in range(KP - 1):
             tile = new("v_words%d" % a, [P, S], U32)
             nc.vector.tensor_copy(tile[:], table[a][:].indirect(offs_sb[:]))
-            v_words.append([tile[:, BANK * s : BANK * (s + 1)] for s in range(2)])
+            v_words.append([(0, S, tile)])
             if a == 0:
                 nc.vector.tensor_copy(v_plane[:], tab_plane[:].indirect(offs_sb[:]))
 
@@ -196,11 +195,39 @@ def tile_list_recipe_citation_cross_kernel(
                 rounder(staged[stage][:, at : at + cols], raw[name][:])
                 at = at + cols
 
+        def round_part(stage, name, e, rounder):
+            staged[stage] = new("stage_" + stage, [P, 4 * P], BF16)
+            rounder(staged[stage][:], raw[name][:, :, P * e : P * (e + 1)])
+
+        def deal(engine, grouped, name, u):
+            if engine == "gpsimd":
+                nc.gpsimd.tensor_scalar(
+                    grouped.rearrange("p (t m j) -> p m t j", t=2, j=4),
+                    raw[name][:].rearrange("p j (m t) -> p m t j", t=4)[:, :, 2 * u : 2 * u + 2, :],
+                    1.0,
+                    0.0,
+                    ALU.mult,
+                    ALU.add,
+                )
+            else:
+                (nc.scalar.copy if engine == "scalar" else nc.vector.tensor_copy)(
+                    grouped.rearrange("p (t m j) -> p m j t", t=2, j=4),
+                    raw[name][:].rearrange("p j (m t) -> p m j t", t=4)[:, :, :, 2 * u : 2 * u + 2],
+                )
+
+        def deal_half(name, u, engine):
+            stage = name + "ab"[u]
+            staged[stage] = new("stage_" + stage, [P, 8 * P], BF16)
+            deal(engine, staged[stage][:], name, u)
+
+        def quantise_half(name, u, a):
+            quantise_stage(name + "ab"[u], 4 + 2 * u, 2, (a,))
+
         def quantise_stage(stage, first, count, passes):
             quantise(stage, staged[stage], first, count, passes)
 
         h, banks, h1, th, h2, z_rows = {}, {}, {}, {}, {}, {}
-        z_moved = [new("z_moved%d" % b, [P, 4 * M], BF16) for b in range(HP)]
+        z_moved = [new("z_moved0", [P, 4 * M], BF16)]
         bank_tags = []
 
         def spans(j):
@@ -214,24 +241,30 @@ def tile_list_recipe_citation_cross_kernel(
 
         def product(j, s, a):
             first, count = spans(j)[s]
-            nc.tensor.matmul_mx(
-                out=banks[j][s][:],
-                lhsT=w1_codes[j, a][0].bitcast(FP8X4),
-                lhsT_scale=w1_codes[j, a][1],
-                rhs=v_words[a][first // BANK][:, first % BANK : first % BANK + count].bitcast(FP8X4),
-                rhs_scale=v_plane[4 * a : P, first : first + count],
-                start=(a == 0),
-                stop=(a == KP - 1),
-            )
+            cuts = [
+                (max(first, lo), min(first + count, hi), lo, tile)
+                for lo, hi, tile in v_words[a]
+                if lo < first + count and first < hi
+            ]
+            for lo, hi, base, tile in cuts:
+                nc.tensor.matmul_mx(
+                    out=banks[j][s][:, lo - first : hi - first],
+                    lhsT=w1_codes[j, a][0].bitcast(FP8X4),
+                    lhsT_scale=w1_codes[j, a][1],
+                    rhs=tile[:, lo - base : hi - base].bitcast(FP8X4),
+                    rhs_scale=v_plane[4 * a : P, lo:hi],
+                    start=(a == 0),
+                    stop=(a == KP - 1 and hi == first + count),
+                )
 
         def multiply(j):
             open_banks(j)
-            for s in range(len(spans(j))):
-                for a in range(KP):
-                    product(j, s, a)
+            steps = [(s, a) for s in range(len(spans(j))) for a in range(KP)]
+            for s, a in sorted(steps, key=lambda step: step[1] > (j < 6)) if j >= 4 else steps:
+                product(j, s, a)
 
         def empty(j):
-            h[j] = new("h%d" % j, [P, S], F32)
+            h[j] = new("h%d" % j, [P, S], F32)[:]
             for s, (first, count) in enumerate(spans(j)):
                 nc.scalar.copy(h[j][:, first : first + count], banks[j][s][:])
 
@@ -248,172 +281,200 @@ def tile_list_recipe_citation_cross_kernel(
                 h1[name] = new(name, [P, cols.stop - cols.start], F32)[:]
                 dst = h1[name]
             else:
-                dst = shared(h1, "h1_", j, {2: 2, 4: 2}, F32)
-            nc.vector.tensor_copy(dst, h[j][:].indirect(pos1_sb[:, cols.start // 16 : cols.stop // 16]))
+                dst = shared(h1, "h1_", j, {}, F32)
+            nc.vector.tensor_copy(dst, h[j].indirect(pos1_sb[:, cols.start // 16 : cols.stop // 16]))
 
         def gather2(j):
-            nc.vector.tensor_copy(shared(h2, "h2_", j, {0: 2, 2: 2}, F32), h[j][:].indirect(pos2_sb[:]))
+            nc.vector.tensor_copy(shared(h2, "h2_", j, {0: 2, 2: 2}, F32), h[j].indirect(pos2_sb[:]))
 
         def bound(j, name=None, cols=slice(0, M)):
-            dst = shared(th, "th", j, {0: 2, 4: 3}, F32)
+            dst = shared(th, "th", j, {2: 2, 5: 2}, F32)
             nc.scalar.activation(dst[:, cols], h1[name or j], ACT.Tanh, bias=column(0, j))
 
         def scale(j, on_gpsimd, cols=slice(0, M)):
-            shared(z_rows, "z", j, {0: 4}, BF16)
+            shared(z_rows, "z", j, {}, BF16)
             if on_gpsimd:
                 nc.gpsimd.tensor_scalar(z_rows[j][:, cols], th[j][:, cols], column(1, j), 0.0, ALU.mult, ALU.add)
             else:
                 nc.scalar.activation(z_rows[j][:, cols], th[j][:, cols], ACT.Copy, scale=column(1, j))
-            moved = z_moved[j // 4][32 * (j % 4) : 32 * (j % 4 + 1), :].rearrange("q (t m) -> q t m", t=4)
-            nc.sync.dma_start(moved[:, :, cols], z_rows[j][:, cols])
+            if j < 4:
+                moved = z_moved[0][32 * j : 32 * (j + 1), :].rearrange("q (t m) -> q t m", t=4)
+                nc.sync.dma_start(moved, z_rows[j])
 
-        round_into("0ab", ("00", round_on_scalar), ("01", round_on_scalar))
-        quantise_stage("0ab", 0, 1, (0, 1))
-        last = [new("v_last%d" % s, [P, BANK], U32) for s in range(2)]
-        v_words.append([tile[:] for tile in last])
-        gather_last(last[0][:], 0, 512)
+        round_into("F", ("F0", round_on_scalar), ("F1", round_on_scalar))
+        quantise_stage("F", 0, 2, (0, 1))
+        last = [new("v_last0", [P, 768], U32), new("v_last1", [P, 256], U32)]
+        v_words.append([(0, 768, last[0]), (768, S, last[1])])
+        gather_last(last[0][:, 0:512], 0, 512)
+        gather_last(last[0][:, 512:768], 512, 256)
         round_into("02", ("02", round_on_scalar))
         quantise_stage("02", 0, 1, (2,))
-        gather_last(last[1][:, 0:256], 512, 256)
-        gather_last(last[1][:, 256:512], 768, 256)
-        multiply(0)
-        round_into("1ab", ("10", round_on_gpsimd), ("11", round_on_scalar))
-        empty(0)
-        round_into("12", ("12", round_on_vector))
-        quantise_stage("1ab", 1, 1, (0, 1))
+        gather_last(last[1][:], 768, 256)
+        round_into("12", ("12", round_on_scalar))
         quantise_stage("12", 1, 1, (2,))
+        multiply(0)
         multiply(1)
-        round_into("A0", ("A0", round_on_scalar))
+        round_into("A0", ("A0", round_on_gpsimd))
+        empty(0)
         gather1(0)
-        quantise_stage("A0", 2, 2, (0,))
-        round_into("A1", ("A1", round_on_gpsimd))
         empty(1)
-        round_into("A2", ("A2", round_on_scalar))
+        quantise_stage("A0", 2, 2, (0,))
+        round_part("21", "A1", 0, round_on_gpsimd)
+        round_part("31", "A1", 1, round_on_scalar)
         gather1(1)
         bound(0)
+        scale(0, False)
         bound(1)
-        round_into("B0", ("B0", round_on_scalar))
-        quantise_stage("A1", 2, 2, (1,))
+        scale(1, False)
+        round_into("A2", ("A2", round_on_vector))
+        quantise_stage("21", 2, 1, (1,))
+        quantise_stage("31", 3, 1, (1,))
         quantise_stage("A2", 2, 2, (2,))
         multiply(2)
         multiply(3)
-        round_into("B1", ("B1", round_on_gpsimd))
+        deal_half("W0", 0, "gpsimd")
         gather2(0)
         gather2(1)
+        quantise_half("W0", 0, 0)
+        deal_half("W1", 0, "gpsimd")
         empty(2)
         empty(3)
-        round_into("C0", ("C0", round_on_scalar))
-        quantise_stage("B0", 4, 2, (0,))
-        round_into("B2", ("B2", round_on_vector))
-        quantise_stage("B1", 4, 2, (1,))
-        quantise_stage("B2", 4, 2, (2,))
-        multiply(4)
-        multiply(5)
-        round_into("C1", ("C1", round_on_gpsimd))
+        deal_half("W0", 1, "scalar")
         gather1(2)
         gather1(3)
-        bound(2)
-        empty(4)
-        bound(3)
-        empty(5)
-        quantise_stage("C0", 6, 2, (0,))
-        round_into("62", ("62", round_on_vector))
-        round_into("72", ("72", round_on_vector))
-        quantise_stage("C1", 6, 2, (1,))
-        quantise_stage("62", 6, 1, (2,))
-        quantise_stage("72", 7, 1, (2,))
+        for j in (2, 3):
+            bound(j)
+        for j in (2, 3):
+            scale(j, False)
+        deal_half("W1", 1, "scalar")
+        quantise_half("W1", 0, 1)
+        deal_half("W2", 0, "vector")
+        quantise_half("W0", 1, 0)
+        quantise_half("W2", 0, 2)
+        deal_half("W2", 1, "gpsimd")
+        multiply(4)
+        multiply(5)
+        gather2(2)
+        gather2(3)
+        quantise_half("W1", 1, 1)
+        for e in range(2):
+            quantise("%d2" % (6 + e), staged["W2b"][:, 4 * P * e : 4 * P * (e + 1)], 6 + e, 1, (2,))
         multiply(6)
         multiply(7)
-        for j in range(4):
-            scale(j, True)
+        z_codes, z_planes, z_il = {}, {}, {}
+        z_il[0] = new("z_il0", [P, 4 * M], BF16)
+        nc.gpsimd.tensor_scalar(
+            z_il[0][:].rearrange("p (m t) -> p m t", t=4),
+            z_moved[0][:].rearrange("p (t m) -> p m t", t=4),
+            1.0,
+            0.0,
+            ALU.mult,
+            ALU.add,
+        )
+        empty(4)
+        empty(5)
         gather1(4)
         gather1(5)
         empty(6)
+        bound(4)
         gather1(6)
         empty(7)
+        def quantise_z(b, m0, width):
+            if b not in z_codes:
+                z_codes[b] = new("z_codes%d" % b, [P, M], U32)
+                z_planes[b] = new("z_plane%d" % b, [P, M], U8)
+            nc.vector.quantize_mx(
+                out=z_codes[b][:, m0 : m0 + width].bitcast(FP8X4),
+                scales=z_planes[b][:, m0 : m0 + width],
+                in_=z_il[b][:, 4 * m0 : 4 * (m0 + width)],
+            )
+
+        quantise_z(0, 0, M)
         halves = (("h1_7a", slice(0, M // 2)), ("h1_7b", slice(M // 2, M)))
         for name, cols in halves:
             gather1(7, name, cols)
-        for j in range(4, 7):
+        z_moved.append(new("z_moved1", [P, 4 * M], BF16))
+        for e in range(4):
+            z_rows[4 + e] = z_moved[1][:, M * e : M * (e + 1)]
+        scale(4, True)
+        for j in range(5, 7):
             bound(j)
-            scale(j, True)
+            scale(j, j == 5)
         for name, cols in halves:
             bound(7, name, cols)
         for name, cols in halves:
             scale(7, False, cols)
-        for j in range(2, PLAIN - 1):
-            gather2(j)
 
-        z_codes, z_planes = [], []
-
-        def quantise_z(b, shares):
-            z_il = new("z_il%d" % b, [P, 4 * M], BF16)
-            codes = new("z_codes%d" % b, [P, M], U32)
-            plane = new("z_plane%d" % b, [P, M], U8)
-            width = M // len(shares)
-            for m0, shared in zip(range(0, M, width), shares):
-                dst = z_il[:].rearrange("p (c i t) -> p c t i", i=4, t=4)
-                src = z_moved[b][:].rearrange("p (t c i) -> p c t i", i=4, t=4)
-                c0, c1 = m0 // 4, (m0 + width) // 4
-                nc.scalar.copy(dst[:, c0 : c0 + shared], src[:, c0 : c0 + shared])
-                if b == 0:
-                    dst = z_il[:].rearrange("p (m t) -> p m t", t=4)[:, 4 * (c0 + shared) : 4 * c1]
-                    src = z_moved[b][:].rearrange("p (t m) -> p m t", t=4)[:, 4 * (c0 + shared) : 4 * c1]
-                    nc.gpsimd.tensor_scalar(dst, src, 1.0, 0.0, ALU.mult, ALU.add)
-                else:
-                    nc.vector.tensor_copy(dst[:, c0 + shared : c1], src[:, c0 + shared : c1])
-                nc.vector.quantize_mx(
-                    out=codes[:, m0 : m0 + width].bitcast(FP8X4),
-                    scales=plane[:, m0 : m0 + width],
-                    in_=z_il[:, 4 * m0 : 4 * (m0 + width)],
-                )
-            z_codes.append(codes)
-            z_planes.append(plane)
-
-        quantise_z(0, (76,))
-        quantise_z(1, (36, 20))
         gather2(PLAIN - 1)
+        z_il[1] = new("z_il1", [P, 4 * M], BF16)
+        dst = z_il[1][:].rearrange("p (c i t) -> p c t i", i=4, t=4)
+        src = z_moved[1][:].rearrange("p (t c i) -> p c t i", i=4, t=4)
+        for c0, share in zip((0, 64), SHARES):
+            nc.scalar.copy(dst[:, c0 : c0 + share], src[:, c0 : c0 + share])
+            nc.vector.tensor_copy(dst[:, c0 + share : c0 + 64], src[:, c0 + share : c0 + 64])
+        for m0 in (0, M // 2):
+            quantise_z(1, m0, M // 2)
 
-        ys = []
+        w4_dealt = new("w4_dealt", [P, HP * H], U8)
+        nc.scalar.copy(
+            w4_dealt[:].bitcast(U16).rearrange("p (a t c) -> p a c t", a=HP, t=4),
+            w4_sb[:].bitcast(U16).rearrange("p (a b c t) -> p b a c t", a=HP, b=2, t=4)[:, 1],
+        )
+        plane_dealt = new("plane_dealt", [P, HP * H // 2], U8)
+        nc.vector.tensor_copy(
+            plane_dealt[:].rearrange("p (a t c) -> p a t c", a=HP, t=4),
+            w4_plane[:].rearrange("p (a b c t) -> p b a t c", a=HP, b=2, t=4)[:, 1],
+        )
+
+        summed = {}
+        turned_sums = new("turned", [P, IN_PSUM, M], F32)
+
+        def turn_in(j, rows, first):
+            for m0 in range(0, M, P):
+                nc.tensor.matmul(
+                    summed[j][:, m0 : m0 + P],
+                    rows[:, m0 : m0 + P],
+                    ident[:],
+                    start=(first and m0 == 0),
+                    stop=(not first and m0 == M - P),
+                    is_transpose=True,
+                )
+
+        for j in (1, 3):
+            summed[j] = psum.tile([P, M], F32, name="summed", tag="bank%d" % ((7 + j // 2) % 8))
+            turn_in(j, h2[j], True)
         for j in range(TILES):
-            y = psum.tile([P, M], F32, name="y", tag="bank%d" % ((j + 1) % 8))
-            order = range(HP) if j < TILES - 2 else range(HP - 1, -1, -1)
+            y = psum.tile([P, M], F32, name="y", tag="bank%d" % (1 + j % 6))
+            order = range(HP) if j < 4 else range(HP - 1, -1, -1)
             for a in order:
-                n0 = H * a + P * j
+                words, plane = (w4_sb, w4_plane) if j < 4 else (w4_dealt, plane_dealt)
+                n0 = H * a + P * j if j < 4 else H // 2 * a + P * (j - 4)
                 nc.tensor.matmul_mx(
                     out=y[:],
-                    lhsT=w4_sb[:, 2 * n0 : 2 * (n0 + P)].bitcast(FP4X4),
-                    lhsT_scale=w4_plane[:, n0 : n0 + P],
+                    lhsT=words[:, 2 * n0 : 2 * (n0 + P)].bitcast(FP4X4),
+                    lhsT_scale=plane[:, n0 : n0 + P],
                     rhs=z_codes[a][:].bitcast(FP8X4),
                     rhs_scale=z_planes[a][:],
                     start=(a == order[0]),
                     stop=(a == order[-1]),
                 )
-            ys.append(y)
-
-        for j in range(TILES):
-            nc.vector.scalar_tensor_tensor(th[j], ys[j][:], column(2, j), th[j], ALU.add, ALU.mult)
+            nc.vector.scalar_tensor_tensor(th[j], y[:], column(2, j), th[j], ALU.add, ALU.mult)
+            if j - LAG in summed:
+                turn_in(j - LAG, th[j - LAG], False)
+                nc.scalar.copy(turned_sums[:, (j - LAG) // 2, :], summed[j - LAG][:])
         for j in range(0, PLAIN, 2):
             nc.gpsimd.tensor_tensor(h2[j], th[j], h2[j], ALU.add)
-            nc.sync.dma_start(out[P * j : P * (j + 1), :], h2[j])
-        turned_sums = new("turned", [P, IN_PSUM, M], F32)
-        for j in range(1, PLAIN, 2):
-            e = j // 2
-            summed = psum.tile([P, M], F32, name="summed", tag="bank%d" % (2 * e + 1))
+            nc.sync.dma_start(rows_of(j), h2[j])
+        for j in summed:
+            back = psum.tile([P, M], F32, name="back", tag="bank%d" % ((7 + j // 2) % 8))
             for m0 in range(0, M, P):
                 cols = slice(m0, m0 + P)
-                nc.tensor.matmul(summed[:, cols], h2[j][:, cols], ident[:], start=True, stop=False, is_transpose=True)
-                nc.tensor.matmul(summed[:, cols], th[j][:, cols], ident[:], start=False, stop=True, is_transpose=True)
-            nc.scalar.copy(turned_sums[:, e, :], summed[:])
-            back = psum.tile([P, M], F32, name="back", tag="bank%d" % (2 * e + 2))
-            for m0 in range(0, M, P):
-                cols = slice(m0, m0 + P)
-                nc.tensor.transpose(back[:, cols], turned_sums[:, e, cols], ident[:])
+                nc.tensor.transpose(back[:, cols], turned_sums[:, j // 2, cols], ident[:])
             nc.scalar.copy(h2[j], back[:])
-            nc.scalar.dma_start(out[P * j : P * (j + 1), :], h2[j])
+            nc.scalar.dma_start(rows_of(j), h2[j])
         result = new("result", [P, TILES - PLAIN, M], F32)
         for j in range(PLAIN, TILES):
             for cols in (slice(0, M - P), slice(M - P, M)) if j == TILES - 1 else (slice(0, M),):
                 picks = pos2_sb[:, cols.start // 16 : cols.stop // 16]
-                nc.vector.tensor_tensor(result[:, j - PLAIN, cols], h[j][:].indirect(picks), th[j][:, cols], ALU.add)
-                nc.sync.dma_start(out[P * j : P * (j + 1), cols], result[:, j - PLAIN, cols])
+                nc.vector.tensor_tensor(result[:, j - PLAIN, cols], h[j].indirect(picks), th[j][:, cols], ALU.add)
+                nc.sync.dma_start(rows_of(j)[:, cols], result[:, j - PLAIN, cols])

@@ -27,23 +27,23 @@ GROUPS = H // GROUP
 PLAIN = 5
 IN_PSUM = 2
 KB = 1024
-LAG = 4
-SHARES = (24, 20)
+SHARES = (28, 24)
 
 
 def lay_out():
     half_kb = {
         "table0": 0, "table1": 32, "table2": 64,
         "h4": 0, "h5": 8, "h6": 16, "h7": 24,
-        "codes_F": 32, "z_moved0": 36, "h1_7a": 36, "h1_7b": 38, "z_il1": 52, "z_codes1": 60,
-        "result": 70, "h1_6": 44, "h2_4": 42, "th7": 92,
+        "codes_F": 32, "z_moved1": 33, "w4_dealt": 33, "plane_dealt": 37, "z_moved0": 40, "h1_7a": 41, "h1_7b": 43,
+        "h2_4": 46, "h1_6": 48, "z_il1": 52, "z_codes1": 60, "result": 70, "th7": 92,
         "raw_02": 96, "v_last1": 96, "stage_12": 100, "stage_A0": 100, "stage_21": 100, "codes_12": 104, "th0": 104,
-        "raw_A1": 108, "codes_21": 108, "codes_31": 109, "stage_A2": 110, "stage_W0a": 110, "stage_W1a": 108, "h1_2": 112, "raw_A2": 118, "h2_0": 118,
-        "th2": 157, "raw_W0": 164, "codes_W1a": 167, "stage_W2b": 169, "stage_W2a": 172, "h2_2": 175,
-        "codes_A2": 148, "stage_W0b": 148, "h1_3": 152, "stage_W1b": 152,
+        "raw_A0": 108, "h1_1": 108, "raw_A2": 118, "h2_0": 118, "plane_72": 126, "th5": 126,
+        "codes_A2": 148, "stage_W0b": 148, "th2": 157, "raw_W0": 164, "codes_W1a": 165,
         "raw_W2": 184, "h1_4": 184, "z_codes0": 184, "h1_5": 188, "codes_62": 192, "codes_72": 193, "codes_W1b": 194,
-        "tab_plane": 200, "v_words1": 200, "plane_12": 208, "stage_31": 208,
-        "plane_62": 212, "th4": 212, "plane_72": 216, "th5": 216, "z_il0": 165, "z_moved1": 165, "w4_dealt": 165, "plane_dealt": 169,
+        "tab_plane": 200, "v_words1": 200, "plane_12": 208, "stage_31": 208, "plane_62": 212, "th4": 212,
+        "raw_A1": 228, "codes_31": 228, "stage_A2": 232, "stage_W0a": 232, "codes_W0b": 233,
+        "z_il0": 217, "stage_W2b": 221, "stage_W2a": 224, "h2_2": 225,
+        "stage_W1a": 229, "h1_2": 235, "stage_W1b": 239,
     }
     return {name: at * KB // 2 for name, at in half_kb.items()}
 
@@ -266,7 +266,8 @@ def tile_list_recipe_citation_cross_kernel(
         def empty(j):
             h[j] = new("h%d" % j, [P, S], F32)[:]
             for s, (first, count) in enumerate(spans(j)):
-                nc.scalar.copy(h[j][:, first : first + count], banks[j][s][:])
+                move = nc.vector.tensor_copy if j == 0 and s > 0 else nc.scalar.copy
+                move(h[j][:, first : first + count], banks[j][s][:])
 
         def shared(book, prefix, j, counts, dtype):
             if j not in book:
@@ -281,7 +282,7 @@ def tile_list_recipe_citation_cross_kernel(
                 h1[name] = new(name, [P, cols.stop - cols.start], F32)[:]
                 dst = h1[name]
             else:
-                dst = shared(h1, "h1_", j, {}, F32)
+                dst = shared(h1, "h1_", j, {2: 2}, F32)
             nc.vector.tensor_copy(dst, h[j].indirect(pos1_sb[:, cols.start // 16 : cols.stop // 16]))
 
         def gather2(j):
@@ -347,9 +348,9 @@ def tile_list_recipe_citation_cross_kernel(
         for j in (2, 3):
             scale(j, False)
         deal_half("W1", 1, "scalar")
+        quantise_half("W0", 1, 0)
         quantise_half("W1", 0, 1)
         deal_half("W2", 0, "vector")
-        quantise_half("W0", 1, 0)
         quantise_half("W2", 0, 2)
         deal_half("W2", 1, "gpsimd")
         multiply(4)
@@ -399,7 +400,7 @@ def tile_list_recipe_citation_cross_kernel(
         scale(4, True)
         for j in range(5, 7):
             bound(j)
-            scale(j, j == 5)
+            scale(j, True)
         for name, cols in halves:
             bound(7, name, cols)
         for name, cols in halves:
@@ -449,19 +450,22 @@ def tile_list_recipe_citation_cross_kernel(
             for a in order:
                 words, plane = (w4_sb, w4_plane) if j < 4 else (w4_dealt, plane_dealt)
                 n0 = H * a + P * j if j < 4 else H // 2 * a + P * (j - 4)
-                nc.tensor.matmul_mx(
-                    out=y[:],
-                    lhsT=words[:, 2 * n0 : 2 * (n0 + P)].bitcast(FP4X4),
-                    lhsT_scale=plane[:, n0 : n0 + P],
-                    rhs=z_codes[a][:].bitcast(FP8X4),
-                    rhs_scale=z_planes[a][:],
-                    start=(a == order[0]),
-                    stop=(a == order[-1]),
-                )
+                width = M // 2 if (j, a) == (0, 1) else M
+                for m0 in range(0, M, width):
+                    nc.tensor.matmul_mx(
+                        out=y[:, m0 : m0 + width],
+                        lhsT=words[:, 2 * n0 : 2 * (n0 + P)].bitcast(FP4X4),
+                        lhsT_scale=plane[:, n0 : n0 + P],
+                        rhs=z_codes[a][:, m0 : m0 + width].bitcast(FP8X4),
+                        rhs_scale=z_planes[a][:, m0 : m0 + width],
+                        start=(a == order[0]),
+                        stop=(a == order[-1] and m0 + width == M),
+                    )
             nc.vector.scalar_tensor_tensor(th[j], y[:], column(2, j), th[j], ALU.add, ALU.mult)
-            if j - LAG in summed:
-                turn_in(j - LAG, th[j - LAG], False)
-                nc.scalar.copy(turned_sums[:, (j - LAG) // 2, :], summed[j - LAG][:])
+            if j >= TILES - IN_PSUM:
+                e = j - (TILES - IN_PSUM)
+                turn_in(2 * e + 1, th[2 * e + 1], False)
+                nc.scalar.copy(turned_sums[:, e, :], summed[2 * e + 1][:])
         for j in range(0, PLAIN, 2):
             nc.gpsimd.tensor_tensor(h2[j], th[j], h2[j], ALU.add)
             nc.sync.dma_start(rows_of(j), h2[j])

@@ -27,6 +27,7 @@ GROUPS = H // GROUP
 PLAIN = 5
 IN_PSUM = 2
 KB = 1024
+LAST = 320
 SHARES = (28, 24)
 
 
@@ -418,8 +419,8 @@ def tile_list_recipe_citation_cross_kernel(
 
         w4_dealt = new("w4_dealt", [P, HP * H], U8)
         nc.scalar.copy(
-            w4_dealt[:].bitcast(U16).rearrange("p (a t c) -> p a c t", a=HP, t=4),
-            w4_sb[:].bitcast(U16).rearrange("p (a b c t) -> p b a c t", a=HP, b=2, t=4)[:, 1],
+            w4_dealt[:].bitcast(U16).rearrange("p (a t c) -> p a t c", a=HP, t=4),
+            w4_sb[:].bitcast(U16).rearrange("p (a b c t) -> p b a t c", a=HP, b=2, t=4)[:, 1],
         )
         plane_dealt = new("plane_dealt", [P, HP * H // 2], U8)
         nc.vector.tensor_copy(
@@ -478,7 +479,7 @@ def tile_list_recipe_citation_cross_kernel(
             nc.scalar.dma_start(rows_of(j), h2[j])
         result = new("result", [P, TILES - PLAIN, M], F32)
         for j in range(PLAIN, TILES):
-            for cols in (slice(0, M - P), slice(M - P, M)) if j == TILES - 1 else (slice(0, M),):
+            for cols in (slice(0, LAST), slice(LAST, M)) if j == TILES - 1 else (slice(0, M),):
                 picks = pos2_sb[:, cols.start // 16 : cols.stop // 16]
                 nc.vector.tensor_tensor(result[:, j - PLAIN, cols], h[j].indirect(picks), th[j][:, cols], ALU.add)
                 nc.sync.dma_start(rows_of(j)[:, cols], result[:, j - PLAIN, cols])

@@ -70,6 +70,7 @@ def tile_list_recipe_citation_cross_kernel(
         vec_rows = keep.tile([P, P], F32, name="vec_rows")
         vec_cols = keep.tile([P, 12], F32, name="vec_cols")
         vec_dealt = keep.tile([P, 3, 8], F32, name="vec_dealt")
+        gain_late = [keep.tile([P, 8], F32, name="gain_late%d" % e) for e in range(2)]
         ident = keep.tile([P, P], F32, name="ident")
         tab_plane = new("tab_plane", [P, T], U8)
         w4_plane = keep.tile([P, HP * H], U8, name="w4_plane", align_bytes=64)
@@ -106,8 +107,8 @@ def tile_list_recipe_citation_cross_kernel(
         load_piece("F0", 0, 0, 2)
         load_piece("F1", 1, 0, 2)
         nc.sync.dma_start(pos1_sb[:], pos1)
-        for i, vec in enumerate((b1, gain, b2)):
-            nc.sync.dma_start(vec_rows[4 * i : 4 * (i + 1), :], vec[0 : H // 2].rearrange("(j p) -> j p", p=P))
+        for i, (vec, tiles) in enumerate(((b1, 4), (gain, 2), (b2, 4))):
+            nc.sync.dma_start(vec_rows[4 * i : 4 * i + tiles, :], vec[0 : P * tiles].rearrange("(j p) -> j p", p=P))
         load_table(1)
         load_table(2)
         load_piece("02", 2, 0, 1)
@@ -118,6 +119,8 @@ def tile_list_recipe_citation_cross_kernel(
         load_piece("A2", 2, 2, 2)
         for a in range(KP):
             load_piece("W%d" % a, a, 4, 4)
+        for e in range(2):
+            nc.sync.dma_start(gain_late[e][:, 0:1], gain[P * (2 + e) : P * (3 + e)].rearrange("(p o) -> p o", o=1))
         for i, vec in enumerate((b1, gain, b2)):
             nc.sync.dma_start(vec_dealt[:, i, 0:4], vec[H // 2 : H].rearrange("(p t) -> p t", t=4))
         nc.sync.dma_start(
@@ -300,8 +303,16 @@ def tile_list_recipe_citation_cross_kernel(
             else:
                 nc.scalar.activation(z_rows[j][:, cols], th[j][:, cols], ACT.Copy, scale=column(1, j))
             if j < 4:
-                moved = z_moved[0][32 * j : 32 * (j + 1), :].rearrange("q (t m) -> q t m", t=4)
-                nc.sync.dma_start(moved, z_rows[j])
+                move_rows(j)
+
+        def move_rows(j):
+            moved = z_moved[0][32 * j : 32 * (j + 1), :].rearrange("q (t m) -> q t m", t=4)
+            nc.sync.dma_start(moved, z_rows[j])
+
+        def scale_on_vector(j):
+            shared(z_rows, "z", j, {}, BF16)
+            nc.vector.tensor_scalar(z_rows[j], th[j], gain_late[j - 2][:, 0:1], 0.0, ALU.mult, ALU.add)
+            move_rows(j)
 
         round_into("F", ("F0", round_on_scalar), ("F1", round_on_scalar))
         quantise_stage("F", 0, 2, (0, 1))
@@ -346,13 +357,13 @@ def tile_list_recipe_citation_cross_kernel(
         gather1(3)
         for j in (2, 3):
             bound(j)
-        for j in (2, 3):
-            scale(j, False)
         deal_half("W1", 1, "scalar")
         quantise_half("W0", 1, 0)
         quantise_half("W1", 0, 1)
         deal_half("W2", 0, "vector")
+        scale_on_vector(2)
         quantise_half("W2", 0, 2)
+        scale_on_vector(3)
         deal_half("W2", 1, "gpsimd")
         multiply(4)
         multiply(5)

from contextlib import ExitStack

import concourse.mybir as mybir
from concourse.masks import make_identity

K, H, T, S, M = 1536, 1024, 4096, 1024, 512
FLOPS = 2 * K * H * S + 2 * H * H * M

F32 = mybir.dt.float32
BF16 = mybir.dt.bfloat16
I32 = mybir.dt.int32
U32 = mybir.dt.uint32
U16 = mybir.dt.uint16
U8 = mybir.dt.uint8
FP8X4 = mybir.dt.float8_e4m3fn_x4
FP4X4 = mybir.dt.float4_e2m1fn_x4
ACT = mybir.ActivationFunctionType
ALU = mybir.AluOpType

P = 128
KP = K // 512
HP = H // 512
BANK = 512
TILES = H // P
GROUP = 256
GROUPS = H // GROUP
PLAIN = 5
IN_PSUM = 2
KB = 1024
LAST = 320
SHARES = (28, 24)


def lay_out():
    half_kb = {
        "table0": 0, "table1": 32, "table2": 64,
        "h4": 0, "h5": 8, "h6": 16, "h7": 24,
        "codes_F": 32, "z_moved1": 33, "w4_dealt": 33, "plane_dealt": 37, "z_moved0": 40, "h1_7a": 41, "h1_7b": 43,
        "h2_4": 46, "h1_6": 48, "z_il1": 52, "z_codes1": 60, "result": 70, "th7": 92,
        "raw_02": 96, "v_last1": 96, "stage_12": 100, "stage_A0": 100, "stage_21": 100, "codes_12": 104, "th0": 104,
        "raw_A0": 108, "h1_1": 108, "raw_A2": 118, "h2_0": 118, "plane_72": 126, "th5": 126,
        "codes_A2": 148, "stage_W0b": 148, "th2": 157, "raw_W0": 164, "codes_W1a": 165,
        "raw_W2": 184, "h1_4": 184, "z_codes0": 184, "h1_5": 188, "codes_62": 192, "codes_72": 193, "codes_W1b": 194,
        "tab_plane": 200, "v_words1": 200, "plane_12": 208, "stage_31": 208, "plane_62": 212, "th4": 212,
        "raw_A1": 228, "codes_31": 228, "stage_A2": 232, "stage_W0a": 232, "codes_W0b": 233,
        "z_il0": 217, "stage_W2b": 221, "stage_W2a": 224, "h2_2": 225,
        "stage_W1a": 229, "h1_2": 235, "stage_W1b": 239,
    }
    return {name: at * KB // 2 for name, at in half_kb.items()}


def tile_list_recipe_citation_cross_kernel(
    tc, tab_words, tab_scales, offs, pos1, pos2, w1, b1, gain, w4_words, w4_scales, b2, out
):
    nc = tc.nc
    place = lay_out()
    with ExitStack() as ctx:
        keep = ctx.enter_context(tc.tile_pool(name="keep", bufs=1))
        laid = ctx.enter_context(tc.tile_pool(name="laid", bufs=1))
        psum = ctx.enter_context(tc.psum_pool(name="psum", bufs=1))

        def new(name, shape, dtype):
            if name in place:
                return laid.tile(shape, dtype, name=name, align_bytes=64, offset=place[name])
            return keep.tile(shape, dtype, name=name, align_bytes=64)

        offs_sb = keep.tile([P, S // 16], U16, name="offs_sb")
        pos1_sb = keep.tile([P, M // 16], U16, name="pos1_sb")
        pos2_sb = keep.tile([P, M // 16], U16, name="pos2_sb")
        vec_rows = keep.tile([P, P], F32, name="vec_rows")
        vec_cols = keep.tile([P, 12], F32, name="vec_cols")
        vec_dealt = keep.tile([P, 3, 8], F32, name="vec_dealt")
        gain_late = [keep.tile([P, 8], F32, name="gain_late%d" % e) for e in range(2)]
        ident = keep.tile([P, P], F32, name="ident")
        tab_plane = new("tab_plane", [P, T], U8)
        w4_plane = keep.tile([P, HP * H], U8, name="w4_plane", align_bytes=64)
        w4_sb = keep.tile([P, HP * 2 * H], U8, name="w4_sb", align_bytes=64)

        nc.vector.memset(tab_plane[:].bitcast(I32), 0)
        nc.vector.memset(vec_rows[:], 0.0)
        nc.vector.memset(w4_plane[:].bitcast(I32), 0)

        table = []

        def load_table(a):
            table.append(new("table%d" % a, [P, T], U32))
            nc.sync.dma_start(table[a][:].bitcast(I32), tab_words[a].rearrange("p t i -> p (t i)").bitcast(I32))

        def load_w1(dst, a, first, count):
            nc.sync.dma_start(
                dst, w1[512 * a : 512 * (a + 1), P * first : P * (first + count)].rearrange("(p j) c -> p j c", j=4)
            )

        raw = {}

        def load_piece(name, a, first, count):
            raw[name] = new("raw_" + name, [P, 4, P * count], F32)
            load_w1(raw[name][:], a, first, count)

        load_table(0)
        nc.sync.dma_start(offs_sb[:], offs)
        for q in range(4):
            (nc.sync if q == 3 else nc.gpsimd).dma_start(
                tab_plane[32 * q : 32 * q + 4 * KP, :].bitcast(I32),
                tab_scales[:, 4 * q : 4 * q + 4, :].bitcast(I32),
            )
        load_piece("F0", 0, 0, 2)
        load_piece("F1", 1, 0, 2)
        nc.sync.dma_start(pos1_sb[:], pos1)
        for i, (vec, tiles) in enumerate(((b1, 4), (gain, 2), (b2, 4))):
            nc.sync.dma_start(vec_rows[4 * i : 4 * i + tiles, :], vec[0 : P * tiles].rearrange("(j p) -> j p", p=P))
        load_table(1)
        load_table(2)
        load_piece("02", 2, 0, 1)
        load_piece("12", 2, 1, 1)
        load_piece("A0", 0, 2, 2)
        nc.sync.dma_start(pos2_sb[:], pos2)
        load_piece("A1", 1, 2, 2)
        load_piece("A2", 2, 2, 2)
        for a in range(KP):
            load_piece("W%d" % a, a, 4, 4)
        for e in range(2):
            nc.sync.dma_start(gain_late[e][:, 0:1], gain[P * (2 + e) : P * (3 + e)].rearrange("(p o) -> p o", o=1))
        for i, vec in enumerate((b1, gain, b2)):
            nc.sync.dma_start(vec_dealt[:, i, 0:4], vec[H // 2 : H].rearrange("(p t) -> p t", t=4))
        nc.sync.dma_start(
            w4_sb[:].bitcast(I32).rearrange("p (a c) -> p a c", a=HP),
            w4_words.bitcast(I32).rearrange("a p c -> p a c"),
        )
        for q in range(4):
            nc.sync.dma_start(
                w4_plane[32 * q : 32 * q + 4, :].bitcast(I32).rearrange("r (a c) -> r a c", a=HP),
                w4_scales[:, 4 * q : 4 * q + 4, :].bitcast(I32).rearrange("a r c -> r a c"),
            )

        make_identity(nc, ident[:])
        turned = psum.tile([P, P], F32, name="turned", tag="bank7")
        nc.tensor.transpose(turned[:], vec_rows[:], ident[:])
        nc.scalar.copy(vec_cols[:], turned[:, 0:12])

        def column(i, j):
            return vec_cols[:, 4 * i + j : 4 * i + j + 1] if j < 4 else vec_dealt[:, i, j - 4 : j - 3]

        def rows_of(j):
            return out[P * j : P * (j + 1), :] if j < 4 else out[H // 2 : H, :].rearrange("(p t) m -> t p m", t=4)[j - 4]

        v_words = []
        v_plane = keep.tile([P, S], U8, name="v_plane", align_bytes=64)
        for a in range(KP - 1):
            tile = new("v_words%d" % a, [P, S], U32)
            nc.vector.tensor_copy(tile[:], table[a][:].indirect(offs_sb[:]))
            v_words.append([(0, S, tile)])
            if a == 0:
                nc.vector.tensor_copy(v_plane[:], tab_plane[:].indirect(offs_sb[:]))

        w1_codes = {}

        def round_on_scalar(grouped, rows):
            nc.scalar.copy(
                grouped.rearrange("p (c i j) -> p c j i", i=4, j=4), rows.rearrange("p j (c i) -> p c j i", i=4)
            )

        def round_on_vector(grouped, rows):
            nc.vector.tensor_copy(
                grouped.rearrange("p (c i j) -> p c j i", i=4, j=4), rows.rearrange("p j (c i) -> p c j i", i=4)
            )

        def round_on_gpsimd(grouped, rows):
            nc.gpsimd.tensor_scalar(
                grouped.rearrange("p (c j) -> p c j", j=4),
                rows.rearrange("p j c -> p c j"),
                1.0,
                0.0,
                ALU.mult,
                ALU.add,
            )

        def quantise(name, grouped, first, count, passes):
            width = P * count * len(passes)
            codes = new("codes_" + name, [P, width], U32)
            plane = new("plane_" + name, [P, width], U8)
            nc.vector.quantize_mx(out=codes[:].bitcast(FP8X4), scales=plane[:], in_=grouped[:])
            for n, a in enumerate(passes):
                for e in range(count):
                    cols = slice(P * (count * n + e), P * (count * n + e + 1))
                    w1_codes[first + e, a] = (codes[:, cols], plane[:, cols])

        def gather_last(dst, first, count):
            nc.vector.tensor_copy(dst, table[KP - 1][:].indirect(offs_sb[:, first // 16 : (first + count) // 16]))

        staged = {}

        def round_into(stage, *pieces):
            width = sum(4 * raw[name].shape[2] for name, rounder in pieces)
            staged[stage] = new("stage_" + stage, [P, width], BF16)
            at = 0
            for name, rounder in pieces:
                cols = 4 * raw[name].shape[2]
                rounder(staged[stage][:, at : at + cols], raw[name][:])
                at = at + cols

        def round_part(stage, name, e, rounder):
            staged[stage] = new("stage_" + stage, [P, 4 * P], BF16)
            rounder(staged[stage][:], raw[name][:, :, P * e : P * (e + 1)])

        def deal(engine, grouped, name, u):
            if engine == "gpsimd":
                nc.gpsimd.tensor_scalar(
                    grouped.rearrange("p (t m j) -> p m t j", t=2, j=4),
                    raw[name][:].rearrange("p j (m t) -> p m t j", t=4)[:, :, 2 * u : 2 * u + 2, :],
                    1.0,
                    0.0,
                    ALU.mult,
                    ALU.add,
                )
            else:
                (nc.scalar.copy if engine == "scalar" else nc.vector.tensor_copy)(
                    grouped.rearrange("p (t m j) -> p m j t", t=2, j=4),
                    raw[name][:].rearrange("p j (m t) -> p m j t", t=4)[:, :, :, 2 * u : 2 * u + 2],
                )

        def deal_half(name, u, engine):
            stage = name + "ab"[u]
            staged[stage] = new("stage_" + stage, [P, 8 * P], BF16)
            deal(engine, staged[stage][:], name, u)

        def quantise_half(name, u, a):
            quantise_stage(name + "ab"[u], 4 + 2 * u, 2, (a,))

        def quantise_stage(stage, first, count, passes):
            quantise(stage, staged[stage], first, count, passes)

        h, banks, h1, th, h2, z_rows = {}, {}, {}, {}, {}, {}
        z_moved = [new("z_moved0", [P, 4 * M], BF16)]
        bank_tags = []

        def spans(j):
            return ((0, 512), (512, 256), (768, 256)) if j == 0 else ((0, 512), (512, 512))

        def open_banks(j):
            banks[j] = []
            for first, count in spans(j):
                banks[j].append(psum.tile([P, count], F32, name="acc", tag="bank%d" % (len(bank_tags) % 8)))
                bank_tags.append(j)

        def product(j, s, a):
            first, count = spans(j)[s]
            cuts = [
                (max(first, lo), min(first + count, hi), lo, tile)
                for lo, hi, tile in v_words[a]
                if lo < first + count and first < hi
            ]
            for lo, hi, base, tile in cuts:
                nc.tensor.matmul_mx(
                    out=banks[j][s][:, lo - first : hi - first],
                    lhsT=w1_codes[j, a][0].bitcast(FP8X4),
                    lhsT_scale=w1_codes[j, a][1],
                    rhs=tile[:, lo - base : hi - base].bitcast(FP8X4),
                    rhs_scale=v_plane[4 * a : P, lo:hi],
                    start=(a == 0),
                    stop=(a == KP - 1 and hi == first + count),
                )

        def multiply(j):
            open_banks(j)
            steps = [(s, a) for s in range(len(spans(j))) for a in range(KP)]
            for s, a in sorted(steps, key=lambda step: step[1] > (j < 6)) if j >= 4 else steps:
                product(j, s, a)

        def empty(j):
            h[j] = new("h%d" % j, [P, S], F32)[:]
            for s, (first, count) in enumerate(spans(j)):
                move = nc.vector.tensor_copy if j == 0 and s > 0 else nc.scalar.copy
                move(h[j][:, first : first + count], banks[j][s][:])

        def shared(book, prefix, j, counts, dtype):
            if j not in book:
                count = counts.get(j, 1)
                tile = new("%s%d" % (prefix, j), [P, count * M], dtype)
                for e in range(count):
                    book[j + e] = tile[:, M * e : M * (e + 1)]
            return book[j]

        def gather1(j, name=None, cols=slice(0, M)):
            if name:
                h1[name] = new(name, [P, cols.stop - cols.start], F32)[:]
                dst = h1[name]
            else:
                dst = shared(h1, "h1_", j, {2: 2}, F32)
            nc.vector.tensor_copy(dst, h[j].indirect(pos1_sb[:, cols.start // 16 : cols.stop // 16]))

        def gather2(j):
            nc.vector.tensor_copy(shared(h2, "h2_", j, {0: 2, 2: 2}, F32), h[j].indirect(pos2_sb[:]))

        def bound(j, name=None, cols=slice(0, M)):
            dst = shared(th, "th", j, {2: 2, 5: 2}, F32)
            nc.scalar.activation(dst[:, cols], h1[name or j], ACT.Tanh, bias=column(0, j))

        def scale(j, on_gpsimd, cols=slice(0, M)):
            shared(z_rows, "z", j, {}, BF16)
            if on_gpsimd:
                nc.gpsimd.tensor_scalar(z_rows[j][:, cols], th[j][:, cols], column(1, j), 0.0, ALU.mult, ALU.add)
            else:
                nc.scalar.activation(z_rows[j][:, cols], th[j][:, cols], ACT.Copy, scale=column(1, j))
            if j < 4:
                move_rows(j)

        def move_rows(j):
            moved = z_moved[0][32 * j : 32 * (j + 1), :].rearrange("q (t m) -> q t m", t=4)
            nc.sync.dma_start(moved, z_rows[j])

        def scale_on_vector(j):
            shared(z_rows, "z", j, {}, BF16)
            nc.vector.tensor_scalar(z_rows[j], th[j], gain_late[j - 2][:, 0:1], 0.0, ALU.mult, ALU.add)
            move_rows(j)

        round_into("F", ("F0", round_on_scalar), ("F1", round_on_scalar))
        quantise_stage("F", 0, 2, (0, 1))
        last = [new("v_last0", [P, 768], U32), new("v_last1", [P, 256], U32)]
        v_words.append([(0, 768, last[0]), (768, S, last[1])])
        gather_last(last[0][:, 0:512], 0, 512)
        gather_last(last[0][:, 512:768], 512, 256)
        round_into("02", ("02", round_on_scalar))
        quantise_stage("02", 0, 1, (2,))
        gather_last(last[1][:], 768, 256)
        round_into("12", ("12", round_on_scalar))
        quantise_stage("12", 1, 1, (2,))
        multiply(0)
        multiply(1)
        round_into("A0", ("A0", round_on_gpsimd))
        empty(0)
        gather1(0)
        empty(1)
        quantise_stage("A0", 2, 2, (0,))
        round_part("21", "A1", 0, round_on_gpsimd)
        round_part("31", "A1", 1, round_on_scalar)
        gather1(1)
        bound(0)
        scale(0, False)
        bound(1)
        scale(1, False)
        round_into("A2", ("A2", round_on_vector))
        quantise_stage("21", 2, 1, (1,))
        quantise_stage("31", 3, 1, (1,))
        quantise_stage("A2", 2, 2, (2,))
        multiply(2)
        multiply(3)
        deal_half("W0", 0, "gpsimd")
        gather2(0)
        gather2(1)
        quantise_half("W0", 0, 0)
        deal_half("W1", 0, "gpsimd")
        empty(2)
        empty(3)
        deal_half("W0", 1, "scalar")
        gather1(2)
        gather1(3)
        for j in (2, 3):
            bound(j)
        deal_half("W1", 1, "scalar")
        quantise_half("W0", 1, 0)
        quantise_half("W1", 0, 1)
        deal_half("W2", 0, "vector")
        scale_on_vector(2)
        quantise_half("W2", 0, 2)
        scale_on_vector(3)
        deal_half("W2", 1, "gpsimd")
        multiply(4)
        multiply(5)
        gather2(2)
        gather2(3)
        quantise_half("W1", 1, 1)
        for e in range(2):
            quantise("%d2" % (6 + e), staged["W2b"][:, 4 * P * e : 4 * P * (e + 1)], 6 + e, 1, (2,))
        multiply(6)
        multiply(7)
        z_codes, z_planes, z_il = {}, {}, {}
        z_il[0] = new("z_il0", [P, 4 * M], BF16)
        nc.gpsimd.tensor_scalar(
            z_il[0][:].rearrange("p (m t) -> p m t", t=4),
            z_moved[0][:].rearrange("p (t m) -> p m t", t=4),
            1.0,
            0.0,
            ALU.mult,
            ALU.add,
        )
        empty(4)
        empty(5)
        gather1(4)
        gather1(5)
        empty(6)
        bound(4)
        gather1(6)
        empty(7)
        def quantise_z(b, m0, width):
            if b not in z_codes:
                z_codes[b] = new("z_codes%d" % b, [P, M], U32)
                z_planes[b] = new("z_plane%d" % b, [P, M], U8)
            nc.vector.quantize_mx(
                out=z_codes[b][:, m0 : m0 + width].bitcast(FP8X4),
                scales=z_planes[b][:, m0 : m0 + width],
                in_=z_il[b][:, 4 * m0 : 4 * (m0 + width)],
            )

        quantise_z(0, 0, M)
        halves = (("h1_7a", slice(0, M // 2)), ("h1_7b", slice(M // 2, M)))
        for name, cols in halves:
            gather1(7, name, cols)
        z_moved.append(new("z_moved1", [P, 4 * M], BF16))
        for e in range(4):
            z_rows[4 + e] = z_moved[1][:, M * e : M * (e + 1)]
        scale(4, True)
        for j in range(5, 7):
            bound(j)
            scale(j, True)
        for name, cols in halves:
            bound(7, name, cols)
        for name, cols in halves:
            scale(7, False, cols)

        gather2(PLAIN - 1)
        z_il[1] = new("z_il1", [P, 4 * M], BF16)
        dst = z_il[1][:].rearrange("p (c i t) -> p c t i", i=4, t=4)
        src = z_moved[1][:].rearrange("p (t c i) -> p c t i", i=4, t=4)
        for c0, share in zip((0, 64), SHARES):
            nc.scalar.copy(dst[:, c0 : c0 + share], src[:, c0 : c0 + share])
            nc.vector.tensor_copy(dst[:, c0 + share : c0 + 64], src[:, c0 + share : c0 + 64])
        for m0 in (0, M // 2):
            quantise_z(1, m0, M // 2)

        w4_dealt = new("w4_dealt", [P, HP * H], U8)
        nc.scalar.copy(
            w4_dealt[:].bitcast(U16).rearrange("p (a t c) -> p a t c", a=HP, t=4),
            w4_sb[:].bitcast(U16).rearrange("p (a b c t) -> p b a t c", a=HP, b=2, t=4)[:, 1],
        )
        plane_dealt = new("plane_dealt", [P, HP * H // 2], U8)
        nc.vector.tensor_copy(
            plane_dealt[:].rearrange("p (a t c) -> p a t c", a=HP, t=4),
            w4_plane[:].rearrange("p (a b c t) -> p b a t c", a=HP, b=2, t=4)[:, 1],
        )

        summed = {}
        turned_sums = new("turned", [P, IN_PSUM, M], F32)

        def turn_in(j, rows, first):
            for m0 in range(0, M, P):
                nc.tensor.matmul(
                    summed[j][:, m0 : m0 + P],
                    rows[:, m0 : m0 + P],
                    ident[:],
                    start=(first and m0 == 0),
                    stop=(not first and m0 == M - P),
                    is_transpose=True,
                )

        for j in (1, 3):
            summed[j] = psum.tile([P, M], F32, name="summed", tag="bank%d" % ((7 + j // 2) % 8))
            turn_in(j, h2[j], True)
        for j in range(TILES):
            y = psum.tile([P, M], F32, name="y", tag="bank%d" % (1 + j % 6))
            order = range(HP) if j < 4 else range(HP - 1, -1, -1)
            for a in order:
                words, plane = (w4_sb, w4_plane) if j < 4 else (w4_dealt, plane_dealt)
                n0 = H * a + P * j if j < 4 else H // 2 * a + P * (j - 4)
                width = M // 2 if (j, a) == (0, 1) else M
                for m0 in range(0, M, width):
                    nc.tensor.matmul_mx(
                        out=y[:, m0 : m0 + width],
                        lhsT=words[:, 2 * n0 : 2 * (n0 + P)].bitcast(FP4X4),
                        lhsT_scale=plane[:, n0 : n0 + P],
                        rhs=z_codes[a][:, m0 : m0 + width].bitcast(FP8X4),
                        rhs_scale=z_planes[a][:, m0 : m0 + width],
                        start=(a == order[0]),
                        stop=(a == order[-1] and m0 + width == M),
                    )
            nc.vector.scalar_tensor_tensor(th[j], y[:], column(2, j), th[j], ALU.add, ALU.mult)
            if j >= TILES - IN_PSUM:
                e = j - (TILES - IN_PSUM)
                turn_in(2 * e + 1, th[2 * e + 1], False)
                nc.scalar.copy(turned_sums[:, e, :], summed[2 * e + 1][:])
        for j in range(0, PLAIN, 2):
            nc.gpsimd.tensor_tensor(h2[j], th[j], h2[j], ALU.add)
            nc.sync.dma_start(rows_of(j), h2[j])
        for j in summed:
            back = psum.tile([P, M], F32, name="back", tag="bank%d" % ((7 + j // 2) % 8))
            for m0 in range(0, M, P):
                cols = slice(m0, m0 + P)
                nc.tensor.transpose(back[:, cols], turned_sums[:, j // 2, cols], ident[:])
            nc.scalar.copy(h2[j], back[:])
            nc.scalar.dma_start(rows_of(j), h2[j])
        result = new("result", [P, TILES - PLAIN, M], F32)
        for j in range(PLAIN, TILES):
            for cols in (slice(0, LAST), slice(LAST, M)) if j == TILES - 1 else (slice(0, M),):
                picks = pos2_sb[:, cols.start // 16 : cols.stop // 16]
                nc.vector.tensor_tensor(result[:, j - PLAIN, cols], h[j].indirect(picks), th[j][:, cols], ALU.add)
                nc.sync.dma_start(rows_of(j)[:, cols], result[:, j - PLAIN, cols])
